import numpy as np
import ml_dtypes


def mxq(x, axis, fmt="e4m3"):
    dtype, down = {"e4m3": (ml_dtypes.float8_e4m3fn, 7), "e5m2": (ml_dtypes.float8_e5m2, 14)}[fmt]
    v = np.moveaxis(np.asarray(x, np.float32).astype(ml_dtypes.bfloat16).astype(np.float64), axis, -1)
    blocks = v.reshape(v.shape[:-1] + (-1, 32))
    amax = np.abs(blocks).max(-1, keepdims=True)
    byte = np.maximum(np.where(amax > 0, np.frexp(amax)[1] - 1 + 127, 0) - down, 1)
    scale = np.exp2(byte - 127.0)
    codes = (blocks / scale).astype(np.float32).astype(dtype).astype(np.float64)
    return np.moveaxis((codes * scale).reshape(v.shape), -1, axis)


WIDE = False


def mx_kscale(k):
    if not WIDE:
        return np.ones(k)
    levels = np.array([10, -10, 5, -5, 0])
    if k % 512:
        return np.exp2(np.random.permutation(np.resize(levels, k // 32))).repeat(32)
    a = np.empty((k // 512, 16))
    for p in range(k // 512):
        a[p, :8] = np.random.permutation(np.resize(levels, 8))
        for g in range(8):
            far = levels[np.abs(levels - a[p, g]) >= 10]
            a[p, g + 8] = far[np.random.randint(len(far))]
    return np.exp2(a.ravel()).repeat(32)


def f64(x):
    return np.asarray(x).astype(np.float64)


def striped(idx):
    return np.tile(idx.reshape(-1, 16).T, (8, 1)).astype(np.uint16)


def unstriped(offs):
    return offs[:16].T.reshape(-1).astype(np.int64)


E2M1 = np.array([0.0, 0.5, 1.0, 1.5, 2.0, 3.0, 4.0, 6.0, -0.0, -0.5, -1.0, -1.5, -2.0, -3.0, -4.0, -6.0])


def pack_weight(w, fmt):
    k, n = w.shape
    w = f64(np.asarray(w, np.float32).astype(ml_dtypes.bfloat16)).reshape(k // 32, 32, n)
    amax = np.abs(w).max(1)
    if fmt == "e4m3":
        byte = np.frexp(amax)[1] - 1 + 127 - 7
    else:
        mant, ex = np.frexp(amax / 6.0)
        byte = np.where(mant > 0.5, ex, ex - 1) + 127
    byte = np.clip(np.where(amax > 0, byte, 1), 1, 254)
    scaled = (w * np.exp2(127.0 - byte)[:, None, :]).reshape(k, n).astype(np.float32)
    by_word = np.ascontiguousarray(scaled.reshape(k // 512, 128, 4, n).transpose(0, 1, 3, 2))
    if fmt == "e4m3":
        words = by_word.astype(ml_dtypes.float8_e4m3fn).view(np.uint8)
    else:
        c = by_word.astype(ml_dtypes.float4_e2m1fn).view(np.uint8) & 0xF
        words = (c[..., 0::2] | (c[..., 1::2] << 4)).reshape(k // 512, 128, 2 * n)
    return np.ascontiguousarray(words), np.ascontiguousarray(byte.astype(np.uint8).reshape(k // 512, 16, n))


def unpack_weight(words, scales, fmt):
    g, _, n = scales.shape
    words = np.ascontiguousarray(words).reshape(g, 128, n, -1)
    if fmt == "e4m3":
        vals = words.view(ml_dtypes.float8_e4m3fn).astype(np.float64)
    else:
        nib = np.empty((g, 128, n, 4), np.uint8)
        nib[..., 0::2] = words & 0xF
        nib[..., 1::2] = words >> 4
        vals = E2M1[nib]
    vals = vals * np.repeat(np.exp2(scales.astype(np.float64) - 127.0), 8, axis=1)[..., None]
    return vals.transpose(0, 1, 3, 2).reshape(g * 512, n)


def gelu(v):
    return 0.5 * v * (1.0 + np.tanh(np.sqrt(2.0 / np.pi) * (v + 0.044715 * v**3)))


def striped8(idx):
    return np.concatenate([v.reshape(-1, 16).T for v in idx]).astype(np.uint16)


def unstriped8(offs):
    return np.stack([offs[16 * g:16 * g + 16].T.reshape(-1) for g in range(8)]).astype(np.int64)


def put_heads(h, wgs, idx8, t2):
    r = np.arange(h.shape[0])
    page = np.zeros((h.shape[0], t2))
    page[r[:, None], idx8[r % 512 // 64]] = wgs[r // 4 % 128] * h
    return page


K, T, S, H, T2, N = 1024, 2048, 512, 1024, 1024, 384

def setup_inputs():
    n = np.random.standard_normal
    s = mx_kscale(K)[:, None]
    u = mx_kscale(H)[:, None]
    tab_words, tab_scales = pack_weight(n((K, T)) * s, "e4m3")
    wg_words, wg_scales = pack_weight(1.5 * n((K, H)) / np.sqrt(K) / s, "e2m1")
    wo_words, wo_scales = pack_weight(n((H, N)) / np.sqrt(H) / u, "e4m3")
    return {
        "tab_words": tab_words, "tab_scales": tab_scales,
        "offs": striped(np.random.permutation(T)[:S]),
        "wa": (n((K, H)) / np.sqrt(K) / s).astype(np.float32),
        "wg_words": wg_words, "wg_scales": wg_scales,
        "prior": n((H, S)).astype(np.float32),
        "wgs": np.repeat(np.random.uniform(0.5, 2.0, (8, S)), 16, axis=0).astype(np.float32),
        "offs2": striped8(np.stack([np.random.permutation(T2)[:S] for _ in range(8)])),
        "load": (np.exp(0.4 * n((H, T2))) * u).astype(np.float32),
        "wo_words": wo_words, "wo_scales": wo_scales,
    }

def reference(tab_words, tab_scales, offs, wa, wg_words, wg_scales, prior, wgs, offs2, load, wo_words, wo_scales):
    v = unpack_weight(tab_words, tab_scales, "e4m3")[:, unstriped(offs)]
    fit = mxq(f64(wa), 0, "e4m3").T @ v
    score = unpack_weight(wg_words, wg_scales, "e2m1").T @ v
    gate = 1.0 / (1.0 + np.exp(-score))
    base = f64(prior)
    h = base + gate * (fit - base)
    page = put_heads(h, f64(wgs), unstriped8(offs2), T2)
    ld = f64(load)
    z = page * ld + ld
    out = unpack_weight(wo_words, wo_scales, "e4m3").T @ mxq(z, 0, "e4m3")
    return out

@@ -1,0 +1,355 @@
+from contextlib import ExitStack
+
+import concourse.mybir as mybir
+from concourse.masks import make_identity
+
+K, T, S, H, T2, N = 1024, 2048, 512, 1024, 1024, 384
+FLOPS = 2 * (2 * K * H * S + H * N * T2)
+
+F32 = mybir.dt.float32
+BF16 = mybir.dt.bfloat16
+I32 = mybir.dt.int32
+U32 = mybir.dt.uint32
+U16 = mybir.dt.uint16
+U8 = mybir.dt.uint8
+FP8X4 = mybir.dt.float8_e4m3fn_x4
+FP4X4 = mybir.dt.float4_e2m1fn_x4
+ADD = mybir.AluOpType.add
+SUB = mybir.AluOpType.subtract
+MULT = mybir.AluOpType.mult
+SIGMOID = mybir.ActivationFunctionType.Sigmoid
+COPY = mybir.ActivationFunctionType.Copy
+
+P = 128
+PACK = 4
+PASS = P * PACK
+SLICES = H // P
+HALF = 512
+QUART = 256
+
+
+def load_scale_rows(queue, plane, scales):
+    rows = scales.bitcast(I32)
+    for q in range(4):
+        queue.dma_start(
+            out=plane[32 * q : 32 * q + 4, :, :].bitcast(I32),
+            in_=rows[:, 4 * q : 4 * q + 4, :].rearrange("a r c -> r a c"),
+        )
+
+
+def tile_list_demand_response_baseline_kernel(
+    tc, tab_words, tab_scales, offs, wa, wg_words, wg_scales, prior, wgs, offs2, load, wo_words, wo_scales, out
+):
+    nc = tc.nc
+    with ExitStack() as ctx:
+        keep = ctx.enter_context(tc.tile_pool(name="keep", bufs=1))
+        psum = ctx.enter_context(tc.psum_pool(name="psum", bufs=1))
+
+        idx = keep.tile([P, S // 16], U16, name="idx")
+        idx2 = keep.tile([P, S // 16], U16, name="idx2")
+        tab_sc = keep.tile([P, 2, T], U8, name="tab_sc", align_bytes=64)
+        wg_sc_raw = keep.tile([P, 2, H], U8, name="wg_sc_raw", align_bytes=64)
+        wo_sc = keep.tile([P, 2, N], U8, name="wo_sc", align_bytes=64)
+        wg_raw = keep.tile([P, 2, 2 * H], U8, name="wg_raw", align_bytes=64)
+        tab_first = keep.tile([P, T], I32, name="tab0", align_bytes=64)
+        pages = [keep.tile([P, T2], F32, name="page%d" % n, align_bytes=64) for n in range(2)]
+        ident = keep.tile([P, P], F32, name="ident", align_bytes=64)
+
+        nc.vector.memset(tab_sc[:].rearrange("p a c -> p (a c)").bitcast(I32), 0)
+        nc.vector.memset(wg_sc_raw[:].rearrange("p a c -> p (a c)").bitcast(I32), 0)
+        with tc.tile_pool(name="early", bufs=1) as early:
+            warm = early.tile([P, 2], F32, name="warm")
+            nc.gpsimd.memset(warm[:, 0:1], 0.0)
+            nc.scalar.activation(warm[:, 1:2], warm[:, 0:1], SIGMOID)
+        late = ctx.enter_context(tc.tile_pool(name="late", bufs=1))
+
+        def sb(name, shape, dtype, tag=None, bufs=1):
+            return late.tile(shape, dtype, name=name, tag=tag or name, bufs=bufs, align_bytes=64)
+
+        tab = [tab_first, sb("tab1", [P, T], I32)]
+        wa_raw = {}
+        for a in range(2):
+            for b in range(2):
+                wa_raw[a, b] = sb("wa_raw%d%d" % (a, b), [P, PACK, PASS], F32)
+        base = [sb("base%d" % b, [P, PACK, S], F32) for b in range(2)]
+        wgs_sb = sb("wgs_sb", [P, S], F32)
+        ld = [sb("ld%d" % s, [P, T2], F32) for s in range(SLICES)]
+        wo_w = sb("wo_w", [P, 2, N], I32)
+        make_identity(nc, ident[:])
+
+        for page in pages:
+            nc.gpsimd.memset(page[:], 0.0)
+        nc.gpsimd.memset(wo_sc[:].rearrange("p a c -> p (a c)").bitcast(I32), 0)
+        wa_view = wa.rearrange("(a p j) (b c) -> a b p j c", a=2, j=PACK, b=2)
+        prior_view = prior.rearrange("(b p i) j -> b p i j", b=2, i=PACK)
+        load_view = load.rearrange("(b p i) t -> b i p t", b=2, i=PACK)
+
+        def load_tab(a):
+            nc.sync.dma_start(out=tab[a][:], in_=tab_words[a].rearrange("p t i -> p (t i)").bitcast(I32))
+
+        def load_ld(s):
+            nc.sync.dma_start(out=ld[s][:], in_=load_view[s // PACK, s % PACK])
+
+        nc.sync.dma_start(idx[:], offs)
+        nc.sync.dma_start(idx2[:], offs2)
+        load_tab(0)
+        nc.sync.dma_start(out=wg_raw[:].bitcast(I32), in_=wg_words.bitcast(I32).rearrange("a p c -> p a c"))
+        load_scale_rows(nc.sync, tab_sc, tab_scales)
+        load_tab(1)
+        load_scale_rows(nc.sync, wg_sc_raw, wg_scales)
+        nc.sync.dma_start(out=wa_raw[0, 0][:], in_=wa_view[0, 0])
+        nc.sync.dma_start(out=wa_raw[1, 0][:], in_=wa_view[1, 0])
+        nc.sync.dma_start(out=base[0][:, 0, :], in_=prior_view[0, :, 0, :])
+        nc.sync.dma_start(out=base[0][:, 1, :], in_=prior_view[0, :, 1, :])
+        nc.sync.dma_start(out=wgs_sb[:], in_=wgs)
+        nc.sync.dma_start(out=base[0][:, 2:PACK, :], in_=prior_view[0, :, 2:PACK, :])
+        nc.sync.dma_start(out=wa_raw[0, 1][:], in_=wa_view[0, 1])
+        nc.sync.dma_start(out=wa_raw[1, 1][:], in_=wa_view[1, 1])
+        nc.sync.dma_start(out=base[1][:], in_=prior_view[1])
+        load_ld(0)
+        nc.sync.dma_start(
+            out=wo_w[:], in_=wo_words.rearrange("a p c i -> a p (c i)").bitcast(I32).rearrange("a p c -> p a c")
+        )
+        load_scale_rows(nc.sync, wo_sc, wo_scales)
+        for s in range(1, SLICES):
+            load_ld(s)
+
+        v_w = [sb("v_w%d" % a, [P, S], U32) for a in range(2)]
+        v_sc = [sb("v_sc%d" % a, [P, S], U8) for a in range(2)]
+        wg_w = sb("wg_w", [P, 2, 2 * P], U8)
+        wg_sc = sb("wg_sc", [P, 2, P], U8)
+        nc.vector.tensor_copy(v_w[0][:], tab[0][:].bitcast(U32).indirect(idx[:]))
+        for a in range(2):
+            nc.vector.tensor_copy(v_sc[a][:], tab_sc[:, a, :].indirect(idx[:]))
+        nc.vector.tensor_copy(v_w[1][:], tab[1][:].bitcast(U32).indirect(idx[:]))
+        nc.vector.tensor_copy(out=wg_w[:].bitcast(U16), in_=wg_raw[:].bitcast(U16)[:, :, 0:PASS:PACK])
+        nc.vector.tensor_copy(out=wg_sc[:], in_=wg_sc_raw[:, :, 0:PASS:PACK])
+
+        wa_w = {}
+        wa_sc = {}
+        for a in range(2):
+            for b in range(2):
+                wa_w[a, b] = sb("wa_w%d%d" % (a, b), [P, PASS], U32)
+                wa_sc[a, b] = sb("wa_sc%d%d" % (a, b), [P, PASS], U8)
+
+        def round_wa(copy, a, b, i0, i1, name):
+            grouped = sb(name, [P, i1 - i0, P, PACK], BF16)
+            copy(
+                out=grouped[:].rearrange("p i m j -> p m j i"),
+                in_=wa_raw[a, b][:].rearrange("p j (m i) -> p m j i", i=PACK)[:, :, :, i0:i1],
+            )
+            return grouped
+
+        def quantize_wa(grouped, a, b, i_first, i0, i1):
+            nc.vector.quantize_mx(
+                out=wa_w[a, b][:, i0 * P : i1 * P].bitcast(FP8X4),
+                scales=wa_sc[a, b][:, i0 * P : i1 * P],
+                in_=grouped[:, i0 - i_first : i1 - i_first, :, :].rearrange("p i m j -> p (i m j)"),
+            )
+
+        blend = {}
+        gate_t = {}
+
+        def gate_stage(b, first, tags):
+            gate_t[b] = sb("gate_t%d" % b, [P, PACK, S], F32, tag=None if b == 0 else "wa_raw10")
+            for c in range(S // P):
+                tag, bufs = tags[c]
+                score = psum.tile([P, PASS], F32, name="score%d%d" % (b, c), tag=tag, bufs=bufs)
+                cols = slice(c * P, (c + 1) * P)
+                for a in range(2):
+                    nc.tensor.matmul_mx(
+                        out=score[:],
+                        lhsT=v_w[a][:, cols].bitcast(FP8X4),
+                        lhsT_scale=v_sc[a][:, cols],
+                        rhs=wg_raw[:, a, 2 * b * PASS : 2 * (b + 1) * PASS].bitcast(FP4X4),
+                        rhs_scale=wg_sc_raw[:, a, b * PASS : (b + 1) * PASS],
+                        start=(a == 0),
+                        stop=(a == 1),
+                    )
+                nc.scalar.activation(
+                    gate_t[b][:, first:PACK, cols],
+                    score[:].rearrange("j (m i) -> j i m", i=PACK)[:, first:PACK, :],
+                    SIGMOID,
+                )
+
+        def fit_stage(s):
+            b, i = divmod(s, PACK)
+            fit = psum.tile([P, S], F32, name="fit%d" % s, tag="fit", bufs=2)
+            for a in range(2):
+                nc.tensor.matmul_mx(
+                    out=fit[:],
+                    lhsT=wa_w[a, b][:, i * P : (i + 1) * P].bitcast(FP8X4),
+                    lhsT_scale=wa_sc[a, b][:, i * P : (i + 1) * P],
+                    rhs=v_w[a][:].bitcast(FP8X4),
+                    rhs_scale=v_sc[a][:],
+                    start=(a == 0),
+                    stop=(a == 1),
+                )
+            return fit
+
+        def base_of(s):
+            return base[s // PACK][:, s % PACK, :]
+
+        def ring(name, s, bufs):
+            return sb("%s%d" % (name, s), [P, S], F32, tag=name, bufs=bufs)
+
+        def turn_into(bank, src, start, stop):
+            for c in range(S // P):
+                cols = slice(c * P, (c + 1) * P)
+                nc.tensor.matmul(
+                    bank[:, cols], src[:, cols], ident[:], is_transpose=True,
+                    start=(start and c == 0), stop=(stop and c == S // P - 1),
+                )
+
+        def direct_blend(s):
+            score = psum.tile([P, S], F32, name="score%d" % s, tag="score")
+            for a in range(2):
+                nc.tensor.matmul_mx(
+                    out=score[:],
+                    lhsT=wg_w[:, a, :].bitcast(FP4X4),
+                    lhsT_scale=wg_sc[:, a, :],
+                    rhs=v_w[a][:].bitcast(FP8X4),
+                    rhs_scale=v_sc[a][:],
+                    start=(a == 0),
+                    stop=(a == 1),
+                )
+            gate = ring("gate", s, 1)
+            nc.scalar.activation(gate[:], score[:], SIGMOID)
+            gate_stage(0, 1, [("gap", 2), ("gap", 2), ("total", 2), ("total", 2)])
+            g = round_wa(nc.vector.tensor_copy, 0, 0, 0, 4, "wa_g00")
+            quantize_wa(g, 0, 0, 0, 0, 4)
+            g = round_wa(nc.vector.tensor_copy, 1, 0, 0, 1, "wa_g10a")
+            quantize_wa(g, 1, 0, 0, 0, 1)
+            g = round_wa(nc.scalar.copy, 1, 0, 1, 2, "wa_g10b")
+            quantize_wa(g, 1, 0, 1, 1, 2)
+            fit = fit_stage(s)
+            diff = ring("minus_fit", s, 2)
+            moved = ring("moved", s, 2)
+            blend[s] = ring("blend", s, 3)
+            nc.vector.tensor_tensor(diff[:], fit[:], base_of(s), SUB)
+            nc.vector.tensor_tensor(moved[:], diff[:], gate[:], MULT)
+            nc.vector.tensor_tensor(blend[s][:], moved[:], base_of(s), ADD)
+
+        turned = {}
+
+        def front_stage(s):
+            gate = gate_t[s // PACK][:, s % PACK, :]
+            fit = fit_stage(s)
+            minus_fit = ring("minus_fit", s, 2)
+            nc.scalar.activation(minus_fit[:], fit[:], COPY, scale=-1.0)
+            gap = psum.tile([P, S], F32, name="gap%d" % s, tag="gap", bufs=2)
+            turn_into(gap, base_of(s), True, False)
+            turn_into(gap, minus_fit, False, True)
+            base_bank = psum.tile([P, S], F32, name="base_bank%d" % s, tag="base_bank")
+            turn_into(base_bank, base_of(s), True, True)
+            base_t = ring("base_t", s, 2)
+            nc.scalar.copy(base_t[:], base_bank[:])
+            turned[s] = (gap, gate, base_t)
+
+        def back_stage(s):
+            gap, gate, base_t = turned[s]
+            moved = ring("moved", s, 2)
+            nc.vector.scalar_tensor_tensor(moved[:], gap[:], -1.0, gate, MULT, MULT)
+            total = psum.tile([P, S], F32, name="total%d" % s, tag="total", bufs=2)
+            turn_into(total, base_t, True, False)
+            turn_into(total, moved, False, True)
+            blend[s] = ring("blend", s, 3)
+            nc.scalar.copy(blend[s][:], total[:])
+
+        def scatter_stage(s):
+            nc.vector.tensor_tensor(pages[s % 2][:].indirect(idx2[:]), blend[s][:], wgs_sb[:], MULT)
+
+        z_rows = [sb("z_rows%d" % b, [P, PACK, T2], BF16) for b in range(2)]
+        z_w = {}
+        z_sc = [sb("z_sc%d" % b, [P, T2], U8) for b in range(2)]
+
+        def z_stage(s, c0, c1):
+            b, i = divmod(s, PACK)
+            nc.vector.scalar_tensor_tensor(
+                z_rows[b][:, i, c0:c1], pages[s % 2][:, c0:c1], 1.0, ld[s][:, c0:c1], ADD, MULT
+            )
+
+        def weave_z(copy, b, c0, c1):
+            woven = sb("woven%d_%d" % (b, c0), [P, c1 - c0, PACK], BF16, tag="woven", bufs=4)
+            for w0 in range(0, c1 - c0, QUART):
+                copy(
+                    out=woven[:, w0 : w0 + QUART, :].rearrange("p (c n) i -> p c i n", n=4),
+                    in_=z_rows[b][:, :, c0 + w0 : c0 + w0 + QUART].rearrange("p i (c n) -> p c i n", n=4),
+                )
+            return woven
+
+        def quantize_z(woven, b, c0, c1):
+            half = c0 // HALF
+            if (b, half) not in z_w:
+                if b == 0:
+                    z_w[b, half] = sb("z_w%d%d" % (b, half), [P, HALF], U32, tag="blend", bufs=3)
+                else:
+                    z_w[b, half] = sb("z_w%d%d" % (b, half), [P, HALF], U32)
+            nc.vector.quantize_mx(
+                out=z_w[b, half][:, c0 - half * HALF : c1 - half * HALF].bitcast(FP8X4),
+                scales=z_sc[b][:, c0:c1],
+                in_=woven[:].rearrange("p c i -> p (c i)"),
+            )
+
+        acc = {}
+
+        def out_pass(b, n, half, c0, c1, start, stop):
+            nc.tensor.matmul_mx(
+                out=acc[n, half][:, c0 - half * HALF : c1 - half * HALF],
+                lhsT=wo_w[:, b, n * P : (n + 1) * P].bitcast(FP8X4),
+                lhsT_scale=wo_sc[:, b, n * P : (n + 1) * P],
+                rhs=z_w[b, half][:, c0 - half * HALF : c1 - half * HALF].bitcast(FP8X4),
+                rhs_scale=z_sc[b][:, c0:c1],
+                start=start,
+                stop=stop,
+            )
+
+        direct_blend(0)
+        front_stage(1)
+        back_stage(1)
+        g = round_wa(nc.scalar.copy, 1, 0, 2, 4, "wa_g10c")
+        quantize_wa(g, 1, 0, 2, 2, 4)
+        front_stage(2)
+        acc_tags = [("fit", 2), ("fit", 2), ("score", 1), ("base_bank", 1), ("gap", 2), ("gap", 2)]
+        for s in range(SLICES):
+            scatter_stage(s)
+            if s + 2 < SLICES:
+                back_stage(s + 2)
+            if s == 0:
+                gate_stage(1, 0, [("score", 1)] * PACK)
+                for a in range(2):
+                    for i0 in (0, 2):
+                        g = round_wa(nc.scalar.copy, a, 1, i0, i0 + 2, "wa_g%d1%d" % (a, i0))
+                        quantize_wa(g, a, 1, i0, i0, i0 + 2)
+            if s + 3 < SLICES:
+                front_stage(s + 3)
+            if s + 1 < SLICES:
+                z_stage(s, 0, T2)
+            if s == PACK - 1:
+                first_woven = [weave_z(nc.scalar.copy, 0, c0, c0 + HALF) for c0 in range(0, T2, HALF)]
+            if s in (SLICES - 3, SLICES - 2):
+                half = s - (SLICES - 3)
+                quantize_z(first_woven[half], 0, half * HALF, (half + 1) * HALF)
+                for n in range(3):
+                    tag, bufs = acc_tags[half * 3 + n]
+                    acc[n, half] = psum.tile([P, HALF], F32, name="acc%d%d" % (n, half), tag=tag, bufs=bufs)
+                    out_pass(0, n, half, half * HALF, (half + 1) * HALF, True, False)
+
+        last = SLICES - 1
+        for q in range(4):
+            z_stage(last, q * QUART, (q + 1) * QUART)
+        for q in range(4):
+            c0, c1 = q * QUART, (q + 1) * QUART
+            copy = nc.scalar.copy if q % 2 == 0 else nc.vector.tensor_copy
+            quantize_z(weave_z(copy, 1, c0, c1), 1, c0, c1)
+            for n in range(3):
+                out_pass(1, n, q // 2, c0, c1, False, q % 2 == 1)
+            if q % 2 == 1:
+                half = q // 2
+                for n in range(3):
+                    res = base[half][:, n, :]
+                    if half == 1 and n == 1:
+                        nc.vector.tensor_copy(res[:], acc[n, half][:])
+                    else:
+                        nc.scalar.copy(res[:], acc[n, half][:])
+                    nc.sync.dma_start(out=out[n * P : (n + 1) * P, half * HALF : (half + 1) * HALF], in_=res[:])

@@ -26,6 +26,8 @@ PASS = P * PACK
 SLICES = H // P
 HALF = 512
 QUART = 256
+DIRECT = 2
+PAGES = 2
 
 
 def load_scale_rows(queue, plane, scales):
@@ -50,9 +52,9 @@ def tile_list_demand_response_baseline_kernel(
         tab_sc = keep.tile([P, 2, T], U8, name="tab_sc", align_bytes=64)
         wg_sc_raw = keep.tile([P, 2, H], U8, name="wg_sc_raw", align_bytes=64)
         wo_sc = keep.tile([P, 2, N], U8, name="wo_sc", align_bytes=64)
-        wg_raw = keep.tile([P, 2, 2 * H], U8, name="wg_raw", align_bytes=64)
+        wg_first = keep.tile([P, 2, 2 * PASS], U8, name="wg_raw0", align_bytes=64)
         tab_first = keep.tile([P, T], I32, name="tab0", align_bytes=64)
-        pages = [keep.tile([P, T2], F32, name="page%d" % n, align_bytes=64) for n in range(2)]
+        pages = [keep.tile([P, T2], F32, name="page%d" % n, align_bytes=64) for n in range(PAGES)]
         ident = keep.tile([P, P], F32, name="ident", align_bytes=64)
 
         nc.vector.memset(tab_sc[:].rearrange("p a c -> p (a c)").bitcast(I32), 0)
@@ -67,6 +69,7 @@ def tile_list_demand_response_baseline_kernel(
             return late.tile(shape, dtype, name=name, tag=tag or name, bufs=bufs, align_bytes=64)
 
         tab = [tab_first, sb("tab1", [P, T], I32)]
+        wg_raw = [wg_first, sb("wg_raw1", [P, 2, 2 * PASS], U8)]
         wa_raw = {}
         for a in range(2):
             for b in range(2):
@@ -87,43 +90,54 @@ def tile_list_demand_response_baseline_kernel(
         def load_tab(a):
             nc.sync.dma_start(out=tab[a][:], in_=tab_words[a].rearrange("p t i -> p (t i)").bitcast(I32))
 
+        def load_wg(b):
+            words = wg_words.bitcast(I32).rearrange("a p (b c) -> b p a c", b=2)
+            nc.sync.dma_start(out=wg_raw[b][:].bitcast(I32), in_=words[b])
+
         def load_ld(s):
             nc.sync.dma_start(out=ld[s][:], in_=load_view[s // PACK, s % PACK])
 
         nc.sync.dma_start(idx[:], offs)
         nc.sync.dma_start(idx2[:], offs2)
         load_tab(0)
-        nc.sync.dma_start(out=wg_raw[:].bitcast(I32), in_=wg_words.bitcast(I32).rearrange("a p c -> p a c"))
+        load_wg(0)
         load_scale_rows(nc.sync, tab_sc, tab_scales)
         load_tab(1)
         load_scale_rows(nc.sync, wg_sc_raw, wg_scales)
         nc.sync.dma_start(out=wa_raw[0, 0][:], in_=wa_view[0, 0])
         nc.sync.dma_start(out=wa_raw[1, 0][:], in_=wa_view[1, 0])
         nc.sync.dma_start(out=base[0][:, 0, :], in_=prior_view[0, :, 0, :])
-        nc.sync.dma_start(out=base[0][:, 1, :], in_=prior_view[0, :, 1, :])
         nc.sync.dma_start(out=wgs_sb[:], in_=wgs)
-        nc.sync.dma_start(out=base[0][:, 2:PACK, :], in_=prior_view[0, :, 2:PACK, :])
+        nc.sync.dma_start(out=base[0][:, 1, :], in_=prior_view[0, :, 1, :])
+        load_wg(1)
         nc.sync.dma_start(out=wa_raw[0, 1][:], in_=wa_view[0, 1])
         nc.sync.dma_start(out=wa_raw[1, 1][:], in_=wa_view[1, 1])
-        nc.sync.dma_start(out=base[1][:], in_=prior_view[1])
+        nc.sync.dma_start(out=base[0][:, 2:PACK, :], in_=prior_view[0, :, 2:PACK, :])
         load_ld(0)
+        nc.sync.dma_start(out=base[1][:], in_=prior_view[1])
+        load_ld(1)
         nc.sync.dma_start(
             out=wo_w[:], in_=wo_words.rearrange("a p c i -> a p (c i)").bitcast(I32).rearrange("a p c -> p a c")
         )
         load_scale_rows(nc.sync, wo_sc, wo_scales)
-        for s in range(1, SLICES):
+        for s in range(2, SLICES):
             load_ld(s)
 
         v_w = [sb("v_w%d" % a, [P, S], U32) for a in range(2)]
         v_sc = [sb("v_sc%d" % a, [P, S], U8) for a in range(2)]
-        wg_w = sb("wg_w", [P, 2, 2 * P], U8)
-        wg_sc = sb("wg_sc", [P, 2, P], U8)
+        wg_w = sb("wg_w", [P, 2, DIRECT, 2 * P], U8)
+        wg_sc = sb("wg_sc", [P, 2, DIRECT, P], U8)
         nc.vector.tensor_copy(v_w[0][:], tab[0][:].bitcast(U32).indirect(idx[:]))
         for a in range(2):
             nc.vector.tensor_copy(v_sc[a][:], tab_sc[:, a, :].indirect(idx[:]))
         nc.vector.tensor_copy(v_w[1][:], tab[1][:].bitcast(U32).indirect(idx[:]))
-        nc.vector.tensor_copy(out=wg_w[:].bitcast(U16), in_=wg_raw[:].bitcast(U16)[:, :, 0:PASS:PACK])
-        nc.vector.tensor_copy(out=wg_sc[:], in_=wg_sc_raw[:, :, 0:PASS:PACK])
+        nc.vector.tensor_copy(
+            out=wg_w[:].bitcast(U16),
+            in_=wg_raw[0][:].bitcast(U16).rearrange("p a (m i) -> p a i m", i=PACK)[:, :, 0:DIRECT, :],
+        )
+        nc.vector.tensor_copy(
+            out=wg_sc[:], in_=wg_sc_raw[:, :, 0:PASS].rearrange("p a (m i) -> p a i m", i=PACK)[:, :, 0:DIRECT, :]
+        )
 
         wa_w = {}
         wa_sc = {}
@@ -161,7 +175,7 @@ def tile_list_demand_response_baseline_kernel(
                         out=score[:],
                         lhsT=v_w[a][:, cols].bitcast(FP8X4),
                         lhsT_scale=v_sc[a][:, cols],
-                        rhs=wg_raw[:, a, 2 * b * PASS : 2 * (b + 1) * PASS].bitcast(FP4X4),
+                        rhs=wg_raw[b][:, a, :].bitcast(FP4X4),
                         rhs_scale=wg_sc_raw[:, a, b * PASS : (b + 1) * PASS],
                         start=(a == 0),
                         stop=(a == 1),
@@ -174,7 +188,7 @@ def tile_list_demand_response_baseline_kernel(
 
         def fit_stage(s):
             b, i = divmod(s, PACK)
-            fit = psum.tile([P, S], F32, name="fit%d" % s, tag="fit", bufs=2)
+            fit = psum.tile([P, S], F32, name="fit%d" % s, tag="total" if s < DIRECT else "fit", bufs=2)
             for a in range(2):
                 nc.tensor.matmul_mx(
                     out=fit[:],
@@ -201,34 +215,43 @@ def tile_list_demand_response_baseline_kernel(
                     start=(start and c == 0), stop=(stop and c == S // P - 1),
                 )
 
-        def direct_blend(s):
-            score = psum.tile([P, S], F32, name="score%d" % s, tag="score")
+        def blend_tile(s):
+            return sb("blend%d" % s, [P, S], F32, tag="wa_g112" if s % 2 else "blend_even")
+
+        direct_gate = {}
+
+        def direct_gate_stage(s):
+            score = psum.tile([P, S], F32, name="score%d" % s, tag="score" if s == 0 else "base_bank")
             for a in range(2):
                 nc.tensor.matmul_mx(
                     out=score[:],
-                    lhsT=wg_w[:, a, :].bitcast(FP4X4),
-                    lhsT_scale=wg_sc[:, a, :],
+                    lhsT=wg_w[:, a, s, :].bitcast(FP4X4),
+                    lhsT_scale=wg_sc[:, a, s, :],
                     rhs=v_w[a][:].bitcast(FP8X4),
                     rhs_scale=v_sc[a][:],
                     start=(a == 0),
                     stop=(a == 1),
                 )
-            gate = ring("gate", s, 1)
-            nc.scalar.activation(gate[:], score[:], SIGMOID)
-            gate_stage(0, 1, [("gap", 2), ("gap", 2), ("total", 2), ("total", 2)])
-            g = round_wa(nc.vector.tensor_copy, 0, 0, 0, 4, "wa_g00")
-            quantize_wa(g, 0, 0, 0, 0, 4)
-            g = round_wa(nc.vector.tensor_copy, 1, 0, 0, 1, "wa_g10a")
-            quantize_wa(g, 1, 0, 0, 0, 1)
-            g = round_wa(nc.scalar.copy, 1, 0, 1, 2, "wa_g10b")
-            quantize_wa(g, 1, 0, 1, 1, 2)
-            fit = fit_stage(s)
-            diff = ring("minus_fit", s, 2)
-            moved = ring("moved", s, 2)
-            blend[s] = ring("blend", s, 3)
-            nc.vector.tensor_tensor(diff[:], fit[:], base_of(s), SUB)
-            nc.vector.tensor_tensor(moved[:], diff[:], gate[:], MULT)
-            nc.vector.tensor_tensor(blend[s][:], moved[:], base_of(s), ADD)
+            direct_gate[s] = ring("gate", s, DIRECT)
+            nc.scalar.activation(direct_gate[s][:], score[:], SIGMOID)
+
+        def direct_blend(s):
+            gate = direct_gate[s]
+            fit = direct_fit[s]
+            diff = sb("diff%d" % s, [P, S], F32, tag="diff")
+            moved = ring("moved", s, 1)
+            blend[s] = blend_tile(s)
+            mixed = blend[s] if s == 0 else diff
+            halves = [slice(0, S // 2), slice(S // 2, S)]
+            for cols in halves:
+                nc.vector.tensor_tensor(diff[:, cols], fit[:, cols], base_of(s)[:, cols], SUB)
+            for cols in halves:
+                nc.vector.tensor_tensor(moved[:, cols], diff[:, cols], gate[:, cols], MULT)
+            for cols in halves:
+                nc.vector.tensor_tensor(mixed[:, cols], moved[:, cols], base_of(s)[:, cols], ADD)
+            if s > 0:
+                for cols in halves:
+                    nc.vector.tensor_tensor(blend[s][:, cols], mixed[:, cols], wgs_sb[:, cols], MULT)
 
         turned = {}
 
@@ -246,18 +269,32 @@ def tile_list_demand_response_baseline_kernel(
             nc.scalar.copy(base_t[:], base_bank[:])
             turned[s] = (gap, gate, base_t)
 
+        totals = {}
+
         def back_stage(s):
             gap, gate, base_t = turned[s]
-            moved = ring("moved", s, 2)
+            moved = ring("turned_moved", s, 2)
             nc.vector.scalar_tensor_tensor(moved[:], gap[:], -1.0, gate, MULT, MULT)
-            total = psum.tile([P, S], F32, name="total%d" % s, tag="total", bufs=2)
-            turn_into(total, base_t, True, False)
-            turn_into(total, moved, False, True)
-            blend[s] = ring("blend", s, 3)
-            nc.scalar.copy(blend[s][:], total[:])
+            totals[s] = psum.tile([P, S], F32, name="total%d" % s, tag="total", bufs=2)
+            turn_into(totals[s], base_t, True, False)
+            turn_into(totals[s], moved, False, True)
+
+        def weigh_stage(s):
+            blend[s] = blend_tile(s)
+            if s == SLICES - 1:
+                nc.scalar.copy(blend[s][:], totals[s][:])
+            else:
+                nc.vector.tensor_tensor(blend[s][:], totals[s][:], wgs_sb[:], MULT)
+
+        def page_of(s):
+            return pages[min(s, SLICES - 2) % 2]
 
         def scatter_stage(s):
-            nc.vector.tensor_tensor(pages[s % 2][:].indirect(idx2[:]), blend[s][:], wgs_sb[:], MULT)
+            window = page_of(s)[:].indirect(idx2[:])
+            if s in (0, SLICES - 1):
+                nc.vector.tensor_tensor(window, blend[s][:], wgs_sb[:], MULT)
+            else:
+                nc.vector.tensor_copy(window, blend[s][:])
 
         z_rows = [sb("z_rows%d" % b, [P, PACK, T2], BF16) for b in range(2)]
         z_w = {}
@@ -266,90 +303,120 @@ def tile_list_demand_response_baseline_kernel(
         def z_stage(s, c0, c1):
             b, i = divmod(s, PACK)
             nc.vector.scalar_tensor_tensor(
-                z_rows[b][:, i, c0:c1], pages[s % 2][:, c0:c1], 1.0, ld[s][:, c0:c1], ADD, MULT
+                z_rows[b][:, i, c0:c1], page_of(s)[:, c0:c1], 1.0, ld[s][:, c0:c1], ADD, MULT
             )
 
-        def weave_z(copy, b, c0, c1):
-            woven = sb("woven%d_%d" % (b, c0), [P, c1 - c0, PACK], BF16, tag="woven", bufs=4)
-            for w0 in range(0, c1 - c0, QUART):
-                copy(
-                    out=woven[:, w0 : w0 + QUART, :].rearrange("p (c n) i -> p c i n", n=4),
-                    in_=z_rows[b][:, :, c0 + w0 : c0 + w0 + QUART].rearrange("p i (c n) -> p c i n", n=4),
-                )
-            return woven
+        def z_stage_pool(s):
+            b, i = divmod(s, PACK)
+            factor = sb("factor%d" % s, [P, T2], F32, tag="diff")
+            nc.gpsimd.tensor_scalar(factor[:], page_of(s)[:], 1.0, 1.0, MULT, ADD)
+            nc.gpsimd.tensor_tensor(z_rows[b][:, i, :], factor[:], ld[s][:], MULT)
+
+        def weave_z(copy, b, woven, c0, i0, i1):
+            copy(
+                out=woven.rearrange("p (c n) i -> p c i n", n=4)[:, :, i0:i1, :],
+                in_=z_rows[b][:, i0:i1, c0 : c0 + QUART].rearrange("p i (c n) -> p c i n", n=4),
+            )
 
         def quantize_z(woven, b, c0, c1):
-            half = c0 // HALF
-            if (b, half) not in z_w:
-                if b == 0:
-                    z_w[b, half] = sb("z_w%d%d" % (b, half), [P, HALF], U32, tag="blend", bufs=3)
-                else:
-                    z_w[b, half] = sb("z_w%d%d" % (b, half), [P, HALF], U32)
+            if b == 0:
+                z_w[b, c0] = sb("z_w%d_%d" % (b, c0), [P, c1 - c0], U32, tag="blend_even")
+            else:
+                z_w[b, c0] = sb("z_w%d_%d" % (b, c0), [P, c1 - c0], U32)
             nc.vector.quantize_mx(
-                out=z_w[b, half][:, c0 - half * HALF : c1 - half * HALF].bitcast(FP8X4),
+                out=z_w[b, c0][:].bitcast(FP8X4),
                 scales=z_sc[b][:, c0:c1],
                 in_=woven[:].rearrange("p c i -> p (c i)"),
             )
 
         acc = {}
 
-        def out_pass(b, n, half, c0, c1, start, stop):
-            nc.tensor.matmul_mx(
-                out=acc[n, half][:, c0 - half * HALF : c1 - half * HALF],
-                lhsT=wo_w[:, b, n * P : (n + 1) * P].bitcast(FP8X4),
-                lhsT_scale=wo_sc[:, b, n * P : (n + 1) * P],
-                rhs=z_w[b, half][:, c0 - half * HALF : c1 - half * HALF].bitcast(FP8X4),
-                rhs_scale=z_sc[b][:, c0:c1],
-                start=start,
-                stop=stop,
-            )
+        def out_passes(b, q):
+            c0 = q * QUART
+            if b == 0:
+                words = z_w[0, 0][:, c0 : c0 + QUART]
+            else:
+                words = z_w[1, c0][:]
+            for n in range(3):
+                nc.tensor.matmul_mx(
+                    out=acc[q, n // 2][:, n % 2, :],
+                    lhsT=wo_w[:, b, n * P : (n + 1) * P].bitcast(FP8X4),
+                    lhsT_scale=wo_sc[:, b, n * P : (n + 1) * P],
+                    rhs=words.bitcast(FP8X4),
+                    rhs_scale=z_sc[b][:, c0 : c0 + QUART],
+                    start=(b == 0 and n != 1),
+                    stop=(b == 1 and n != 0),
+                )
 
-        direct_blend(0)
-        front_stage(1)
-        back_stage(1)
+        for s in range(DIRECT):
+            direct_gate_stage(s)
+        gate_stage(0, DIRECT, [("gap", 2), ("gap", 2), ("total", 2), ("total", 2)])
+        g = round_wa(nc.vector.tensor_copy, 0, 0, 0, 4, "wa_g00")
+        quantize_wa(g, 0, 0, 0, 0, 4)
+        g = round_wa(nc.vector.tensor_copy, 1, 0, 0, 1, "wa_g10a")
+        quantize_wa(g, 1, 0, 0, 0, 1)
+        g = round_wa(nc.scalar.copy, 1, 0, 1, 2, "wa_g10b")
+        quantize_wa(g, 1, 0, 1, 1, 2)
         g = round_wa(nc.scalar.copy, 1, 0, 2, 4, "wa_g10c")
         quantize_wa(g, 1, 0, 2, 2, 4)
+        direct_fit = [fit_stage(s) for s in range(DIRECT)]
+        direct_blend(0)
         front_stage(2)
-        acc_tags = [("fit", 2), ("fit", 2), ("score", 1), ("base_bank", 1), ("gap", 2), ("gap", 2)]
+        acc_tags = [("fit", 2), ("fit", 2), ("score", 1), ("base_bank", 1), ("gap", 2), ("gap", 2), ("total", 2), ("total", 2)]
         for s in range(SLICES):
             scatter_stage(s)
-            if s + 2 < SLICES:
-                back_stage(s + 2)
             if s == 0:
                 gate_stage(1, 0, [("score", 1)] * PACK)
-                for a in range(2):
-                    for i0 in (0, 2):
+                for i0 in (0, 2):
+                    for a in range(2):
                         g = round_wa(nc.scalar.copy, a, 1, i0, i0 + 2, "wa_g%d1%d" % (a, i0))
                         quantize_wa(g, a, 1, i0, i0, i0 + 2)
+                direct_blend(1)
+                back_stage(2)
+                front_stage(3)
+            if s + 2 < SLICES:
+                z_stage_pool(s)
+                weigh_stage(s + 2)
             if s + 3 < SLICES:
-                front_stage(s + 3)
-            if s + 1 < SLICES:
-                z_stage(s, 0, T2)
+                back_stage(s + 3)
+            if s + 4 < SLICES:
+                front_stage(s + 4)
             if s == PACK - 1:
-                first_woven = [weave_z(nc.scalar.copy, 0, c0, c0 + HALF) for c0 in range(0, T2, HALF)]
-            if s in (SLICES - 3, SLICES - 2):
-                half = s - (SLICES - 3)
-                quantize_z(first_woven[half], 0, half * HALF, (half + 1) * HALF)
-                for n in range(3):
-                    tag, bufs = acc_tags[half * 3 + n]
-                    acc[n, half] = psum.tile([P, HALF], F32, name="acc%d%d" % (n, half), tag=tag, bufs=bufs)
-                    out_pass(0, n, half, half * HALF, (half + 1) * HALF, True, False)
+                first_woven = sb("first_woven", [P, T2, PACK], BF16)
+                for q in range(4):
+                    weave_z(nc.scalar.copy, 0, first_woven[:, q * QUART : (q + 1) * QUART, :], q * QUART, 0, PACK)
+            if s == SLICES - 2:
+                z_stage(s, 0, T2)
+                quantize_z(first_woven, 0, 0, T2)
+                for q in range(4):
+                    for u in range(2):
+                        tag, bufs = acc_tags[2 * q + u]
+                        acc[q, u] = psum.tile([P, 2 - u, QUART], F32, name="acc%d%d" % (q, u), tag=tag, bufs=bufs)
+                    out_passes(0, q)
+                woven = [sb("woven%d" % q, [P, QUART, PACK], BF16) for q in range(4)]
+                for q in range(3):
+                    weave_z(nc.scalar.copy, 1, woven[q][:], q * QUART, 0, PACK - 1)
 
         last = SLICES - 1
         for q in range(4):
             z_stage(last, q * QUART, (q + 1) * QUART)
-        for q in range(4):
-            c0, c1 = q * QUART, (q + 1) * QUART
-            copy = nc.scalar.copy if q % 2 == 0 else nc.vector.tensor_copy
-            quantize_z(weave_z(copy, 1, c0, c1), 1, c0, c1)
-            for n in range(3):
-                out_pass(1, n, q // 2, c0, c1, False, q % 2 == 1)
-            if q % 2 == 1:
-                half = q // 2
-                for n in range(3):
-                    res = base[half][:, n, :]
-                    if half == 1 and n == 1:
-                        nc.vector.tensor_copy(res[:], acc[n, half][:])
-                    else:
-                        nc.scalar.copy(res[:], acc[n, half][:])
-                    nc.sync.dma_start(out=out[n * P : (n + 1) * P, half * HALF : (half + 1) * HALF], in_=res[:])
+        for q in range(3):
+            nc.scalar.copy(woven[q][:, :, PACK - 1], z_rows[1][:, PACK - 1, q * QUART : (q + 1) * QUART])
+        weave_z(nc.vector.tensor_copy, 1, woven[3][:], 3 * QUART, 0, PACK)
+        out_view = out.rearrange("(n p) t -> p n t", p=P)
+        order = (0, 3, 1, 2)
+        for q in order:
+            quantize_z(woven[q], 1, q * QUART, (q + 1) * QUART)
+            out_passes(1, q)
+        for place, q in enumerate(order):
+            cols = slice(q * QUART, (q + 1) * QUART)
+            pair = sb("pair%d" % q, [P, 2, QUART], F32, tag="minus_fit" if place % 2 else "base_t", bufs=2)
+            single = sb("single%d" % q, [P, QUART], F32)
+            if place < 2:
+                nc.scalar.copy(pair[:], acc[q, 0][:])
+                nc.scalar.copy(single[:], acc[q, 1][:, 0, :])
+            else:
+                nc.vector.tensor_copy(pair[:], acc[q, 0][:])
+                nc.scalar.copy(single[:], acc[q, 1][:, 0, :])
+            nc.sync.dma_start(out=out_view[:, 0:2, cols], in_=pair[:])
+            nc.sync.dma_start(out=out_view[:, 2, cols], in_=single[:])

@@ -26,7 +26,8 @@ PASS = P * PACK
 SLICES = H // P
 HALF = 512
 QUART = 256
-DIRECT = 2
+DIRECT = 1
+PREFILLED = (1, 2)
 PAGES = 2
 
 
@@ -59,14 +60,12 @@ def tile_list_demand_response_baseline_kernel(
 
         nc.vector.memset(tab_sc[:].rearrange("p a c -> p (a c)").bitcast(I32), 0)
         nc.vector.memset(wg_sc_raw[:].rearrange("p a c -> p (a c)").bitcast(I32), 0)
-        with tc.tile_pool(name="early", bufs=1) as early:
-            warm = early.tile([P, 2], F32, name="warm")
-            nc.gpsimd.memset(warm[:, 0:1], 0.0)
-            nc.scalar.activation(warm[:, 1:2], warm[:, 0:1], SIGMOID)
-        late = ctx.enter_context(tc.tile_pool(name="late", bufs=1))
+        warm = keep.tile([P, 2], F32, name="warm")
+        nc.gpsimd.memset(warm[:, 0:1], 0.0)
+        nc.scalar.activation(warm[:, 1:2], warm[:, 0:1], SIGMOID)
 
         def sb(name, shape, dtype, tag=None, bufs=1):
-            return late.tile(shape, dtype, name=name, tag=tag or name, bufs=bufs, align_bytes=64)
+            return keep.tile(shape, dtype, name=name, tag=tag or name, bufs=bufs, align_bytes=64)
 
         tab = [tab_first, sb("tab1", [P, T], I32)]
         wg_raw = [wg_first, sb("wg_raw1", [P, 2, 2 * PASS], U8)]
@@ -108,19 +107,18 @@ def tile_list_demand_response_baseline_kernel(
         nc.sync.dma_start(out=wa_raw[1, 0][:], in_=wa_view[1, 0])
         nc.sync.dma_start(out=base[0][:, 0, :], in_=prior_view[0, :, 0, :])
         nc.sync.dma_start(out=wgs_sb[:], in_=wgs)
-        nc.sync.dma_start(out=base[0][:, 1, :], in_=prior_view[0, :, 1, :])
-        load_wg(1)
+        nc.sync.dma_start(out=base[0][:, 1:2, :], in_=prior_view[0, :, 1:2, :])
         nc.sync.dma_start(out=wa_raw[0, 1][:], in_=wa_view[0, 1])
         nc.sync.dma_start(out=wa_raw[1, 1][:], in_=wa_view[1, 1])
+        load_wg(1)
         nc.sync.dma_start(out=base[0][:, 2:PACK, :], in_=prior_view[0, :, 2:PACK, :])
         load_ld(0)
         nc.sync.dma_start(out=base[1][:], in_=prior_view[1])
-        load_ld(1)
         nc.sync.dma_start(
             out=wo_w[:], in_=wo_words.rearrange("a p c i -> a p (c i)").bitcast(I32).rearrange("a p c -> p a c")
         )
         load_scale_rows(nc.sync, wo_sc, wo_scales)
-        for s in range(2, SLICES):
+        for s in range(1, SLICES):
             load_ld(s)
 
         v_w = [sb("v_w%d" % a, [P, S], U32) for a in range(2)]
@@ -165,7 +163,7 @@ def tile_list_demand_response_baseline_kernel(
         gate_t = {}
 
         def gate_stage(b, first, tags):
-            gate_t[b] = sb("gate_t%d" % b, [P, PACK, S], F32, tag=None if b == 0 else "wa_raw10")
+            gate_t[b] = sb("gate_t%d" % b, [P, PACK, S], F32, tag=None if b == 0 else "wa_raw01")
             for c in range(S // P):
                 tag, bufs = tags[c]
                 score = psum.tile([P, PASS], F32, name="score%d%d" % (b, c), tag=tag, bufs=bufs)
@@ -188,7 +186,7 @@ def tile_list_demand_response_baseline_kernel(
 
         def fit_stage(s):
             b, i = divmod(s, PACK)
-            fit = psum.tile([P, S], F32, name="fit%d" % s, tag="total" if s < DIRECT else "fit", bufs=2)
+            fit = psum.tile([P, S], F32, name="fit%d" % s, tag="total" if s < DIRECT else "fit", bufs=2 if s < DIRECT else 1)
             for a in range(2):
                 nc.tensor.matmul_mx(
                     out=fit[:],
@@ -216,12 +214,16 @@ def tile_list_demand_response_baseline_kernel(
                 )
 
         def blend_tile(s):
-            return sb("blend%d" % s, [P, S], F32, tag="wa_g112" if s % 2 else "blend_even")
+            if s == SLICES - 1:
+                return ld[s - 2][:, 0:S]
+            if s >= 3:
+                return ld[s - 3][:, 0:S]
+            return sb("blend%d" % s, [P, S], F32, tag="wa_g012" if s % 2 else "blend_even")[:]
 
         direct_gate = {}
 
         def direct_gate_stage(s):
-            score = psum.tile([P, S], F32, name="score%d" % s, tag="score" if s == 0 else "base_bank")
+            score = psum.tile([P, S], F32, name="score%d" % s, tag="score", bufs=2)
             for a in range(2):
                 nc.tensor.matmul_mx(
                     out=score[:],
@@ -237,44 +239,39 @@ def tile_list_demand_response_baseline_kernel(
 
         def direct_blend(s):
             gate = direct_gate[s]
-            fit = direct_fit[s]
-            diff = sb("diff%d" % s, [P, S], F32, tag="diff")
-            moved = ring("moved", s, 1)
+            fit = fit_stage(s)
+            kept = sb("kept", [P, S], F32)
+            moved = sb("moved", [P, S], F32)
             blend[s] = blend_tile(s)
-            mixed = blend[s] if s == 0 else diff
+            nc.vector.scalar_tensor_tensor(kept[:], gate[:], 1.0, base_of(s), SUB, MULT)
             halves = [slice(0, S // 2), slice(S // 2, S)]
             for cols in halves:
-                nc.vector.tensor_tensor(diff[:, cols], fit[:, cols], base_of(s)[:, cols], SUB)
+                nc.vector.tensor_tensor(moved[:, cols], fit[:, cols], gate[:, cols], MULT)
             for cols in halves:
-                nc.vector.tensor_tensor(moved[:, cols], diff[:, cols], gate[:, cols], MULT)
-            for cols in halves:
-                nc.vector.tensor_tensor(mixed[:, cols], moved[:, cols], base_of(s)[:, cols], ADD)
-            if s > 0:
-                for cols in halves:
-                    nc.vector.tensor_tensor(blend[s][:, cols], mixed[:, cols], wgs_sb[:, cols], MULT)
+                nc.vector.tensor_tensor(blend[s][:, cols], moved[:, cols], kept[:, cols], SUB)
 
         turned = {}
 
         def front_stage(s):
             gate = gate_t[s // PACK][:, s % PACK, :]
             fit = fit_stage(s)
-            minus_fit = ring("minus_fit", s, 2)
-            nc.scalar.activation(minus_fit[:], fit[:], COPY, scale=-1.0)
+            minus_fit = wa_raw[1, 1][:, 0, :] if s == 3 else ring("minus_fit", s, 2)[:]
+            nc.scalar.activation(minus_fit, fit[:], COPY, scale=-1.0)
             gap = psum.tile([P, S], F32, name="gap%d" % s, tag="gap", bufs=2)
             turn_into(gap, base_of(s), True, False)
             turn_into(gap, minus_fit, False, True)
             base_bank = psum.tile([P, S], F32, name="base_bank%d" % s, tag="base_bank")
             turn_into(base_bank, base_of(s), True, True)
-            base_t = ring("base_t", s, 2)
-            nc.scalar.copy(base_t[:], base_bank[:])
+            base_t = wa_raw[1, 1][:, 1, :] if s == 3 else ring("base_t", s, 2)[:]
+            nc.scalar.copy(base_t, base_bank[:])
             turned[s] = (gap, gate, base_t)
 
         totals = {}
 
         def back_stage(s):
             gap, gate, base_t = turned[s]
-            moved = ring("turned_moved", s, 2)
-            nc.vector.scalar_tensor_tensor(moved[:], gap[:], -1.0, gate, MULT, MULT)
+            moved = ld[s - 4][:, S : 2 * S] if s >= 4 else ring("turned_moved", s, 2)[:]
+            nc.vector.scalar_tensor_tensor(moved, gap[:], -1.0, gate, MULT, MULT)
             totals[s] = psum.tile([P, S], F32, name="total%d" % s, tag="total", bufs=2)
             turn_into(totals[s], base_t, True, False)
             turn_into(totals[s], moved, False, True)
@@ -282,19 +279,19 @@ def tile_list_demand_response_baseline_kernel(
         def weigh_stage(s):
             blend[s] = blend_tile(s)
             if s == SLICES - 1:
-                nc.scalar.copy(blend[s][:], totals[s][:])
+                nc.scalar.copy(blend[s], totals[s][:])
             else:
-                nc.vector.tensor_tensor(blend[s][:], totals[s][:], wgs_sb[:], MULT)
+                nc.vector.tensor_tensor(blend[s], totals[s][:], wgs_sb[:], MULT)
 
         def page_of(s):
-            return pages[min(s, SLICES - 2) % 2]
+            return pages[s % 2]
 
         def scatter_stage(s):
             window = page_of(s)[:].indirect(idx2[:])
             if s in (0, SLICES - 1):
-                nc.vector.tensor_tensor(window, blend[s][:], wgs_sb[:], MULT)
+                nc.vector.tensor_tensor(window, blend[s], wgs_sb[:], MULT)
             else:
-                nc.vector.tensor_copy(window, blend[s][:])
+                nc.vector.tensor_copy(window, blend[s])
 
         z_rows = [sb("z_rows%d" % b, [P, PACK, T2], BF16) for b in range(2)]
         z_w = {}
@@ -308,7 +305,7 @@ def tile_list_demand_response_baseline_kernel(
 
         def z_stage_pool(s):
             b, i = divmod(s, PACK)
-            factor = sb("factor%d" % s, [P, T2], F32, tag="diff")
+            factor = sb("factor%d" % s, [P, T2], F32, tag="wa_g112")
             nc.gpsimd.tensor_scalar(factor[:], page_of(s)[:], 1.0, 1.0, MULT, ADD)
             nc.gpsimd.tensor_tensor(z_rows[b][:, i, :], factor[:], ld[s][:], MULT)
 
@@ -320,7 +317,7 @@ def tile_list_demand_response_baseline_kernel(
 
         def quantize_z(woven, b, c0, c1):
             if b == 0:
-                z_w[b, c0] = sb("z_w%d_%d" % (b, c0), [P, c1 - c0], U32, tag="blend_even")
+                z_w[b, c0] = sb("z_w%d_%d" % (b, c0), [P, c1 - c0], U32, tag="ld3")
             else:
                 z_w[b, c0] = sb("z_w%d_%d" % (b, c0), [P, c1 - c0], U32)
             nc.vector.quantize_mx(
@@ -351,31 +348,32 @@ def tile_list_demand_response_baseline_kernel(
         for s in range(DIRECT):
             direct_gate_stage(s)
         gate_stage(0, DIRECT, [("gap", 2), ("gap", 2), ("total", 2), ("total", 2)])
-        g = round_wa(nc.vector.tensor_copy, 0, 0, 0, 4, "wa_g00")
+        g = round_wa(nc.vector.tensor_copy, 0, 0, 0, 4, "wa_g000")
         quantize_wa(g, 0, 0, 0, 0, 4)
-        g = round_wa(nc.vector.tensor_copy, 1, 0, 0, 1, "wa_g10a")
+        g = round_wa(nc.vector.tensor_copy, 1, 0, 0, 1, "wa_g100")
         quantize_wa(g, 1, 0, 0, 0, 1)
-        g = round_wa(nc.scalar.copy, 1, 0, 1, 2, "wa_g10b")
-        quantize_wa(g, 1, 0, 1, 1, 2)
-        g = round_wa(nc.scalar.copy, 1, 0, 2, 4, "wa_g10c")
-        quantize_wa(g, 1, 0, 2, 2, 4)
-        direct_fit = [fit_stage(s) for s in range(DIRECT)]
         direct_blend(0)
+        for a, i0, i1 in ((1, 1, 2), (1, 2, 4)):
+            g = round_wa(nc.scalar.copy, a, 0, i0, i1, "wa_g%d0%d" % (a, i0))
+            quantize_wa(g, a, 0, i0, i0, i1)
+        front_stage(1)
         front_stage(2)
-        acc_tags = [("fit", 2), ("fit", 2), ("score", 1), ("base_bank", 1), ("gap", 2), ("gap", 2), ("total", 2), ("total", 2)]
+        acc_tags = [("fit", 1), ("score", 2), ("score", 2), ("base_bank", 1), ("gap", 2), ("gap", 2), ("total", 2), ("total", 2)]
         for s in range(SLICES):
             scatter_stage(s)
             if s == 0:
-                gate_stage(1, 0, [("score", 1)] * PACK)
                 for i0 in (0, 2):
                     for a in range(2):
                         g = round_wa(nc.scalar.copy, a, 1, i0, i0 + 2, "wa_g%d1%d" % (a, i0))
                         quantize_wa(g, a, 1, i0, i0, i0 + 2)
-                direct_blend(1)
+                back_stage(1)
                 back_stage(2)
+                weigh_stage(1)
+                gate_stage(1, 0, [("score", 2)] * PACK)
                 front_stage(3)
-            if s + 2 < SLICES:
+            if s < SLICES - 2:
                 z_stage_pool(s)
+            if s + 2 < SLICES:
                 weigh_stage(s + 2)
             if s + 3 < SLICES:
                 back_stage(s + 3)
@@ -394,29 +392,32 @@ def tile_list_demand_response_baseline_kernel(
                         acc[q, u] = psum.tile([P, 2 - u, QUART], F32, name="acc%d%d" % (q, u), tag=tag, bufs=bufs)
                     out_passes(0, q)
                 woven = [sb("woven%d" % q, [P, QUART, PACK], BF16) for q in range(4)]
-                for q in range(3):
+                for q in PREFILLED:
                     weave_z(nc.scalar.copy, 1, woven[q][:], q * QUART, 0, PACK - 1)
 
         last = SLICES - 1
+        out_view = out.rearrange("(n p) t -> p n t", p=P)
         for q in range(4):
             z_stage(last, q * QUART, (q + 1) * QUART)
-        for q in range(3):
-            nc.scalar.copy(woven[q][:, :, PACK - 1], z_rows[1][:, PACK - 1, q * QUART : (q + 1) * QUART])
-        weave_z(nc.vector.tensor_copy, 1, woven[3][:], 3 * QUART, 0, PACK)
-        out_view = out.rearrange("(n p) t -> p n t", p=P)
-        order = (0, 3, 1, 2)
-        for q in order:
+            if q in PREFILLED:
+                nc.scalar.copy(woven[q][:, :, PACK - 1], z_rows[1][:, PACK - 1, q * QUART : (q + 1) * QUART])
+            if q == 1:
+                weave_z(nc.vector.tensor_copy, 1, woven[0][:], 0, 0, PACK)
+            if q == 2:
+                quantize_z(woven[0], 1, 0, QUART)
+                out_passes(1, 0)
+        for q in range(1, 4):
             quantize_z(woven[q], 1, q * QUART, (q + 1) * QUART)
             out_passes(1, q)
-        for place, q in enumerate(order):
+            if q == 1:
+                weave_z(nc.vector.tensor_copy, 1, woven[3][:], 3 * QUART, 0, PACK)
+        for q in range(4):
             cols = slice(q * QUART, (q + 1) * QUART)
-            pair = sb("pair%d" % q, [P, 2, QUART], F32, tag="minus_fit" if place % 2 else "base_t", bufs=2)
+            pair = sb("pair%d" % q, [P, 2, QUART], F32, tag="minus_fit" if q % 2 else "base_t", bufs=2)
             single = sb("single%d" % q, [P, QUART], F32)
-            if place < 2:
-                nc.scalar.copy(pair[:], acc[q, 0][:])
-                nc.scalar.copy(single[:], acc[q, 1][:, 0, :])
-            else:
-                nc.vector.tensor_copy(pair[:], acc[q, 0][:])
-                nc.scalar.copy(single[:], acc[q, 1][:, 0, :])
+            copy_pair = nc.vector.tensor_copy if q == 3 else nc.scalar.copy
+            copy_single = nc.vector.tensor_copy if q == 2 else nc.scalar.copy
+            copy_pair(pair[:], acc[q, 0][:])
+            copy_single(single[:], acc[q, 1][:, 0, :])
             nc.sync.dma_start(out=out_view[:, 0:2, cols], in_=pair[:])
             nc.sync.dma_start(out=out_view[:, 2, cols], in_=single[:])

@@ -23,18 +23,20 @@ COPY = mybir.ActivationFunctionType.Copy
 P = 128
 PACK = 4
 PASS = P * PACK
+PASSES = 2
 SLICES = H // P
-HALF = 512
-QUART = 256
-DIRECT = 1
-PREFILLED = (1, 2)
-PAGES = 2
+LAST = SLICES - 1
+POOL_SLICES = SLICES - 2
+QUARTERS = 4
+QUART = T2 // QUARTERS
+N_TILES = N // P
+NEIGHBOURS = 4
 
 
-def load_scale_rows(queue, plane, scales):
+def load_scale_rows(nc, plane, scales):
     rows = scales.bitcast(I32)
     for q in range(4):
-        queue.dma_start(
+        nc.sync.dma_start(
             out=plane[32 * q : 32 * q + 4, :, :].bitcast(I32),
             in_=rows[:, 4 * q : 4 * q + 4, :].rearrange("a r c -> r a c"),
         )
@@ -48,146 +50,160 @@ def tile_list_demand_response_baseline_kernel(
         keep = ctx.enter_context(tc.tile_pool(name="keep", bufs=1))
         psum = ctx.enter_context(tc.psum_pool(name="psum", bufs=1))
 
+        def sb(name, shape, dtype, tag=None, bufs=1):
+            return keep.tile(shape, dtype, name=name, tag=tag or name, bufs=bufs, align_bytes=64)
+
+        bank_count = {"fit": 1, "score": 2, "prior_t": 1, "gap": 2, "total": 2}
+
+        def bank(name, shape, role):
+            return psum.tile(shape, F32, name=name, tag=role, bufs=bank_count[role])
+
         idx = keep.tile([P, S // 16], U16, name="idx")
         idx2 = keep.tile([P, S // 16], U16, name="idx2")
-        tab_sc = keep.tile([P, 2, T], U8, name="tab_sc", align_bytes=64)
-        wg_sc_raw = keep.tile([P, 2, H], U8, name="wg_sc_raw", align_bytes=64)
-        wo_sc = keep.tile([P, 2, N], U8, name="wo_sc", align_bytes=64)
-        wg_first = keep.tile([P, 2, 2 * PASS], U8, name="wg_raw0", align_bytes=64)
-        tab_first = keep.tile([P, T], I32, name="tab0", align_bytes=64)
-        pages = [keep.tile([P, T2], F32, name="page%d" % n, align_bytes=64) for n in range(PAGES)]
-        ident = keep.tile([P, P], F32, name="ident", align_bytes=64)
+        tab_sc = sb("tab_sc", [P, PASSES, T], U8)
+        wg_sc = sb("wg_sc", [P, PASSES, H], U8)
+        wo_sc = sb("wo_sc", [P, PASSES, N], U8)
+        wg_w = [sb("wg_w0", [P, PASSES, 2 * PASS], U8)]
+        tab_w = [sb("tab_w0", [P, T], I32)]
+        pages = [sb("page%d" % n, [P, T2], F32) for n in range(2)]
+        ident = sb("ident", [P, P], F32)
 
         nc.vector.memset(tab_sc[:].rearrange("p a c -> p (a c)").bitcast(I32), 0)
-        nc.vector.memset(wg_sc_raw[:].rearrange("p a c -> p (a c)").bitcast(I32), 0)
+        nc.vector.memset(wg_sc[:].rearrange("p a c -> p (a c)").bitcast(I32), 0)
+
         warm = keep.tile([P, 2], F32, name="warm")
         nc.gpsimd.memset(warm[:, 0:1], 0.0)
         nc.scalar.activation(warm[:, 1:2], warm[:, 0:1], SIGMOID)
 
-        def sb(name, shape, dtype, tag=None, bufs=1):
-            return keep.tile(shape, dtype, name=name, tag=tag or name, bufs=bufs, align_bytes=64)
-
-        tab = [tab_first, sb("tab1", [P, T], I32)]
-        wg_raw = [wg_first, sb("wg_raw1", [P, 2, 2 * PASS], U8)]
+        tab_w.append(sb("tab_w1", [P, T], I32))
+        wg_w.append(sb("wg_w1", [P, PASSES, 2 * PASS], U8))
         wa_raw = {}
-        for a in range(2):
-            for b in range(2):
+        for a in range(PASSES):
+            for b in range(PASSES):
                 wa_raw[a, b] = sb("wa_raw%d%d" % (a, b), [P, PACK, PASS], F32)
-        base = [sb("base%d" % b, [P, PACK, S], F32) for b in range(2)]
+        prior_sb = [sb("prior%d" % b, [P, PACK, S], F32) for b in range(PASSES)]
         wgs_sb = sb("wgs_sb", [P, S], F32)
-        ld = [sb("ld%d" % s, [P, T2], F32) for s in range(SLICES)]
-        wo_w = sb("wo_w", [P, 2, N], I32)
+        load_sb = [sb("load%d" % s, [P, T2], F32) for s in range(SLICES)]
+        wo_w = sb("wo_w", [P, PASSES, N], I32)
         make_identity(nc, ident[:])
 
         for page in pages:
             nc.gpsimd.memset(page[:], 0.0)
         nc.gpsimd.memset(wo_sc[:].rearrange("p a c -> p (a c)").bitcast(I32), 0)
-        wa_view = wa.rearrange("(a p j) (b c) -> a b p j c", a=2, j=PACK, b=2)
-        prior_view = prior.rearrange("(b p i) j -> b p i j", b=2, i=PACK)
-        load_view = load.rearrange("(b p i) t -> b i p t", b=2, i=PACK)
 
-        def load_tab(a):
-            nc.sync.dma_start(out=tab[a][:], in_=tab_words[a].rearrange("p t i -> p (t i)").bitcast(I32))
+        wa_view = wa.rearrange("(a p j) (b c) -> a b p j c", a=PASSES, j=PACK, b=PASSES)
+        prior_view = prior.rearrange("(b p i) j -> b p i j", b=PASSES, i=PACK)
+        load_view = load.rearrange("(b p i) t -> b i p t", b=PASSES, i=PACK)
 
-        def load_wg(b):
-            words = wg_words.bitcast(I32).rearrange("a p (b c) -> b p a c", b=2)
-            nc.sync.dma_start(out=wg_raw[b][:].bitcast(I32), in_=words[b])
+        def fetch_tab(a):
+            nc.sync.dma_start(out=tab_w[a][:], in_=tab_words[a].rearrange("p t i -> p (t i)").bitcast(I32))
 
-        def load_ld(s):
-            nc.sync.dma_start(out=ld[s][:], in_=load_view[s // PACK, s % PACK])
+        def fetch_wg(b):
+            words = wg_words.bitcast(I32).rearrange("a p (b c) -> b p a c", b=PASSES)
+            nc.sync.dma_start(out=wg_w[b][:].bitcast(I32), in_=words[b])
+
+        def fetch_wa(b):
+            for a in range(PASSES):
+                nc.sync.dma_start(out=wa_raw[a, b][:], in_=wa_view[a, b])
+
+        def fetch_prior(b, i0, i1):
+            nc.sync.dma_start(out=prior_sb[b][:, i0:i1, :], in_=prior_view[b, :, i0:i1, :])
+
+        def fetch_load(s):
+            nc.sync.dma_start(out=load_sb[s][:], in_=load_view[s // PACK, s % PACK])
 
         nc.sync.dma_start(idx[:], offs)
         nc.sync.dma_start(idx2[:], offs2)
-        load_tab(0)
-        load_wg(0)
-        load_scale_rows(nc.sync, tab_sc, tab_scales)
-        load_tab(1)
-        load_scale_rows(nc.sync, wg_sc_raw, wg_scales)
-        nc.sync.dma_start(out=wa_raw[0, 0][:], in_=wa_view[0, 0])
-        nc.sync.dma_start(out=wa_raw[1, 0][:], in_=wa_view[1, 0])
-        nc.sync.dma_start(out=base[0][:, 0, :], in_=prior_view[0, :, 0, :])
+        fetch_tab(0)
+        fetch_wg(0)
+        load_scale_rows(nc, tab_sc, tab_scales)
+        fetch_tab(1)
+        load_scale_rows(nc, wg_sc, wg_scales)
+        fetch_wa(0)
+        nc.sync.dma_start(out=prior_sb[0][:, 0, :], in_=prior_view[0, :, 0, :])
         nc.sync.dma_start(out=wgs_sb[:], in_=wgs)
-        nc.sync.dma_start(out=base[0][:, 1:2, :], in_=prior_view[0, :, 1:2, :])
-        nc.sync.dma_start(out=wa_raw[0, 1][:], in_=wa_view[0, 1])
-        nc.sync.dma_start(out=wa_raw[1, 1][:], in_=wa_view[1, 1])
-        load_wg(1)
-        nc.sync.dma_start(out=base[0][:, 2:PACK, :], in_=prior_view[0, :, 2:PACK, :])
-        load_ld(0)
-        nc.sync.dma_start(out=base[1][:], in_=prior_view[1])
+        fetch_prior(0, 1, 3)
+        fetch_load(0)
+        fetch_wa(1)
+        fetch_prior(0, 3, PACK)
+        fetch_wg(1)
+        nc.sync.dma_start(out=prior_sb[1][:], in_=prior_view[1])
         nc.sync.dma_start(
             out=wo_w[:], in_=wo_words.rearrange("a p c i -> a p (c i)").bitcast(I32).rearrange("a p c -> p a c")
         )
-        load_scale_rows(nc.sync, wo_sc, wo_scales)
+        load_scale_rows(nc, wo_sc, wo_scales)
         for s in range(1, SLICES):
-            load_ld(s)
+            fetch_load(s)
 
-        v_w = [sb("v_w%d" % a, [P, S], U32) for a in range(2)]
-        v_sc = [sb("v_sc%d" % a, [P, S], U8) for a in range(2)]
-        wg_w = sb("wg_w", [P, 2, DIRECT, 2 * P], U8)
-        wg_sc = sb("wg_sc", [P, 2, DIRECT, P], U8)
-        nc.vector.tensor_copy(v_w[0][:], tab[0][:].bitcast(U32).indirect(idx[:]))
-        for a in range(2):
+        v_w = [sb("v_w%d" % a, [P, S], U32) for a in range(PASSES)]
+        v_sc = [sb("v_sc%d" % a, [P, S], U8) for a in range(PASSES)]
+        nc.vector.tensor_copy(v_w[0][:], tab_w[0][:].bitcast(U32).indirect(idx[:]))
+        for a in range(PASSES):
             nc.vector.tensor_copy(v_sc[a][:], tab_sc[:, a, :].indirect(idx[:]))
-        nc.vector.tensor_copy(v_w[1][:], tab[1][:].bitcast(U32).indirect(idx[:]))
+        nc.vector.tensor_copy(v_w[1][:], tab_w[1][:].bitcast(U32).indirect(idx[:]))
+
+        first_wg_w = sb("first_wg_w", [P, PASSES, 1, 2 * P], U8)
+        first_wg_sc = sb("first_wg_sc", [P, PASSES, 1, P], U8)
         nc.vector.tensor_copy(
-            out=wg_w[:].bitcast(U16),
-            in_=wg_raw[0][:].bitcast(U16).rearrange("p a (m i) -> p a i m", i=PACK)[:, :, 0:DIRECT, :],
+            out=first_wg_w[:].bitcast(U16),
+            in_=wg_w[0][:].bitcast(U16).rearrange("p a (m i) -> p a i m", i=PACK)[:, :, 0:1, :],
         )
         nc.vector.tensor_copy(
-            out=wg_sc[:], in_=wg_sc_raw[:, :, 0:PASS].rearrange("p a (m i) -> p a i m", i=PACK)[:, :, 0:DIRECT, :]
+            out=first_wg_sc[:], in_=wg_sc[:, :, 0:PASS].rearrange("p a (m i) -> p a i m", i=PACK)[:, :, 0:1, :]
         )
 
         wa_w = {}
         wa_sc = {}
-        for a in range(2):
-            for b in range(2):
+        for a in range(PASSES):
+            for b in range(PASSES):
                 wa_w[a, b] = sb("wa_w%d%d" % (a, b), [P, PASS], U32)
                 wa_sc[a, b] = sb("wa_sc%d%d" % (a, b), [P, PASS], U8)
 
-        def round_wa(copy, a, b, i0, i1, name):
-            grouped = sb(name, [P, i1 - i0, P, PACK], BF16)
+        def round_wa(copy, rounded, a, b, i0, i1):
             copy(
-                out=grouped[:].rearrange("p i m j -> p m j i"),
+                out=rounded.rearrange("p i m j -> p m j i"),
                 in_=wa_raw[a, b][:].rearrange("p j (m i) -> p m j i", i=PACK)[:, :, :, i0:i1],
             )
-            return grouped
 
-        def quantize_wa(grouped, a, b, i_first, i0, i1):
+        def quantize_wa(rounded, a, b, i0, i1):
             nc.vector.quantize_mx(
                 out=wa_w[a, b][:, i0 * P : i1 * P].bitcast(FP8X4),
                 scales=wa_sc[a, b][:, i0 * P : i1 * P],
-                in_=grouped[:, i0 - i_first : i1 - i_first, :, :].rearrange("p i m j -> p (i m j)"),
+                in_=rounded.rearrange("p i m j -> p (i m j)"),
             )
 
-        blend = {}
+        def first_half_of_wa(copy, a, i0, i1):
+            rounded = sb("wa_rounded%d0%d" % (a, i0), [P, i1 - i0, P, PACK], BF16)[:]
+            round_wa(copy, rounded, a, 0, i0, i1)
+            quantize_wa(rounded, a, 0, i0, i1)
+
         gate_t = {}
 
-        def gate_stage(b, first, tags):
-            gate_t[b] = sb("gate_t%d" % b, [P, PACK, S], F32, tag=None if b == 0 else "wa_raw01")
+        def turned_gates(b, first, roles):
+            gate_t[b] = sb("gate_t%d" % b, [P, PACK, S], F32, tag="wa_raw11" if b else None)
             for c in range(S // P):
-                tag, bufs = tags[c]
-                score = psum.tile([P, PASS], F32, name="score%d%d" % (b, c), tag=tag, bufs=bufs)
+                score = bank("score%d%d" % (b, c), [P, PASS], roles[c])
                 cols = slice(c * P, (c + 1) * P)
-                for a in range(2):
+                for a in range(PASSES):
                     nc.tensor.matmul_mx(
                         out=score[:],
                         lhsT=v_w[a][:, cols].bitcast(FP8X4),
                         lhsT_scale=v_sc[a][:, cols],
-                        rhs=wg_raw[b][:, a, :].bitcast(FP4X4),
-                        rhs_scale=wg_sc_raw[:, a, b * PASS : (b + 1) * PASS],
+                        rhs=wg_w[b][:, a, :].bitcast(FP4X4),
+                        rhs_scale=wg_sc[:, a, b * PASS : (b + 1) * PASS],
                         start=(a == 0),
-                        stop=(a == 1),
+                        stop=(a == PASSES - 1),
                     )
                 nc.scalar.activation(
                     gate_t[b][:, first:PACK, cols],
-                    score[:].rearrange("j (m i) -> j i m", i=PACK)[:, first:PACK, :],
+                    score[:].rearrange("e (m i) -> e i m", i=PACK)[:, first:PACK, :],
                     SIGMOID,
                 )
 
-        def fit_stage(s):
+        def make_fit(s, role):
             b, i = divmod(s, PACK)
-            fit = psum.tile([P, S], F32, name="fit%d" % s, tag="total" if s < DIRECT else "fit", bufs=2 if s < DIRECT else 1)
-            for a in range(2):
+            fit = bank("fit%d" % s, [P, S], role)
+            for a in range(PASSES):
                 nc.tensor.matmul_mx(
                     out=fit[:],
                     lhsT=wa_w[a, b][:, i * P : (i + 1) * P].bitcast(FP8X4),
@@ -195,229 +211,236 @@ def tile_list_demand_response_baseline_kernel(
                     rhs=v_w[a][:].bitcast(FP8X4),
                     rhs_scale=v_sc[a][:],
                     start=(a == 0),
-                    stop=(a == 1),
+                    stop=(a == PASSES - 1),
                 )
             return fit
 
-        def base_of(s):
-            return base[s // PACK][:, s % PACK, :]
+        def prior_of(s):
+            return prior_sb[s // PACK][:, s % PACK, :]
 
-        def ring(name, s, bufs):
-            return sb("%s%d" % (name, s), [P, S], F32, tag=name, bufs=bufs)
-
-        def turn_into(bank, src, start, stop):
+        def turn_into(target, src, start, stop):
             for c in range(S // P):
                 cols = slice(c * P, (c + 1) * P)
                 nc.tensor.matmul(
-                    bank[:, cols], src[:, cols], ident[:], is_transpose=True,
-                    start=(start and c == 0), stop=(stop and c == S // P - 1),
+                    target[:, cols],
+                    src[:, cols],
+                    ident[:],
+                    is_transpose=True,
+                    start=(start and c == 0),
+                    stop=(stop and c == S // P - 1),
                 )
 
-        def blend_tile(s):
-            if s == SLICES - 1:
-                return ld[s - 2][:, 0:S]
-            if s >= 3:
-                return ld[s - 3][:, 0:S]
-            return sb("blend%d" % s, [P, S], F32, tag="wa_g012" if s % 2 else "blend_even")[:]
+        shared = sb("shared", [P, S + T2], F32)
+        shared_wa = shared[:, S // 2 : S // 2 + T2].bitcast(BF16).rearrange("p (i m j) -> p i m j", i=PACK, j=PACK)
+        shared_step = shared[:, 0:S]
+        shared_factor = shared[:, S : S + T2]
 
-        direct_gate = {}
+        def source_room(s):
+            if s < 2:
+                return sb("source%d" % s, [P, S], F32)[:]
+            if s == 2:
+                return gate_t[0][:, 3, :]
+            if s == LAST:
+                return load_sb[POOL_SLICES - 1][:, 0:S]
+            return load_sb[s - 3][:, 0:S]
 
-        def direct_gate_stage(s):
-            score = psum.tile([P, S], F32, name="score%d" % s, tag="score", bufs=2)
-            for a in range(2):
+        def step_room(s):
+            if s == 1:
+                return sb("step1", [P, S], F32, tag="minus_fit_of_2")[:]
+            if s == 2:
+                return sb("step2", [P, S], F32)[:]
+            if s == 3:
+                return shared_step
+            return load_sb[s - 4][:, S : 2 * S]
+
+        source = {}
+
+        def first_gate():
+            score = bank("first_score", [P, S], "score")
+            for a in range(PASSES):
                 nc.tensor.matmul_mx(
                     out=score[:],
-                    lhsT=wg_w[:, a, s, :].bitcast(FP4X4),
-                    lhsT_scale=wg_sc[:, a, s, :],
+                    lhsT=first_wg_w[:, a, 0, :].bitcast(FP4X4),
+                    lhsT_scale=first_wg_sc[:, a, 0, :],
                     rhs=v_w[a][:].bitcast(FP8X4),
                     rhs_scale=v_sc[a][:],
                     start=(a == 0),
-                    stop=(a == 1),
+                    stop=(a == PASSES - 1),
                 )
-            direct_gate[s] = ring("gate", s, DIRECT)
-            nc.scalar.activation(direct_gate[s][:], score[:], SIGMOID)
+            gate = sb("first_gate", [P, S], F32)
+            nc.scalar.activation(gate[:], score[:], SIGMOID)
+            return gate
 
-        def direct_blend(s):
-            gate = direct_gate[s]
-            fit = fit_stage(s)
+        def first_h(gate):
+            fit = make_fit(0, "total")
             kept = sb("kept", [P, S], F32)
-            moved = sb("moved", [P, S], F32)
-            blend[s] = blend_tile(s)
-            nc.vector.scalar_tensor_tensor(kept[:], gate[:], 1.0, base_of(s), SUB, MULT)
+            taken = sb("taken", [P, S], F32)
+            source[0] = source_room(0)
+            nc.vector.scalar_tensor_tensor(kept[:], gate[:], 1.0, prior_of(0), SUB, MULT)
             halves = [slice(0, S // 2), slice(S // 2, S)]
             for cols in halves:
-                nc.vector.tensor_tensor(moved[:, cols], fit[:, cols], gate[:, cols], MULT)
+                nc.vector.tensor_tensor(taken[:, cols], fit[:, cols], gate[:, cols], MULT)
             for cols in halves:
-                nc.vector.tensor_tensor(blend[s][:, cols], moved[:, cols], kept[:, cols], SUB)
+                nc.vector.tensor_tensor(source[0][:, cols], taken[:, cols], kept[:, cols], SUB)
 
-        turned = {}
+        gap = {}
+        prior_t = {}
+        total = {}
 
-        def front_stage(s):
-            gate = gate_t[s // PACK][:, s % PACK, :]
-            fit = fit_stage(s)
-            minus_fit = wa_raw[1, 1][:, 0, :] if s == 3 else ring("minus_fit", s, 2)[:]
-            nc.scalar.activation(minus_fit, fit[:], COPY, scale=-1.0)
-            gap = psum.tile([P, S], F32, name="gap%d" % s, tag="gap", bufs=2)
-            turn_into(gap, base_of(s), True, False)
-            turn_into(gap, minus_fit, False, True)
-            base_bank = psum.tile([P, S], F32, name="base_bank%d" % s, tag="base_bank")
-            turn_into(base_bank, base_of(s), True, True)
-            base_t = wa_raw[1, 1][:, 1, :] if s == 3 else ring("base_t", s, 2)[:]
-            nc.scalar.copy(base_t, base_bank[:])
-            turned[s] = (gap, gate, base_t)
-
-        totals = {}
-
-        def back_stage(s):
-            gap, gate, base_t = turned[s]
-            moved = ld[s - 4][:, S : 2 * S] if s >= 4 else ring("turned_moved", s, 2)[:]
-            nc.vector.scalar_tensor_tensor(moved, gap[:], -1.0, gate, MULT, MULT)
-            totals[s] = psum.tile([P, S], F32, name="total%d" % s, tag="total", bufs=2)
-            turn_into(totals[s], base_t, True, False)
-            turn_into(totals[s], moved, False, True)
-
-        def weigh_stage(s):
-            blend[s] = blend_tile(s)
-            if s == SLICES - 1:
-                nc.scalar.copy(blend[s], totals[s][:])
+        def make_gap(s):
+            fit = make_fit(s, "fit")
+            if s == 2:
+                minus_fit = sb("minus_fit2", [P, S], F32, tag="minus_fit_of_2")
             else:
-                nc.vector.tensor_tensor(blend[s], totals[s][:], wgs_sb[:], MULT)
+                minus_fit = sb("minus_fit%d" % s, [P, S], F32, tag="minus_fit", bufs=2)
+            nc.scalar.activation(minus_fit[:], fit[:], COPY, scale=-1.0)
+            gap[s] = bank("gap%d" % s, [P, S], "gap")
+            turn_into(gap[s], prior_of(s), True, False)
+            turn_into(gap[s], minus_fit, False, True)
+            turned = bank("turned_prior%d" % s, [P, S], "prior_t")
+            turn_into(turned, prior_of(s), True, True)
+            prior_t[s] = sb("prior_t%d" % s, [P, S], F32, tag="prior_t", bufs=2)
+            nc.scalar.copy(prior_t[s][:], turned[:])
 
-        def page_of(s):
-            return pages[s % 2]
+        def make_total(s):
+            step = step_room(s)
+            nc.vector.scalar_tensor_tensor(step, gap[s][:], -1.0, gate_t[s // PACK][:, s % PACK, :], MULT, MULT)
+            total[s] = bank("total%d" % s, [P, S], "total")
+            turn_into(total[s], prior_t[s], True, False)
+            turn_into(total[s], step, False, True)
 
-        def scatter_stage(s):
-            window = page_of(s)[:].indirect(idx2[:])
-            if s in (0, SLICES - 1):
-                nc.vector.tensor_tensor(window, blend[s], wgs_sb[:], MULT)
+        def make_source(s):
+            source[s] = source_room(s)
+            if s == LAST:
+                nc.scalar.copy(source[s], total[s][:])
             else:
-                nc.vector.tensor_copy(window, blend[s])
+                nc.vector.tensor_tensor(source[s], total[s][:], wgs_sb[:], MULT)
 
-        z_rows = [sb("z_rows%d" % b, [P, PACK, T2], BF16) for b in range(2)]
-        z_w = {}
-        z_sc = [sb("z_sc%d" % b, [P, T2], U8) for b in range(2)]
+        def scatter(s):
+            window = pages[s % 2][:].indirect(idx2[:])
+            if s in (0, LAST):
+                nc.vector.tensor_tensor(window, source[s], wgs_sb[:], MULT)
+            else:
+                nc.vector.tensor_copy(window, source[s])
 
-        def z_stage(s, c0, c1):
+        z_rows = [sb("z_rows%d" % b, [P, PACK, T2], BF16) for b in range(PASSES)]
+        z_sc = [sb("z_sc%d" % b, [P, T2], U8) for b in range(PASSES)]
+
+        def z_on_vector(s, c0, c1):
             b, i = divmod(s, PACK)
             nc.vector.scalar_tensor_tensor(
-                z_rows[b][:, i, c0:c1], page_of(s)[:, c0:c1], 1.0, ld[s][:, c0:c1], ADD, MULT
+                z_rows[b][:, i, c0:c1], pages[s % 2][:, c0:c1], 1.0, load_sb[s][:, c0:c1], ADD, MULT
             )
 
-        def z_stage_pool(s):
+        def z_on_gpsimd(s):
             b, i = divmod(s, PACK)
-            factor = sb("factor%d" % s, [P, T2], F32, tag="wa_g112")
-            nc.gpsimd.tensor_scalar(factor[:], page_of(s)[:], 1.0, 1.0, MULT, ADD)
-            nc.gpsimd.tensor_tensor(z_rows[b][:, i, :], factor[:], ld[s][:], MULT)
+            factor = shared_factor if s else sb("first_factor", [P, T2], F32, tag="wa_raw00")[:]
+            nc.gpsimd.tensor_scalar(factor, pages[s % 2][:], 1.0, 1.0, MULT, ADD)
+            nc.gpsimd.tensor_tensor(z_rows[b][:, i, :], factor, load_sb[s][:], MULT)
 
-        def weave_z(copy, b, woven, c0, i0, i1):
+        def weave(copy, b, woven, q, rows):
             copy(
-                out=woven.rearrange("p (c n) i -> p c i n", n=4)[:, :, i0:i1, :],
-                in_=z_rows[b][:, i0:i1, c0 : c0 + QUART].rearrange("p i (c n) -> p c i n", n=4),
+                out=woven.rearrange("p (c n) i -> p c i n", n=NEIGHBOURS)[:, :, 0:rows, :],
+                in_=z_rows[b][:, 0:rows, q * QUART : (q + 1) * QUART].rearrange("p i (c n) -> p c i n", n=NEIGHBOURS),
             )
 
-        def quantize_z(woven, b, c0, c1):
-            if b == 0:
-                z_w[b, c0] = sb("z_w%d_%d" % (b, c0), [P, c1 - c0], U32, tag="ld3")
-            else:
-                z_w[b, c0] = sb("z_w%d_%d" % (b, c0), [P, c1 - c0], U32)
-            nc.vector.quantize_mx(
-                out=z_w[b, c0][:].bitcast(FP8X4),
-                scales=z_sc[b][:, c0:c1],
-                in_=woven[:].rearrange("p c i -> p (c i)"),
-            )
+        def quantize_z(words, scales, woven):
+            nc.vector.quantize_mx(out=words.bitcast(FP8X4), scales=scales, in_=woven.rearrange("p c i -> p (c i)"))
 
         acc = {}
 
-        def out_passes(b, q):
-            c0 = q * QUART
-            if b == 0:
-                words = z_w[0, 0][:, c0 : c0 + QUART]
-            else:
-                words = z_w[1, c0][:]
-            for n in range(3):
+        def out_passes(b, q, words):
+            for n in range(N_TILES):
                 nc.tensor.matmul_mx(
                     out=acc[q, n // 2][:, n % 2, :],
                     lhsT=wo_w[:, b, n * P : (n + 1) * P].bitcast(FP8X4),
                     lhsT_scale=wo_sc[:, b, n * P : (n + 1) * P],
                     rhs=words.bitcast(FP8X4),
-                    rhs_scale=z_sc[b][:, c0 : c0 + QUART],
-                    start=(b == 0 and n != 1),
-                    stop=(b == 1 and n != 0),
+                    rhs_scale=z_sc[b][:, q * QUART : (q + 1) * QUART],
+                    start=(b == 0 and n % 2 == 0),
+                    stop=(b == PASSES - 1 and n > 0),
                 )
 
-        for s in range(DIRECT):
-            direct_gate_stage(s)
-        gate_stage(0, DIRECT, [("gap", 2), ("gap", 2), ("total", 2), ("total", 2)])
-        g = round_wa(nc.vector.tensor_copy, 0, 0, 0, 4, "wa_g000")
-        quantize_wa(g, 0, 0, 0, 0, 4)
-        g = round_wa(nc.vector.tensor_copy, 1, 0, 0, 1, "wa_g100")
-        quantize_wa(g, 1, 0, 0, 0, 1)
-        direct_blend(0)
-        for a, i0, i1 in ((1, 1, 2), (1, 2, 4)):
-            g = round_wa(nc.scalar.copy, a, 0, i0, i1, "wa_g%d0%d" % (a, i0))
-            quantize_wa(g, a, 0, i0, i0, i1)
-        front_stage(1)
-        front_stage(2)
-        acc_tags = [("fit", 1), ("score", 2), ("score", 2), ("base_bank", 1), ("gap", 2), ("gap", 2), ("total", 2), ("total", 2)]
-        for s in range(SLICES):
-            scatter_stage(s)
-            if s == 0:
-                for i0 in (0, 2):
-                    for a in range(2):
-                        g = round_wa(nc.scalar.copy, a, 1, i0, i0 + 2, "wa_g%d1%d" % (a, i0))
-                        quantize_wa(g, a, 1, i0, i0, i0 + 2)
-                back_stage(1)
-                back_stage(2)
-                weigh_stage(1)
-                gate_stage(1, 0, [("score", 2)] * PACK)
-                front_stage(3)
-            if s < SLICES - 2:
-                z_stage_pool(s)
-            if s + 2 < SLICES:
-                weigh_stage(s + 2)
-            if s + 3 < SLICES:
-                back_stage(s + 3)
-            if s + 4 < SLICES:
-                front_stage(s + 4)
-            if s == PACK - 1:
-                first_woven = sb("first_woven", [P, T2, PACK], BF16)
-                for q in range(4):
-                    weave_z(nc.scalar.copy, 0, first_woven[:, q * QUART : (q + 1) * QUART, :], q * QUART, 0, PACK)
-            if s == SLICES - 2:
-                z_stage(s, 0, T2)
-                quantize_z(first_woven, 0, 0, T2)
-                for q in range(4):
-                    for u in range(2):
-                        tag, bufs = acc_tags[2 * q + u]
-                        acc[q, u] = psum.tile([P, 2 - u, QUART], F32, name="acc%d%d" % (q, u), tag=tag, bufs=bufs)
-                    out_passes(0, q)
-                woven = [sb("woven%d" % q, [P, QUART, PACK], BF16) for q in range(4)]
-                for q in PREFILLED:
-                    weave_z(nc.scalar.copy, 1, woven[q][:], q * QUART, 0, PACK - 1)
+        gate = first_gate()
+        turned_gates(0, 1, ["gap", "gap", "total", "total"])
+        first_half_of_wa(nc.vector.tensor_copy, 0, 0, PACK)
+        first_half_of_wa(nc.vector.tensor_copy, 1, 0, 1)
+        first_h(gate)
+        first_half_of_wa(nc.scalar.copy, 1, 1, 2)
+        first_half_of_wa(nc.scalar.copy, 1, 2, PACK)
+        make_gap(1)
+        make_gap(2)
 
-        last = SLICES - 1
-        out_view = out.rearrange("(n p) t -> p n t", p=P)
-        for q in range(4):
-            z_stage(last, q * QUART, (q + 1) * QUART)
-            if q in PREFILLED:
+        scatter(0)
+        make_total(1)
+        make_total(2)
+        make_source(1)
+        z_on_gpsimd(0)
+        make_gap(3)
+
+        scatter(1)
+        for a in range(PASSES):
+            rounded = shared_wa if a else sb("wa_rounded01", [P, PACK, P, PACK], BF16)[:]
+            for i0 in range(0, PACK, 2):
+                round_wa(nc.scalar.copy, rounded[:, i0 : i0 + 2, :, :], a, 1, i0, i0 + 2)
+            quantize_wa(rounded, a, 1, 0, PACK)
+        turned_gates(1, 0, ["score"] * PACK)
+        make_total(3)
+        make_source(2)
+        make_gap(4)
+        z_on_gpsimd(1)
+        make_gap(5)
+
+        first_woven = sb("first_woven", [P, T2, PACK], BF16)
+        for s in range(2, LAST):
+            scatter(s)
+            if s < POOL_SLICES:
+                z_on_gpsimd(s)
+            make_source(s + 1)
+            if s + 2 < SLICES:
+                make_total(s + 2)
+            if s + 4 < SLICES:
+                make_gap(s + 4)
+            if s == PACK - 1:
+                for q in range(QUARTERS):
+                    weave(nc.scalar.copy, 0, first_woven[:, q * QUART : (q + 1) * QUART, :], q, PACK)
+
+        z_on_vector(LAST - 1, 0, T2)
+        first_words = sb("first_words", [P, T2], U32, tag="load%d" % (LAST - 1 - 3))
+        quantize_z(first_words[:], z_sc[0][:], first_woven[:])
+        roles = [role for role in bank_count for n in range(bank_count[role])]
+        for q in range(QUARTERS):
+            for u in range(2):
+                acc[q, u] = bank("acc%d%d" % (q, u), [P, 2 - u, QUART], roles[2 * q + u])
+            out_passes(0, q, first_words[:, q * QUART : (q + 1) * QUART])
+
+        woven = [sb("woven%d" % q, [P, QUART, PACK], BF16) for q in range(QUARTERS)]
+        for q in range(0, QUARTERS, 2):
+            weave(nc.scalar.copy, 1, woven[q][:], q, PACK - 1)
+
+        def finish(q):
+            words = sb("last_words%d" % q, [P, QUART], U32)
+            quantize_z(words[:], z_sc[1][:, q * QUART : (q + 1) * QUART], woven[q][:])
+            out_passes(1, q, words[:])
+
+        scatter(LAST)
+        for q in range(QUARTERS):
+            z_on_vector(LAST, q * QUART, (q + 1) * QUART)
+            if q % 2 == 0:
                 nc.scalar.copy(woven[q][:, :, PACK - 1], z_rows[1][:, PACK - 1, q * QUART : (q + 1) * QUART])
-            if q == 1:
-                weave_z(nc.vector.tensor_copy, 1, woven[0][:], 0, 0, PACK)
-            if q == 2:
-                quantize_z(woven[0], 1, 0, QUART)
-                out_passes(1, 0)
-        for q in range(1, 4):
-            quantize_z(woven[q], 1, q * QUART, (q + 1) * QUART)
-            out_passes(1, q)
-            if q == 1:
-                weave_z(nc.vector.tensor_copy, 1, woven[3][:], 3 * QUART, 0, PACK)
-        for q in range(4):
+            else:
+                weave(nc.vector.tensor_copy, 1, woven[q][:], q, PACK)
+            if q > 0:
+                finish(q - 1)
+        finish(QUARTERS - 1)
+
+        out_view = out.rearrange("(n p) t -> p n t", p=P)
+        for q in range(QUARTERS):
+            half, w0 = divmod(q * QUART, S)
+            staged = prior_sb[half][:, 0:N_TILES, w0 : w0 + QUART]
+            copy_wide = nc.scalar.copy if q < QUARTERS // 2 else nc.vector.tensor_copy
+            copy_wide(staged[:, 0:2, :], acc[q, 0][:])
+            nc.scalar.copy(staged[:, 2:N_TILES, :], acc[q, 1][:])
             cols = slice(q * QUART, (q + 1) * QUART)
-            pair = sb("pair%d" % q, [P, 2, QUART], F32, tag="minus_fit" if q % 2 else "base_t", bufs=2)
-            single = sb("single%d" % q, [P, QUART], F32)
-            copy_pair = nc.vector.tensor_copy if q == 3 else nc.scalar.copy
-            copy_single = nc.vector.tensor_copy if q == 2 else nc.scalar.copy
-            copy_pair(pair[:], acc[q, 0][:])
-            copy_single(single[:], acc[q, 1][:, 0, :])
-            nc.sync.dma_start(out=out_view[:, 0:2, cols], in_=pair[:])
-            nc.sync.dma_start(out=out_view[:, 2, cols], in_=single[:])
+            nc.sync.dma_start(out=out_view[:, 0:2, cols], in_=staged[:, 0:2, :])
+            nc.sync.dma_start(out=out_view[:, 2, cols], in_=staged[:, 2, :])

@@ -71,10 +71,6 @@ def tile_list_demand_response_baseline_kernel(
         nc.vector.memset(tab_sc[:].rearrange("p a c -> p (a c)").bitcast(I32), 0)
         nc.vector.memset(wg_sc[:].rearrange("p a c -> p (a c)").bitcast(I32), 0)
 
-        warm = keep.tile([P, 2], F32, name="warm")
-        nc.gpsimd.memset(warm[:, 0:1], 0.0)
-        nc.scalar.activation(warm[:, 1:2], warm[:, 0:1], SIGMOID)
-
         tab_w.append(sb("tab_w1", [P, T], I32))
         wg_w.append(sb("wg_w1", [P, PASSES, 2 * PASS], U8))
         wa_raw = {}
@@ -156,7 +152,8 @@ def tile_list_demand_response_baseline_kernel(
         wa_sc = {}
         for a in range(PASSES):
             for b in range(PASSES):
-                wa_w[a, b] = sb("wa_w%d%d" % (a, b), [P, PASS], U32)
+                if (a, b) != (0, 1):
+                    wa_w[a, b] = sb("wa_w%d%d" % (a, b), [P, PASS], U32)
                 wa_sc[a, b] = sb("wa_sc%d%d" % (a, b), [P, PASS], U8)
 
         def round_wa(copy, rounded, a, b, i0, i1):
@@ -238,17 +235,15 @@ def tile_list_demand_response_baseline_kernel(
         def source_room(s):
             if s < 2:
                 return sb("source%d" % s, [P, S], F32)[:]
-            if s == 2:
-                return gate_t[0][:, 3, :]
+            if s < PACK:
+                return gate_t[(s + 1) // PACK][:, (s + 1) % PACK, :]
             if s == LAST:
                 return load_sb[POOL_SLICES - 1][:, 0:S]
             return load_sb[s - 3][:, 0:S]
 
         def step_room(s):
-            if s == 1:
-                return sb("step1", [P, S], F32, tag="minus_fit_of_2")[:]
-            if s == 2:
-                return sb("step2", [P, S], F32)[:]
+            if s < 3:
+                return sb("step%d" % s, [P, S], F32)[:]
             if s == 3:
                 return shared_step
             return load_sb[s - 4][:, S : 2 * S]
@@ -289,10 +284,7 @@ def tile_list_demand_response_baseline_kernel(
 
         def make_gap(s):
             fit = make_fit(s, "fit")
-            if s == 2:
-                minus_fit = sb("minus_fit2", [P, S], F32, tag="minus_fit_of_2")
-            else:
-                minus_fit = sb("minus_fit%d" % s, [P, S], F32, tag="minus_fit", bufs=2)
+            minus_fit = sb("minus_fit%d" % s, [P, S], F32, tag="minus_fit", bufs=2)
             nc.scalar.activation(minus_fit[:], fit[:], COPY, scale=-1.0)
             gap[s] = bank("gap%d" % s, [P, S], "gap")
             turn_into(gap[s], prior_of(s), True, False)
@@ -379,6 +371,7 @@ def tile_list_demand_response_baseline_kernel(
         make_gap(3)
 
         scatter(1)
+        wa_w[0, 1] = sb("wa_w01", [P, PASS], U32, tag="source1")
         for a in range(PASSES):
             rounded = shared_wa if a else sb("wa_rounded01", [P, PACK, P, PACK], BF16)[:]
             for i0 in range(0, PACK, 2):
@@ -396,8 +389,10 @@ def tile_list_demand_response_baseline_kernel(
             scatter(s)
             if s < POOL_SLICES:
                 z_on_gpsimd(s)
+            if s + 1 < PACK:
+                make_total(s + 2)
             make_source(s + 1)
-            if s + 2 < SLICES:
+            if PACK < s + 2 < SLICES:
                 make_total(s + 2)
             if s + 4 < SLICES:
                 make_gap(s + 4)
@@ -438,7 +433,7 @@ def tile_list_demand_response_baseline_kernel(
         for q in range(QUARTERS):
             half, w0 = divmod(q * QUART, S)
             staged = prior_sb[half][:, 0:N_TILES, w0 : w0 + QUART]
-            copy_wide = nc.scalar.copy if q < QUARTERS // 2 else nc.vector.tensor_copy
+            copy_wide = nc.scalar.copy if q < QUARTERS - 1 else nc.vector.tensor_copy
             copy_wide(staged[:, 0:2, :], acc[q, 0][:])
             nc.scalar.copy(staged[:, 2:N_TILES, :], acc[q, 1][:])
             cols = slice(q * QUART, (q + 1) * QUART)

@@ -27,19 +27,19 @@ PASSES = 2
 SLICES = H // P
 LAST = SLICES - 1
 POOL_SLICES = SLICES - 2
-QUARTERS = 4
-QUART = T2 // QUARTERS
+RING = 2
+CUTS = [0, 256, 512, 768, 1024]
+WEAVE = 256
+SCALAR_FILLS = ()
+VECTOR_LEAVES = ((3, 0),)
 N_TILES = N // P
 NEIGHBOURS = 4
 
 
-def load_scale_rows(nc, plane, scales):
-    rows = scales.bitcast(I32)
-    for q in range(4):
-        nc.sync.dma_start(
-            out=plane[32 * q : 32 * q + 4, :, :].bitcast(I32),
-            in_=rows[:, 4 * q : 4 * q + 4, :].rearrange("a r c -> r a c"),
-        )
+def load_scale_rows(nc, plane, scales, c0, c1):
+    rows = scales.bitcast(I32).rearrange("a (q r) c -> r q a c", r=4)
+    for r in range(4):
+        nc.sync.dma_start(out=plane[r:P:32, :, :].bitcast(I32), in_=rows[r, :, :, c0 // 4 : c1 // 4])
 
 
 def tile_list_demand_response_baseline_kernel(
@@ -50,42 +50,47 @@ def tile_list_demand_response_baseline_kernel(
         keep = ctx.enter_context(tc.tile_pool(name="keep", bufs=1))
         psum = ctx.enter_context(tc.psum_pool(name="psum", bufs=1))
 
-        def sb(name, shape, dtype, tag=None, bufs=1):
-            return keep.tile(shape, dtype, name=name, tag=tag or name, bufs=bufs, align_bytes=64)
+        def sb(name, shape, dtype, tag=None):
+            return keep.tile(shape, dtype, name=name, tag=tag or name, align_bytes=64)
 
-        bank_count = {"fit": 1, "score": 2, "prior_t": 1, "gap": 2, "total": 2}
-
-        def bank(name, shape, role):
-            return psum.tile(shape, F32, name=name, tag=role, bufs=bank_count[role])
+        banks = [psum.tile([P, S], F32, name="bank%d" % n) for n in range(8)]
+        fit_banks, total_banks, side_banks = banks[0:4], banks[4:6], banks[6:8]
 
         idx = keep.tile([P, S // 16], U16, name="idx")
         idx2 = keep.tile([P, S // 16], U16, name="idx2")
         tab_sc = sb("tab_sc", [P, PASSES, T], U8)
-        wg_sc = sb("wg_sc", [P, PASSES, H], U8)
+        wg_sc = [sb("wg_sc%d" % b, [P, PASSES, PASS], U8) for b in range(PASSES)]
         wo_sc = sb("wo_sc", [P, PASSES, N], U8)
-        wg_w = [sb("wg_w0", [P, PASSES, 2 * PASS], U8)]
-        tab_w = [sb("tab_w0", [P, T], I32)]
+        wg_w = [sb("wg_w%d" % b, [P, PASSES, 2 * PASS], U8) for b in range(PASSES)]
+        tab_w = [sb("tab_w%d" % a, [P, T], I32) for a in range(PASSES)]
         pages = [sb("page%d" % n, [P, T2], F32) for n in range(2)]
+        one_page = sb("one_page", [P, T2], F32)
         ident = sb("ident", [P, P], F32)
-
-        nc.vector.memset(tab_sc[:].rearrange("p a c -> p (a c)").bitcast(I32), 0)
-        nc.vector.memset(wg_sc[:].rearrange("p a c -> p (a c)").bitcast(I32), 0)
-
-        tab_w.append(sb("tab_w1", [P, T], I32))
-        wg_w.append(sb("wg_w1", [P, PASSES, 2 * PASS], U8))
         wa_raw = {}
         for a in range(PASSES):
             for b in range(PASSES):
                 wa_raw[a, b] = sb("wa_raw%d%d" % (a, b), [P, PACK, PASS], F32)
         prior_sb = [sb("prior%d" % b, [P, PACK, S], F32) for b in range(PASSES)]
         wgs_sb = sb("wgs_sb", [P, S], F32)
-        load_sb = [sb("load%d" % s, [P, T2], F32) for s in range(SLICES)]
+        late_loads = sb("late_loads", [P, PACK, T2], F32)
+        late_rows = late_loads[:].bitcast(BF16)[:, :, 0:T2]
+        load_sb = [
+            late_loads[:, s - PACK + 1, :] if PACK - 1 <= s < LAST else sb("load%d" % s, [P, T2], F32)[:]
+            for s in range(SLICES)
+        ]
         wo_w = sb("wo_w", [P, PASSES, N], I32)
-        make_identity(nc, ident[:])
 
+        def clear(engine, plane):
+            engine.memset(plane[:].rearrange("p a c -> p (a c)").bitcast(I32), 0)
+
+        clear(nc.vector, tab_sc)
+        clear(nc.vector, wg_sc[0])
+        make_identity(nc, ident[:])
         for page in pages:
             nc.gpsimd.memset(page[:], 0.0)
-        nc.gpsimd.memset(wo_sc[:].rearrange("p a c -> p (a c)").bitcast(I32), 0)
+        nc.gpsimd.memset(one_page[:], 1.0)
+        clear(nc.gpsimd, wg_sc[1])
+        clear(nc.gpsimd, wo_sc)
 
         wa_view = wa.rearrange("(a p j) (b c) -> a b p j c", a=PASSES, j=PACK, b=PASSES)
         prior_view = prior.rearrange("(b p i) j -> b p i j", b=PASSES, i=PACK)
@@ -97,6 +102,7 @@ def tile_list_demand_response_baseline_kernel(
         def fetch_wg(b):
             words = wg_words.bitcast(I32).rearrange("a p (b c) -> b p a c", b=PASSES)
             nc.sync.dma_start(out=wg_w[b][:].bitcast(I32), in_=words[b])
+            load_scale_rows(nc, wg_sc[b], wg_scales, b * PASS, (b + 1) * PASS)
 
         def fetch_wa(b):
             for a in range(PASSES):
@@ -106,30 +112,27 @@ def tile_list_demand_response_baseline_kernel(
             nc.sync.dma_start(out=prior_sb[b][:, i0:i1, :], in_=prior_view[b, :, i0:i1, :])
 
         def fetch_load(s):
-            nc.sync.dma_start(out=load_sb[s][:], in_=load_view[s // PACK, s % PACK])
+            nc.sync.dma_start(out=load_sb[s], in_=load_view[s // PACK, s % PACK])
 
         nc.sync.dma_start(idx[:], offs)
-        nc.sync.dma_start(idx2[:], offs2)
         fetch_tab(0)
-        fetch_wg(0)
-        load_scale_rows(nc, tab_sc, tab_scales)
+        load_scale_rows(nc, tab_sc, tab_scales, 0, T)
         fetch_tab(1)
-        load_scale_rows(nc, wg_sc, wg_scales)
+        fetch_wg(0)
         fetch_wa(0)
-        nc.sync.dma_start(out=prior_sb[0][:, 0, :], in_=prior_view[0, :, 0, :])
+        fetch_prior(0, 0, 1)
         nc.sync.dma_start(out=wgs_sb[:], in_=wgs)
-        fetch_prior(0, 1, 3)
-        fetch_load(0)
-        fetch_wa(1)
-        fetch_prior(0, 3, PACK)
+        nc.sync.dma_start(idx2[:], offs2)
+        fetch_prior(0, 1, PACK)
         fetch_wg(1)
-        nc.sync.dma_start(out=prior_sb[1][:], in_=prior_view[1])
+        fetch_wa(1)
+        fetch_prior(1, 0, PACK)
+        for s in range(SLICES):
+            fetch_load(s)
         nc.sync.dma_start(
             out=wo_w[:], in_=wo_words.rearrange("a p c i -> a p (c i)").bitcast(I32).rearrange("a p c -> p a c")
         )
-        load_scale_rows(nc, wo_sc, wo_scales)
-        for s in range(1, SLICES):
-            fetch_load(s)
+        load_scale_rows(nc, wo_sc, wo_scales, 0, N)
 
         v_w = [sb("v_w%d" % a, [P, S], U32) for a in range(PASSES)]
         v_sc = [sb("v_sc%d" % a, [P, S], U8) for a in range(PASSES)]
@@ -145,16 +148,10 @@ def tile_list_demand_response_baseline_kernel(
             in_=wg_w[0][:].bitcast(U16).rearrange("p a (m i) -> p a i m", i=PACK)[:, :, 0:1, :],
         )
         nc.vector.tensor_copy(
-            out=first_wg_sc[:], in_=wg_sc[:, :, 0:PASS].rearrange("p a (m i) -> p a i m", i=PACK)[:, :, 0:1, :]
+            out=first_wg_sc[:], in_=wg_sc[0][:].rearrange("p a (m i) -> p a i m", i=PACK)[:, :, 0:1, :]
         )
 
-        wa_w = {}
-        wa_sc = {}
-        for a in range(PASSES):
-            for b in range(PASSES):
-                if (a, b) != (0, 1):
-                    wa_w[a, b] = sb("wa_w%d%d" % (a, b), [P, PASS], U32)
-                wa_sc[a, b] = sb("wa_sc%d%d" % (a, b), [P, PASS], U8)
+        pieces = [[], []]
 
         def round_wa(copy, rounded, a, b, i0, i1):
             copy(
@@ -162,24 +159,23 @@ def tile_list_demand_response_baseline_kernel(
                 in_=wa_raw[a, b][:].rearrange("p j (m i) -> p m j i", i=PACK)[:, :, :, i0:i1],
             )
 
-        def quantize_wa(rounded, a, b, i0, i1):
-            nc.vector.quantize_mx(
-                out=wa_w[a, b][:, i0 * P : i1 * P].bitcast(FP8X4),
-                scales=wa_sc[a, b][:, i0 * P : i1 * P],
-                in_=rounded.rearrange("p i m j -> p (i m j)"),
-            )
+        def quantize(words, scales, values):
+            nc.vector.quantize_mx(out=words.bitcast(FP8X4), scales=scales, in_=values)
 
-        def first_half_of_wa(copy, a, i0, i1):
+        def first_half_of_wa(copy, a, i0, i1, tag=None):
             rounded = sb("wa_rounded%d0%d" % (a, i0), [P, i1 - i0, P, PACK], BF16)[:]
             round_wa(copy, rounded, a, 0, i0, i1)
-            quantize_wa(rounded, a, 0, i0, i1)
+            codes = sb("wa_w%d0%d" % (a, i0), [P, (i1 - i0) * P], U32, tag=tag)[:]
+            scales = sb("wa_sc%d0%d" % (a, i0), [P, (i1 - i0) * P], U8)[:]
+            quantize(codes, scales, rounded.rearrange("p i m j -> p (i m j)"))
+            pieces[0].append((a, slice(i0 * P, i1 * P), codes, scales))
 
         gate_t = {}
 
-        def turned_gates(b, first, roles):
-            gate_t[b] = sb("gate_t%d" % b, [P, PACK, S], F32, tag="wa_raw11" if b else None)
+        def turned_gates(b, first, scores):
+            gate_t[b] = wa_raw[1, 1] if b else sb("gate_t0", [P, PACK, S], F32)
             for c in range(S // P):
-                score = bank("score%d%d" % (b, c), [P, PASS], roles[c])
+                score = scores[c]
                 cols = slice(c * P, (c + 1) * P)
                 for a in range(PASSES):
                     nc.tensor.matmul_mx(
@@ -187,7 +183,7 @@ def tile_list_demand_response_baseline_kernel(
                         lhsT=v_w[a][:, cols].bitcast(FP8X4),
                         lhsT_scale=v_sc[a][:, cols],
                         rhs=wg_w[b][:, a, :].bitcast(FP4X4),
-                        rhs_scale=wg_sc[:, a, b * PASS : (b + 1) * PASS],
+                        rhs_scale=wg_sc[b][:, a, :],
                         start=(a == 0),
                         stop=(a == PASSES - 1),
                     )
@@ -195,22 +191,8 @@ def tile_list_demand_response_baseline_kernel(
                     gate_t[b][:, first:PACK, cols],
                     score[:].rearrange("e (m i) -> e i m", i=PACK)[:, first:PACK, :],
                     SIGMOID,
+                    scale=-1.0,
                 )
-
-        def make_fit(s, role):
-            b, i = divmod(s, PACK)
-            fit = bank("fit%d" % s, [P, S], role)
-            for a in range(PASSES):
-                nc.tensor.matmul_mx(
-                    out=fit[:],
-                    lhsT=wa_w[a, b][:, i * P : (i + 1) * P].bitcast(FP8X4),
-                    lhsT_scale=wa_sc[a, b][:, i * P : (i + 1) * P],
-                    rhs=v_w[a][:].bitcast(FP8X4),
-                    rhs_scale=v_sc[a][:],
-                    start=(a == 0),
-                    stop=(a == PASSES - 1),
-                )
-            return fit
 
         def prior_of(s):
             return prior_sb[s // PACK][:, s % PACK, :]
@@ -227,31 +209,8 @@ def tile_list_demand_response_baseline_kernel(
                     stop=(stop and c == S // P - 1),
                 )
 
-        shared = sb("shared", [P, S + T2], F32)
-        shared_wa = shared[:, S // 2 : S // 2 + T2].bitcast(BF16).rearrange("p (i m j) -> p i m j", i=PACK, j=PACK)
-        shared_step = shared[:, 0:S]
-        shared_factor = shared[:, S : S + T2]
-
-        def source_room(s):
-            if s < 2:
-                return sb("source%d" % s, [P, S], F32)[:]
-            if s < PACK:
-                return gate_t[(s + 1) // PACK][:, (s + 1) % PACK, :]
-            if s == LAST:
-                return load_sb[POOL_SLICES - 1][:, 0:S]
-            return load_sb[s - 3][:, 0:S]
-
-        def step_room(s):
-            if s < 3:
-                return sb("step%d" % s, [P, S], F32)[:]
-            if s == 3:
-                return shared_step
-            return load_sb[s - 4][:, S : 2 * S]
-
-        source = {}
-
         def first_gate():
-            score = bank("first_score", [P, S], "score")
+            score = banks[0]
             for a in range(PASSES):
                 nc.tensor.matmul_mx(
                     out=score[:],
@@ -266,176 +225,258 @@ def tile_list_demand_response_baseline_kernel(
             nc.scalar.activation(gate[:], score[:], SIGMOID)
             return gate
 
+        late_room = sb("late_room", [P, 2 * PACK - 1, S], F32)
+        late_values = late_room[:, PACK - 1 :, :].rearrange("p r j -> p (r j)").bitcast(BF16)
+        late_rounded = late_values.rearrange("p (a i m j) -> p a i m j", a=PASSES, i=PACK, j=PACK)
+        taken_t = [sb("taken_t0", [P, PACK, S], F32, tag="tab_w1"), late_room[:, 0:PACK, :]]
+        late_prior_t = sb("late_prior_t", [P, PACK, S], F32, tag="tab_w0")
+        prior_t = [(late_prior_t if s // PACK else wa_raw[0, 0])[:, s % PACK, :] for s in range(SLICES)]
+        kept_t = [wa_raw[1 - s // PACK, s // PACK][:, s % PACK, :] for s in range(SLICES)]
+        source = [sb("source%d" % s, [P, S], F32)[:] if s in (0, 1, 5, 6, 7) else None for s in range(SLICES)]
+        source[2] = late_room[:, PACK - 1, :]
+        source[3] = late_room[:, PACK, :]
+        source[4] = kept_t[6]
+        total = [total_banks[s % 2] for s in range(SLICES)]
+        total[6] = side_banks[0]
+        total[7] = total_banks[0]
+
         def first_h(gate):
-            fit = make_fit(0, "total")
+            fit = total_banks[1]
+            for a, unused, codes, scales in pieces[0]:
+                nc.tensor.matmul_mx(
+                    out=fit[:],
+                    lhsT=codes[:, 0:P].bitcast(FP8X4),
+                    lhsT_scale=scales[:, 0:P],
+                    rhs=v_w[a][:].bitcast(FP8X4),
+                    rhs_scale=v_sc[a][:],
+                    start=(a == 0),
+                    stop=(a == PASSES - 1),
+                )
             kept = sb("kept", [P, S], F32)
             taken = sb("taken", [P, S], F32)
-            source[0] = source_room(0)
             nc.vector.scalar_tensor_tensor(kept[:], gate[:], 1.0, prior_of(0), SUB, MULT)
             halves = [slice(0, S // 2), slice(S // 2, S)]
             for cols in halves:
                 nc.vector.tensor_tensor(taken[:, cols], fit[:, cols], gate[:, cols], MULT)
             for cols in halves:
-                nc.vector.tensor_tensor(source[0][:, cols], taken[:, cols], kept[:, cols], SUB)
+                nc.vector.tensor_tensor(taken[:, cols], kept[:, cols], taken[:, cols], SUB)
+            return taken[:]
 
-        gap = {}
-        prior_t = {}
-        total = {}
-
-        def make_gap(s):
-            fit = make_fit(s, "fit")
-            minus_fit = sb("minus_fit%d" % s, [P, S], F32, tag="minus_fit", bufs=2)
-            nc.scalar.activation(minus_fit[:], fit[:], COPY, scale=-1.0)
-            gap[s] = bank("gap%d" % s, [P, S], "gap")
-            turn_into(gap[s], prior_of(s), True, False)
-            turn_into(gap[s], minus_fit, False, True)
-            turned = bank("turned_prior%d" % s, [P, S], "prior_t")
-            turn_into(turned, prior_of(s), True, True)
-            prior_t[s] = sb("prior_t%d" % s, [P, S], F32, tag="prior_t", bufs=2)
-            nc.scalar.copy(prior_t[s][:], turned[:])
-
-        def make_total(s):
-            step = step_room(s)
-            nc.vector.scalar_tensor_tensor(step, gap[s][:], -1.0, gate_t[s // PACK][:, s % PACK, :], MULT, MULT)
-            total[s] = bank("total%d" % s, [P, S], "total")
-            turn_into(total[s], prior_t[s], True, False)
-            turn_into(total[s], step, False, True)
-
-        def make_source(s):
-            source[s] = source_room(s)
-            if s == LAST:
-                nc.scalar.copy(source[s], total[s][:])
-            else:
-                nc.vector.tensor_tensor(source[s], total[s][:], wgs_sb[:], MULT)
-
-        def scatter(s):
-            window = pages[s % 2][:].indirect(idx2[:])
-            if s in (0, LAST):
-                nc.vector.tensor_tensor(window, source[s], wgs_sb[:], MULT)
-            else:
-                nc.vector.tensor_copy(window, source[s])
-
-        z_rows = [sb("z_rows%d" % b, [P, PACK, T2], BF16) for b in range(PASSES)]
-        z_sc = [sb("z_sc%d" % b, [P, T2], U8) for b in range(PASSES)]
-
-        def z_on_vector(s, c0, c1):
-            b, i = divmod(s, PACK)
-            nc.vector.scalar_tensor_tensor(
-                z_rows[b][:, i, c0:c1], pages[s % 2][:, c0:c1], 1.0, load_sb[s][:, c0:c1], ADD, MULT
-            )
-
-        def z_on_gpsimd(s):
-            b, i = divmod(s, PACK)
-            factor = shared_factor if s else sb("first_factor", [P, T2], F32, tag="wa_raw00")[:]
-            nc.gpsimd.tensor_scalar(factor, pages[s % 2][:], 1.0, 1.0, MULT, ADD)
-            nc.gpsimd.tensor_tensor(z_rows[b][:, i, :], factor, load_sb[s][:], MULT)
-
-        def weave(copy, b, woven, q, rows):
-            copy(
-                out=woven.rearrange("p (c n) i -> p c i n", n=NEIGHBOURS)[:, :, 0:rows, :],
-                in_=z_rows[b][:, 0:rows, q * QUART : (q + 1) * QUART].rearrange("p i (c n) -> p c i n", n=NEIGHBOURS),
-            )
-
-        def quantize_z(words, scales, woven):
-            nc.vector.quantize_mx(out=words.bitcast(FP8X4), scales=scales, in_=woven.rearrange("p c i -> p (c i)"))
-
-        acc = {}
-
-        def out_passes(b, q, words):
-            for n in range(N_TILES):
+        def turned_fit(b, c):
+            cols = slice(c * P, (c + 1) * P)
+            for n, (a, rows, codes, scales) in enumerate(pieces[b]):
                 nc.tensor.matmul_mx(
-                    out=acc[q, n // 2][:, n % 2, :],
-                    lhsT=wo_w[:, b, n * P : (n + 1) * P].bitcast(FP8X4),
-                    lhsT_scale=wo_sc[:, b, n * P : (n + 1) * P],
-                    rhs=words.bitcast(FP8X4),
-                    rhs_scale=z_sc[b][:, q * QUART : (q + 1) * QUART],
-                    start=(b == 0 and n % 2 == 0),
-                    stop=(b == PASSES - 1 and n > 0),
+                    out=fit_banks[c][:, rows],
+                    lhsT=v_w[a][:, cols].bitcast(FP8X4),
+                    lhsT_scale=v_sc[a][:, cols],
+                    rhs=codes.bitcast(FP8X4),
+                    rhs_scale=scales,
+                    start=(n == 0),
+                    stop=(n == len(pieces[b]) - 1),
                 )
 
+        def make_taken(b, c, first):
+            cols = slice(c * P, (c + 1) * P)
+            nc.vector.scalar_tensor_tensor(
+                taken_t[b][:, first:PACK, cols],
+                gate_t[b][:, first:PACK, cols],
+                1.0,
+                fit_banks[c][:].rearrange("e (i m) -> e i m", i=PACK)[:, first:PACK, :],
+                SUB,
+                MULT,
+            )
+
+        def make_kept(s):
+            b, i = divmod(s, PACK)
+            turned = side_banks[s % 2]
+            turn_into(turned, prior_of(s), True, True)
+            nc.scalar.activation(prior_t[s], turned[:], COPY, scale=-1.0)
+            nc.gpsimd.tensor_tensor(kept_t[s], gate_t[b][:, i, :], prior_t[s], MULT)
+
+        def make_total(s):
+            b, i = divmod(s, PACK)
+            parts = [kept_t[s], taken_t[b][:, i, :]]
+            if s == 6:
+                parts = parts[::-1]
+            turn_into(total[s], parts[0], True, False)
+            turn_into(total[s], parts[1], False, True)
+
+        def make_source(s, h):
+            if s == LAST - 1:
+                product = kept_t[4]
+                nc.vector.scalar_tensor_tensor(product, h, -1.0, wgs_sb[:], MULT, MULT)
+                nc.gpsimd.tensor_scalar(source[s], product, 1.0, 1.0, MULT, ADD)
+            else:
+                nc.vector.scalar_tensor_tensor(source[s], h, -1.0, wgs_sb[:], MULT, MULT)
+
+        page_of = [one_page if s == LAST - 1 else pages[s % 2] for s in range(SLICES)]
+
+        def scatter(s):
+            nc.vector.tensor_copy(page_of[s][:].indirect(idx2[:]), source[s])
+
+        early_rows = sb("early_rows", [P, T2 // WEAVE, PACK, WEAVE], BF16)
+        early_room = early_rows[:].rearrange("p q i t -> p (q i t)").bitcast(F32)
+
+        def z_on_vector(s, cols):
+            nc.vector.scalar_tensor_tensor(late_rows[:, s - PACK, cols], pages[s % 2][:, cols], 1.0, load_sb[s][:, cols], ADD, MULT)
+
+        factors = [wa_raw[0, 0][:, j : j + 2, :].rearrange("p j c -> p (j c)") for j in (2, 2, 0, 2, 0)]
+        factors += [early_room[:, 0:T2], one_page[:]]
+
+        def z_on_gpsimd(s):
+            if s < 2:
+                nc.gpsimd.tensor_scalar(factors[s], pages[s % 2][:], 1.0, 1.0, MULT, ADD)
+            elif s < LAST - 1:
+                nc.scalar.activation(factors[s], pages[s % 2][:], COPY, bias=1.0)
+            if s < PACK:
+                nc.gpsimd.tensor_tensor(
+                    early_rows[:, :, s, :],
+                    factors[s].rearrange("p (q t) -> p q t", t=WEAVE),
+                    load_sb[s].rearrange("p (q t) -> p q t", t=WEAVE),
+                    MULT,
+                )
+            else:
+                nc.gpsimd.tensor_tensor(late_rows[:, s - PACK, :], factors[s], load_sb[s], MULT)
+
+        chunks = [slice(c0, c1) for c0, c1 in zip(CUTS, CUTS[1:])]
+        woven = [sb("woven%d" % q, [P, PASSES, cols.stop - cols.start, PACK], BF16) for q, cols in enumerate(chunks)]
+
+        def weave(copy, q, b, rows, c0, c1, i0, i1):
+            copy(
+                out=woven[q][:, b, c0:c1, :].rearrange("p (c n) i -> p c i n", n=NEIGHBOURS)[:, :, i0:i1, :],
+                in_=rows[:, i0:i1, :].rearrange("p i (c n) -> p c i n", n=NEIGHBOURS),
+            )
+
+        def weave_early(piece):
+            for q, cols in enumerate(chunks):
+                c0, c1 = max(cols.start, piece * WEAVE), min(cols.stop, (piece + 1) * WEAVE)
+                if c0 < c1:
+                    rows = early_rows[:, piece, :, c0 - piece * WEAVE : c1 - piece * WEAVE]
+                    weave(nc.scalar.copy, q, 0, rows, c0 - cols.start, c1 - cols.start, 0, PACK)
+
+        def weave_late(copy, q, i0, i1):
+            weave(copy, q, 1, late_rows[:, 0:PACK, chunks[q]], 0, chunks[q].stop - chunks[q].start, i0, i1)
+
         gate = first_gate()
-        turned_gates(0, 1, ["gap", "gap", "total", "total"])
+        turned_gates(0, 1, [banks[1], banks[2], banks[3], banks[4]])
         first_half_of_wa(nc.vector.tensor_copy, 0, 0, PACK)
-        first_half_of_wa(nc.vector.tensor_copy, 1, 0, 1)
-        first_h(gate)
-        first_half_of_wa(nc.scalar.copy, 1, 1, 2)
-        first_half_of_wa(nc.scalar.copy, 1, 2, PACK)
-        make_gap(1)
-        make_gap(2)
+        first_half_of_wa(nc.vector.tensor_copy, 1, 0, 2)
+        first = first_h(gate)
+        first_half_of_wa(nc.scalar.copy, 1, 2, PACK, tag="kept")
+        make_source(0, first)
+        for c in range(PACK):
+            turned_fit(0, c)
+            make_taken(0, c, 1)
+        for s in range(1, PACK):
+            make_kept(s)
+
+        def blend(s):
+            make_total(s)
+            make_source(s, total[s][:])
 
         scatter(0)
-        make_total(1)
-        make_total(2)
-        make_source(1)
+        blend(1)
         z_on_gpsimd(0)
-        make_gap(3)
-
-        scatter(1)
-        wa_w[0, 1] = sb("wa_w01", [P, PASS], U32, tag="source1")
         for a in range(PASSES):
-            rounded = shared_wa if a else sb("wa_rounded01", [P, PACK, P, PACK], BF16)[:]
             for i0 in range(0, PACK, 2):
-                round_wa(nc.scalar.copy, rounded[:, i0 : i0 + 2, :, :], a, 1, i0, i0 + 2)
-            quantize_wa(rounded, a, 1, 0, PACK)
-        turned_gates(1, 0, ["score"] * PACK)
-        make_total(3)
-        make_source(2)
-        make_gap(4)
+                round_wa(nc.scalar.copy, late_rounded[:, a, i0 : i0 + 2, :, :], a, 1, i0, i0 + 2)
+
+        turned_gates(1, 0, fit_banks)
+        scatter(1)
+        late_words = sb("late_words", [P, PASSES, PASS], U32)
+        late_sc = sb("late_sc", [P, PASSES, PASS], U8)
+        quantize(late_words[:].rearrange("p a c -> p (a c)"), late_sc[:].rearrange("p a c -> p (a c)"), late_values)
+        pieces[1] = [(a, slice(0, PASS), late_words[:, a, :], late_sc[:, a, :]) for a in range(PASSES)]
+        blend(2)
+        blend(3)
         z_on_gpsimd(1)
-        make_gap(5)
+        for c in range(PACK):
+            turned_fit(1, c)
+        for s in range(PACK, SLICES):
+            make_kept(s)
 
-        first_woven = sb("first_woven", [P, T2, PACK], BF16)
-        for s in range(2, LAST):
-            scatter(s)
-            if s < POOL_SLICES:
-                z_on_gpsimd(s)
-            if s + 1 < PACK:
-                make_total(s + 2)
-            make_source(s + 1)
-            if PACK < s + 2 < SLICES:
-                make_total(s + 2)
-            if s + 4 < SLICES:
-                make_gap(s + 4)
-            if s == PACK - 1:
-                for q in range(QUARTERS):
-                    weave(nc.scalar.copy, 0, first_woven[:, q * QUART : (q + 1) * QUART, :], q, PACK)
+        scatter(2)
+        for c in range(PACK):
+            make_taken(1, c, 0)
+        z_on_gpsimd(2)
+        scatter(3)
+        for s in (4, 5, 6):
+            make_total(s)
+        for s in (4, 5, 6):
+            make_source(s, total[s][:])
+        z_on_gpsimd(3)
+        scatter(4)
+        blend(7)
+        z_on_gpsimd(4)
+        weave_early(0)
+        weave_early(1)
+        scatter(5)
+        z_on_gpsimd(5)
+        weave_early(2)
+        weave_early(3)
+        scatter(6)
+        z_on_gpsimd(6)
+        for q in range(len(chunks)):
+            weave_late(nc.scalar.copy, q, 0, 2)
 
-        z_on_vector(LAST - 1, 0, T2)
-        first_words = sb("first_words", [P, T2], U32, tag="load%d" % (LAST - 1 - 3))
-        quantize_z(first_words[:], z_sc[0][:], first_woven[:])
-        roles = [role for role in bank_count for n in range(bank_count[role])]
-        for q in range(QUARTERS):
-            for u in range(2):
-                acc[q, u] = bank("acc%d%d" % (q, u), [P, 2 - u, QUART], roles[2 * q + u])
-            out_passes(0, q, first_words[:, q * QUART : (q + 1) * QUART])
-
-        woven = [sb("woven%d" % q, [P, QUART, PACK], BF16) for q in range(QUARTERS)]
-        for q in range(0, QUARTERS, 2):
-            weave(nc.scalar.copy, 1, woven[q][:], q, PACK - 1)
-
-        def finish(q):
-            words = sb("last_words%d" % q, [P, QUART], U32)
-            quantize_z(words[:], z_sc[1][:, q * QUART : (q + 1) * QUART], woven[q][:])
-            out_passes(1, q, words[:])
-
-        scatter(LAST)
-        for q in range(QUARTERS):
-            z_on_vector(LAST, q * QUART, (q + 1) * QUART)
-            if q % 2 == 0:
-                nc.scalar.copy(woven[q][:, :, PACK - 1], z_rows[1][:, PACK - 1, q * QUART : (q + 1) * QUART])
-            else:
-                weave(nc.vector.tensor_copy, 1, woven[q][:], q, PACK)
-            if q > 0:
-                finish(q - 1)
-        finish(QUARTERS - 1)
+        free_banks = list(banks)
+        held = {}
+        for q, cols in enumerate(chunks):
+            width = cols.stop - cols.start
+            per_bank = min(N_TILES, S // width)
+            held[q] = []
+            for n0 in range(0, N_TILES, per_bank):
+                count = min(per_bank, N_TILES - n0)
+                tile = free_banks.pop(0)[:, 0 : count * width].rearrange("p (n t) -> p n t", n=count)
+                held[q].append((tile, n0, count))
 
         out_view = out.rearrange("(n p) t -> p n t", p=P)
-        for q in range(QUARTERS):
-            half, w0 = divmod(q * QUART, S)
-            staged = prior_sb[half][:, 0:N_TILES, w0 : w0 + QUART]
-            copy_wide = nc.scalar.copy if q < QUARTERS - 1 else nc.vector.tensor_copy
-            copy_wide(staged[:, 0:2, :], acc[q, 0][:])
-            nc.scalar.copy(staged[:, 2:N_TILES, :], acc[q, 1][:])
-            cols = slice(q * QUART, (q + 1) * QUART)
-            nc.sync.dma_start(out=out_view[:, 0:2, cols], in_=staged[:, 0:2, :])
-            nc.sync.dma_start(out=out_view[:, 2, cols], in_=staged[:, 2, :])
+        staged = [wa_raw[a, b][:].rearrange("p j c -> p (j c)") for a in range(PASSES) for b in range(PASSES)]
+        staged.append(prior_sb[0][:].rearrange("p i j -> p (i j)"))
+
+        def fill(q):
+            weave_late(nc.scalar.copy if q in SCALAR_FILLS else nc.vector.tensor_copy, q, 2, PACK)
+
+        def finish(q):
+            width = chunks[q].stop - chunks[q].start
+            words = sb("z_words%d" % q, [P, PASSES, width], U32)
+            scales = sb("z_sc%d" % q, [P, PASSES, width], U8)
+            quantize(
+                words[:].rearrange("p b t -> p (b t)"),
+                scales[:].rearrange("p b t -> p (b t)"),
+                woven[q][:].rearrange("p b t i -> p (b t i)"),
+            )
+            for tile, n0, count in held[q]:
+                for k in range(count):
+                    rows = slice((n0 + k) * P, (n0 + k + 1) * P)
+                    for b in range(PASSES):
+                        nc.tensor.matmul_mx(
+                            out=tile[:, k, :],
+                            lhsT=wo_w[:, b, rows].bitcast(FP8X4),
+                            lhsT_scale=wo_sc[:, b, rows],
+                            rhs=words[:, b, :].bitcast(FP8X4),
+                            rhs_scale=scales[:, b, :],
+                            start=(b == 0),
+                            stop=(b == PASSES - 1),
+                        )
+
+        def leave(q):
+            cols = chunks[q]
+            width = cols.stop - cols.start
+            room = staged[q][:, 0 : N_TILES * width].rearrange("p (n t) -> p n t", n=N_TILES)
+            for k, (tile, n0, count) in enumerate(held[q]):
+                copy = nc.vector.tensor_copy if (q, k) in VECTOR_LEAVES else nc.scalar.copy
+                copy(room[:, n0 : n0 + count, :], tile)
+            nc.sync.dma_start(out=out_view[:, :, cols], in_=room)
+
+        scatter(LAST)
+        last_chunk = len(chunks) - 1
+        z_on_vector(LAST, chunks[0])
+        z_on_vector(LAST, chunks[1])
+        for q in range(len(chunks)):
+            fill(q)
+            if q + 2 <= last_chunk:
+                z_on_vector(LAST, chunks[q + 2])
+            finish(q)
+        for q in range(len(chunks)):
+            leave(q)

@@ -27,7 +27,7 @@ PASSES = 2
 SLICES = H // P
 LAST = SLICES - 1
 POOL_SLICES = SLICES - 2
-RING = 2
+ONE_PAGE_SLICES = (5, 6)
 CUTS = [0, 256, 512, 768, 1024]
 WEAVE = 256
 SCALAR_FILLS = ()
@@ -64,7 +64,7 @@ def tile_list_demand_response_baseline_kernel(
         wg_w = [sb("wg_w%d" % b, [P, PASSES, 2 * PASS], U8) for b in range(PASSES)]
         tab_w = [sb("tab_w%d" % a, [P, T], I32) for a in range(PASSES)]
         pages = [sb("page%d" % n, [P, T2], F32) for n in range(2)]
-        one_page = sb("one_page", [P, T2], F32)
+        one_pages = {s: sb("one_page%d" % s, [P, T2], F32) for s in ONE_PAGE_SLICES}
         ident = sb("ident", [P, P], F32)
         wa_raw = {}
         for a in range(PASSES):
@@ -72,8 +72,8 @@ def tile_list_demand_response_baseline_kernel(
                 wa_raw[a, b] = sb("wa_raw%d%d" % (a, b), [P, PACK, PASS], F32)
         prior_sb = [sb("prior%d" % b, [P, PACK, S], F32) for b in range(PASSES)]
         wgs_sb = sb("wgs_sb", [P, S], F32)
-        late_loads = sb("late_loads", [P, PACK, T2], F32)
-        late_rows = late_loads[:].bitcast(BF16)[:, :, 0:T2]
+        late_loads = sb("late_loads", [P, PACK * T2], F32)[:].rearrange("p (r t) -> p r t", r=PACK)
+        late_rows = late_loads.bitcast(BF16)[:, :, 0:T2]
         load_sb = [
             late_loads[:, s - PACK + 1, :] if PACK - 1 <= s < LAST else sb("load%d" % s, [P, T2], F32)[:]
             for s in range(SLICES)
@@ -88,7 +88,8 @@ def tile_list_demand_response_baseline_kernel(
         make_identity(nc, ident[:])
         for page in pages:
             nc.gpsimd.memset(page[:], 0.0)
-        nc.gpsimd.memset(one_page[:], 1.0)
+        for s in ONE_PAGE_SLICES:
+            nc.gpsimd.memset(one_pages[s][:], 1.0)
         clear(nc.gpsimd, wg_sc[1])
         clear(nc.gpsimd, wo_sc)
 
@@ -120,8 +121,8 @@ def tile_list_demand_response_baseline_kernel(
         fetch_tab(1)
         fetch_wg(0)
         fetch_wa(0)
-        fetch_prior(0, 0, 1)
         nc.sync.dma_start(out=wgs_sb[:], in_=wgs)
+        fetch_prior(0, 0, 1)
         nc.sync.dma_start(idx2[:], offs2)
         fetch_prior(0, 1, PACK)
         fetch_wg(1)
@@ -188,7 +189,7 @@ def tile_list_demand_response_baseline_kernel(
                         stop=(a == PASSES - 1),
                     )
                 nc.scalar.activation(
-                    gate_t[b][:, first:PACK, cols],
+                    gate_t[b][:, c, first * P :].rearrange("e (i m) -> e i m", m=P),
                     score[:].rearrange("e (m i) -> e i m", i=PACK)[:, first:PACK, :],
                     SIGMOID,
                     scale=-1.0,
@@ -197,12 +198,14 @@ def tile_list_demand_response_baseline_kernel(
         def prior_of(s):
             return prior_sb[s // PACK][:, s % PACK, :]
 
-        def turn_into(target, src, start, stop):
-            for c in range(S // P):
-                cols = slice(c * P, (c + 1) * P)
+        def quarters(src):
+            return [src[:, c * P : (c + 1) * P] for c in range(S // P)]
+
+        def turn_into(target, parts, start, stop):
+            for c, part in enumerate(parts):
                 nc.tensor.matmul(
-                    target[:, cols],
-                    src[:, cols],
+                    target[:, c * P : (c + 1) * P],
+                    part,
                     ident[:],
                     is_transpose=True,
                     start=(start and c == 0),
@@ -225,24 +228,29 @@ def tile_list_demand_response_baseline_kernel(
             nc.scalar.activation(gate[:], score[:], SIGMOID)
             return gate
 
-        late_room = sb("late_room", [P, 2 * PACK - 1, S], F32)
-        late_values = late_room[:, PACK - 1 :, :].rearrange("p r j -> p (r j)").bitcast(BF16)
+        late_room = sb("late_room", [P, 6 * S + S // 2], F32)[:]
+        late_values = late_room[:, 0 : PACK * S].bitcast(BF16)
         late_rounded = late_values.rearrange("p (a i m j) -> p a i m j", a=PASSES, i=PACK, j=PACK)
-        taken_t = [sb("taken_t0", [P, PACK, S], F32, tag="tab_w1"), late_room[:, 0:PACK, :]]
+        taken_t = [sb("taken_t0", [P, PACK, S], F32, tag="tab_w1"), late_room[:, 2 * S + S // 2 :].rearrange("p (c r) -> p c r", c=PACK)]
         late_prior_t = sb("late_prior_t", [P, PACK, S], F32, tag="tab_w0")
         prior_t = [(late_prior_t if s // PACK else wa_raw[0, 0])[:, s % PACK, :] for s in range(SLICES)]
         kept_t = [wa_raw[1 - s // PACK, s // PACK][:, s % PACK, :] for s in range(SLICES)]
-        source = [sb("source%d" % s, [P, S], F32)[:] if s in (0, 1, 5, 6, 7) else None for s in range(SLICES)]
-        source[2] = late_room[:, PACK - 1, :]
-        source[3] = late_room[:, PACK, :]
-        source[4] = kept_t[6]
+        late_kept = wa_raw[0, 1][:].rearrange("p j c -> p (j c)")
+        for place, s in enumerate((7, 5, 6, 4)):
+            kept_t[s] = late_kept[:, place * S : (place + 1) * S]
+        source = [sb("source%d" % s, [P, S], F32)[:] if s in (0, 1, 5, 6) else None for s in range(SLICES)]
+        source[2] = late_room[:, 3 * S : 4 * S]
+        source[3] = late_room[:, 0:S]
+        source[4] = late_kept[:, S + S // 2 : 2 * S + S // 2]
+        product = {5: late_kept[:, 2 * S + S // 2 : 3 * S + S // 2], 6: source[0]}
+        source[7] = source[0]
         total = [total_banks[s % 2] for s in range(SLICES)]
         total[6] = side_banks[0]
         total[7] = total_banks[0]
 
         def first_h(gate):
             fit = total_banks[1]
-            for a, unused, codes, scales in pieces[0]:
+            for a, unused, codes, scales in pieces[0][0:PASSES]:
                 nc.tensor.matmul_mx(
                     out=fit[:],
                     lhsT=codes[:, 0:P].bitcast(FP8X4),
@@ -276,65 +284,65 @@ def tile_list_demand_response_baseline_kernel(
                 )
 
         def make_taken(b, c, first):
-            cols = slice(c * P, (c + 1) * P)
+            rows = slice(first * P, PASS)
             nc.vector.scalar_tensor_tensor(
-                taken_t[b][:, first:PACK, cols],
-                gate_t[b][:, first:PACK, cols],
-                1.0,
-                fit_banks[c][:].rearrange("e (i m) -> e i m", i=PACK)[:, first:PACK, :],
-                SUB,
-                MULT,
+                taken_t[b][:, c, rows], gate_t[b][:, c, rows], 1.0, fit_banks[c][:, rows], SUB, MULT
             )
 
         def make_kept(s):
             b, i = divmod(s, PACK)
             turned = side_banks[s % 2]
-            turn_into(turned, prior_of(s), True, True)
+            turn_into(turned, quarters(prior_of(s)), True, True)
             nc.scalar.activation(prior_t[s], turned[:], COPY, scale=-1.0)
-            nc.gpsimd.tensor_tensor(kept_t[s], gate_t[b][:, i, :], prior_t[s], MULT)
+            nc.gpsimd.tensor_tensor(
+                kept_t[s].rearrange("e (c m) -> e c m", m=P),
+                gate_t[b][:, :, i * P : (i + 1) * P],
+                prior_t[s].rearrange("e (c m) -> e c m", m=P),
+                MULT,
+            )
 
         def make_total(s):
             b, i = divmod(s, PACK)
-            parts = [kept_t[s], taken_t[b][:, i, :]]
+            parts = [quarters(kept_t[s]), [taken_t[b][:, c, i * P : (i + 1) * P] for c in range(S // P)]]
             if s == 6:
                 parts = parts[::-1]
             turn_into(total[s], parts[0], True, False)
             turn_into(total[s], parts[1], False, True)
 
         def make_source(s, h):
-            if s == LAST - 1:
-                product = kept_t[4]
-                nc.vector.scalar_tensor_tensor(product, h, -1.0, wgs_sb[:], MULT, MULT)
-                nc.gpsimd.tensor_scalar(source[s], product, 1.0, 1.0, MULT, ADD)
+            if s in ONE_PAGE_SLICES:
+                nc.vector.scalar_tensor_tensor(product[s], h, -1.0, wgs_sb[:], MULT, MULT)
+                nc.gpsimd.tensor_scalar(source[s], product[s], 1.0, 1.0, MULT, ADD)
             else:
                 nc.vector.scalar_tensor_tensor(source[s], h, -1.0, wgs_sb[:], MULT, MULT)
 
-        page_of = [one_page if s == LAST - 1 else pages[s % 2] for s in range(SLICES)]
+        page_of = [one_pages.get(s, pages[s % 2]) for s in range(SLICES)]
 
         def scatter(s):
             nc.vector.tensor_copy(page_of[s][:].indirect(idx2[:]), source[s])
 
-        early_rows = sb("early_rows", [P, T2 // WEAVE, PACK, WEAVE], BF16)
-        early_room = early_rows[:].rearrange("p q i t -> p (q i t)").bitcast(F32)
+        early_room = sb("early_room", [P, 2 * T2], F32)[:]
+        early_rows = early_room.bitcast(BF16).rearrange("p (q i t) -> p q i t", i=PACK, t=WEAVE)
 
         def z_on_vector(s, cols):
             nc.vector.scalar_tensor_tensor(late_rows[:, s - PACK, cols], pages[s % 2][:, cols], 1.0, load_sb[s][:, cols], ADD, MULT)
 
         factors = [wa_raw[0, 0][:, j : j + 2, :].rearrange("p j c -> p (j c)") for j in (2, 2, 0, 2, 0)]
-        factors += [early_room[:, 0:T2], one_page[:]]
+        factors += [one_pages[s][:] for s in ONE_PAGE_SLICES]
 
         def z_on_gpsimd(s):
             if s < 2:
                 nc.gpsimd.tensor_scalar(factors[s], pages[s % 2][:], 1.0, 1.0, MULT, ADD)
-            elif s < LAST - 1:
+            elif s not in ONE_PAGE_SLICES:
                 nc.scalar.activation(factors[s], pages[s % 2][:], COPY, bias=1.0)
             if s < PACK:
-                nc.gpsimd.tensor_tensor(
-                    early_rows[:, :, s, :],
-                    factors[s].rearrange("p (q t) -> p q t", t=WEAVE),
-                    load_sb[s].rearrange("p (q t) -> p q t", t=WEAVE),
-                    MULT,
-                )
+                for q in ([slice(0, 2), slice(2, 4)] if s == 0 else [slice(0, 4)]):
+                    nc.gpsimd.tensor_tensor(
+                        early_rows[:, q, s, :],
+                        factors[s].rearrange("p (q t) -> p q t", t=WEAVE)[:, q, :],
+                        load_sb[s].rearrange("p (q t) -> p q t", t=WEAVE)[:, q, :],
+                        MULT,
+                    )
             else:
                 nc.gpsimd.tensor_tensor(late_rows[:, s - PACK, :], factors[s], load_sb[s], MULT)
 
@@ -361,8 +369,9 @@ def tile_list_demand_response_baseline_kernel(
         turned_gates(0, 1, [banks[1], banks[2], banks[3], banks[4]])
         first_half_of_wa(nc.vector.tensor_copy, 0, 0, PACK)
         first_half_of_wa(nc.vector.tensor_copy, 1, 0, 2)
+        first_half_of_wa(nc.vector.tensor_copy, 1, 2, PACK)
         first = first_h(gate)
-        first_half_of_wa(nc.scalar.copy, 1, 2, PACK, tag="kept")
+
         make_source(0, first)
         for c in range(PACK):
             turned_fit(0, c)

@@ -27,11 +27,12 @@ PASSES = 2
 SLICES = H // P
 LAST = SLICES - 1
 POOL_SLICES = SLICES - 2
-ONE_PAGE_SLICES = (5, 6)
+ONE_PAGE_SLICES = (4, 5, 6)
 CUTS = [0, 256, 512, 768, 1024]
 WEAVE = 256
 SCALAR_FILLS = ()
 VECTOR_LEAVES = ((3, 0),)
+BY_BANK = ()
 N_TILES = N // P
 NEIGHBOURS = 4
 
@@ -241,8 +242,8 @@ def tile_list_demand_response_baseline_kernel(
         source = [sb("source%d" % s, [P, S], F32)[:] if s in (0, 1, 5, 6) else None for s in range(SLICES)]
         source[2] = late_room[:, 3 * S : 4 * S]
         source[3] = late_room[:, 0:S]
-        source[4] = late_kept[:, S + S // 2 : 2 * S + S // 2]
-        product = {5: late_kept[:, 2 * S + S // 2 : 3 * S + S // 2], 6: source[0]}
+        source[4] = source[1]
+        product = {4: late_kept[:, S + S // 2 : 2 * S + S // 2], 5: late_kept[:, 2 * S + S // 2 : 3 * S + S // 2], 6: source[0]}
         source[7] = source[0]
         total = [total_banks[s % 2] for s in range(SLICES)]
         total[6] = side_banks[0]
@@ -313,6 +314,9 @@ def tile_list_demand_response_baseline_kernel(
             if s in ONE_PAGE_SLICES:
                 nc.vector.scalar_tensor_tensor(product[s], h, -1.0, wgs_sb[:], MULT, MULT)
                 nc.gpsimd.tensor_scalar(source[s], product[s], 1.0, 1.0, MULT, ADD)
+            elif s == LAST:
+                nc.scalar.activation(factors[0][:, 0:S], h, COPY, scale=-1.0)
+                nc.gpsimd.tensor_tensor(source[s], factors[0][:, 0:S], wgs_sb[:], MULT)
             else:
                 nc.vector.scalar_tensor_tensor(source[s], h, -1.0, wgs_sb[:], MULT, MULT)
 
@@ -327,11 +331,11 @@ def tile_list_demand_response_baseline_kernel(
         def z_on_vector(s, cols):
             nc.vector.scalar_tensor_tensor(late_rows[:, s - PACK, cols], pages[s % 2][:, cols], 1.0, load_sb[s][:, cols], ADD, MULT)
 
-        factors = [wa_raw[0, 0][:, j : j + 2, :].rearrange("p j c -> p (j c)") for j in (2, 2, 0, 2, 0)]
+        factors = [wa_raw[0, 0][:, j : j + 2, :].rearrange("p j c -> p (j c)") for j in (2, 2, 2, 2)]
         factors += [one_pages[s][:] for s in ONE_PAGE_SLICES]
 
         def z_on_gpsimd(s):
-            if s < 2:
+            if s == 0:
                 nc.gpsimd.tensor_scalar(factors[s], pages[s % 2][:], 1.0, 1.0, MULT, ADD)
             elif s not in ONE_PAGE_SLICES:
                 nc.scalar.activation(factors[s], pages[s % 2][:], COPY, bias=1.0)
@@ -476,7 +480,10 @@ def tile_list_demand_response_baseline_kernel(
             for k, (tile, n0, count) in enumerate(held[q]):
                 copy = nc.vector.tensor_copy if (q, k) in VECTOR_LEAVES else nc.scalar.copy
                 copy(room[:, n0 : n0 + count, :], tile)
-            nc.sync.dma_start(out=out_view[:, :, cols], in_=room)
+                if q in BY_BANK:
+                    nc.sync.dma_start(out=out_view[:, n0 : n0 + count, cols], in_=room[:, n0 : n0 + count, :])
+            if q not in BY_BANK:
+                nc.sync.dma_start(out=out_view[:, :, cols], in_=room)
 
         scatter(LAST)
         last_chunk = len(chunks) - 1

@@ -28,11 +28,11 @@ SLICES = H // P
 LAST = SLICES - 1
 POOL_SLICES = SLICES - 2
 ONE_PAGE_SLICES = (4, 5, 6)
-CUTS = [0, 256, 512, 768, 1024]
+CUTS = [0, 128, 384, 640, 896, 1024]
 WEAVE = 256
-SCALAR_FILLS = ()
-VECTOR_LEAVES = ((3, 0),)
-BY_BANK = ()
+SCALAR_FILLS = (1,)
+VECTOR_LEAVES = ((3, 0), (4, 0))
+BY_BANK = (1, 2, 3)
 N_TILES = N // P
 NEIGHBOURS = 4
 
@@ -351,23 +351,20 @@ def tile_list_demand_response_baseline_kernel(
                 nc.gpsimd.tensor_tensor(late_rows[:, s - PACK, :], factors[s], load_sb[s], MULT)
 
         chunks = [slice(c0, c1) for c0, c1 in zip(CUTS, CUTS[1:])]
-        woven = [sb("woven%d" % q, [P, PASSES, cols.stop - cols.start, PACK], BF16) for q, cols in enumerate(chunks)]
+        early_woven = sb("early_woven", [P, T2, PACK], BF16)
+        late_woven = [sb("late_woven%d" % q, [P, cols.stop - cols.start, PACK], BF16) for q, cols in enumerate(chunks)]
 
-        def weave(copy, q, b, rows, c0, c1, i0, i1):
+        def weave(copy, woven, rows, i0, i1):
             copy(
-                out=woven[q][:, b, c0:c1, :].rearrange("p (c n) i -> p c i n", n=NEIGHBOURS)[:, :, i0:i1, :],
+                out=woven.rearrange("p (c n) i -> p c i n", n=NEIGHBOURS)[:, :, i0:i1, :],
                 in_=rows[:, i0:i1, :].rearrange("p i (c n) -> p c i n", n=NEIGHBOURS),
             )
 
         def weave_early(piece):
-            for q, cols in enumerate(chunks):
-                c0, c1 = max(cols.start, piece * WEAVE), min(cols.stop, (piece + 1) * WEAVE)
-                if c0 < c1:
-                    rows = early_rows[:, piece, :, c0 - piece * WEAVE : c1 - piece * WEAVE]
-                    weave(nc.scalar.copy, q, 0, rows, c0 - cols.start, c1 - cols.start, 0, PACK)
+            weave(nc.scalar.copy, early_woven[:, piece * WEAVE : (piece + 1) * WEAVE, :], early_rows[:, piece, :, :], 0, PACK)
 
         def weave_late(copy, q, i0, i1):
-            weave(copy, q, 1, late_rows[:, 0:PACK, chunks[q]], 0, chunks[q].stop - chunks[q].start, i0, i1)
+            weave(copy, late_woven[q][:], late_rows[:, :, chunks[q]], i0, i1)
 
         gate = first_gate()
         turned_gates(0, 1, [banks[1], banks[2], banks[3], banks[4]])
@@ -443,6 +440,20 @@ def tile_list_demand_response_baseline_kernel(
                 tile = free_banks.pop(0)[:, 0 : count * width].rearrange("p (n t) -> p n t", n=count)
                 held[q].append((tile, n0, count))
 
+        def out_pass(b, q, words, scales):
+            for tile, n0, count in held[q]:
+                for k in range(count):
+                    rows = slice((n0 + k) * P, (n0 + k + 1) * P)
+                    nc.tensor.matmul_mx(
+                        out=tile[:, k, :],
+                        lhsT=wo_w[:, b, rows].bitcast(FP8X4),
+                        lhsT_scale=wo_sc[:, b, rows],
+                        rhs=words.bitcast(FP8X4),
+                        rhs_scale=scales,
+                        start=(b == 0 and k == 0),
+                        stop=(b == PASSES - 1 and k == count - 1),
+                    )
+
         out_view = out.rearrange("(n p) t -> p n t", p=P)
         staged = [wa_raw[a, b][:].rearrange("p j c -> p (j c)") for a in range(PASSES) for b in range(PASSES)]
         staged.append(prior_sb[0][:].rearrange("p i j -> p (i j)"))
@@ -450,28 +461,13 @@ def tile_list_demand_response_baseline_kernel(
         def fill(q):
             weave_late(nc.scalar.copy if q in SCALAR_FILLS else nc.vector.tensor_copy, q, 2, PACK)
 
-        def finish(q):
+        def finish(b, q):
             width = chunks[q].stop - chunks[q].start
-            words = sb("z_words%d" % q, [P, PASSES, width], U32)
-            scales = sb("z_sc%d" % q, [P, PASSES, width], U8)
-            quantize(
-                words[:].rearrange("p b t -> p (b t)"),
-                scales[:].rearrange("p b t -> p (b t)"),
-                woven[q][:].rearrange("p b t i -> p (b t i)"),
-            )
-            for tile, n0, count in held[q]:
-                for k in range(count):
-                    rows = slice((n0 + k) * P, (n0 + k + 1) * P)
-                    for b in range(PASSES):
-                        nc.tensor.matmul_mx(
-                            out=tile[:, k, :],
-                            lhsT=wo_w[:, b, rows].bitcast(FP8X4),
-                            lhsT_scale=wo_sc[:, b, rows],
-                            rhs=words[:, b, :].bitcast(FP8X4),
-                            rhs_scale=scales[:, b, :],
-                            start=(b == 0),
-                            stop=(b == PASSES - 1),
-                        )
+            words = sb("z_words%d%d" % (b, q), [P, width], U32)
+            scales = sb("z_sc%d%d" % (b, q), [P, width], U8)
+            woven = late_woven[q][:] if b else early_woven[:, chunks[q], :]
+            quantize(words[:], scales[:], woven.rearrange("p t i -> p (t i)"))
+            out_pass(b, q, words[:], scales[:])
 
         def leave(q):
             cols = chunks[q]
@@ -486,6 +482,8 @@ def tile_list_demand_response_baseline_kernel(
                 nc.sync.dma_start(out=out_view[:, :, cols], in_=room)
 
         scatter(LAST)
+        for q in range(len(chunks)):
+            finish(0, q)
         last_chunk = len(chunks) - 1
         z_on_vector(LAST, chunks[0])
         z_on_vector(LAST, chunks[1])
@@ -493,6 +491,6 @@ def tile_list_demand_response_baseline_kernel(
             fill(q)
             if q + 2 <= last_chunk:
                 z_on_vector(LAST, chunks[q + 2])
-            finish(q)
+            finish(1, q)
         for q in range(len(chunks)):
             leave(q)

@@ -463,11 +463,11 @@ def tile_list_demand_response_baseline_kernel(
 
         def finish(b, q):
             width = chunks[q].stop - chunks[q].start
-            words = sb("z_words%d%d" % (b, q), [P, width], U32)
+            words = sb("late_z_words%d" % q, [P, width], U32)[:] if b else early_words[:, chunks[q]]
             scales = sb("z_sc%d%d" % (b, q), [P, width], U8)
             woven = late_woven[q][:] if b else early_woven[:, chunks[q], :]
-            quantize(words[:], scales[:], woven.rearrange("p t i -> p (t i)"))
-            out_pass(b, q, words[:], scales[:])
+            quantize(words, scales[:], woven.rearrange("p t i -> p (t i)"))
+            out_pass(b, q, words, scales[:])
 
         def leave(q):
             cols = chunks[q]
@@ -482,6 +482,7 @@ def tile_list_demand_response_baseline_kernel(
                 nc.sync.dma_start(out=out_view[:, :, cols], in_=room)
 
         scatter(LAST)
+        early_words = sb("early_words", [P, T2], U32, tag="source0")
         for q in range(len(chunks)):
             finish(0, q)
         last_chunk = len(chunks) - 1

@@ -27,7 +27,7 @@ PASSES = 2
 SLICES = H // P
 LAST = SLICES - 1
 POOL_SLICES = SLICES - 2
-ONE_PAGE_SLICES = (4, 5, 6)
+ONE_PAGE_SLICES = (3, 4, 5, 6)
 CUTS = [0, 128, 384, 640, 896, 1024]
 WEAVE = 256
 SCALAR_FILLS = (1,)
@@ -73,10 +73,12 @@ def tile_list_demand_response_baseline_kernel(
                 wa_raw[a, b] = sb("wa_raw%d%d" % (a, b), [P, PACK, PASS], F32)
         prior_sb = [sb("prior%d" % b, [P, PACK, S], F32) for b in range(PASSES)]
         wgs_sb = sb("wgs_sb", [P, S], F32)
-        late_loads = sb("late_loads", [P, PACK * T2], F32)[:].rearrange("p (r t) -> p r t", r=PACK)
+        late_tile = sb("late_tile", [P, (PACK + 1) * T2], F32)[:]
+        late_loads = late_tile[:, 0 : PACK * T2].rearrange("p (r t) -> p r t", r=PACK)
         late_rows = late_loads.bitcast(BF16)[:, :, 0:T2]
+        late_kept = late_tile[:, (PACK - 1) * T2 :]
         load_sb = [
-            late_loads[:, s - PACK + 1, :] if PACK - 1 <= s < LAST else sb("load%d" % s, [P, T2], F32)[:]
+            late_loads[:, s - PACK + 1, :] if PACK - 1 <= s < LAST - 1 else sb("load%d" % s, [P, T2], F32)[:]
             for s in range(SLICES)
         ]
         wo_w = sb("wo_w", [P, PASSES, N], I32)
@@ -88,7 +90,7 @@ def tile_list_demand_response_baseline_kernel(
         clear(nc.vector, wg_sc[0])
         make_identity(nc, ident[:])
         for page in pages:
-            nc.gpsimd.memset(page[:], 0.0)
+            nc.vector.memset(page[:], 0.0)
         for s in ONE_PAGE_SLICES:
             nc.gpsimd.memset(one_pages[s][:], 1.0)
         clear(nc.gpsimd, wg_sc[1])
@@ -236,14 +238,13 @@ def tile_list_demand_response_baseline_kernel(
         late_prior_t = sb("late_prior_t", [P, PACK, S], F32, tag="tab_w0")
         prior_t = [(late_prior_t if s // PACK else wa_raw[0, 0])[:, s % PACK, :] for s in range(SLICES)]
         kept_t = [wa_raw[1 - s // PACK, s // PACK][:, s % PACK, :] for s in range(SLICES)]
-        late_kept = wa_raw[0, 1][:].rearrange("p j c -> p (j c)")
         for place, s in enumerate((7, 5, 6, 4)):
             kept_t[s] = late_kept[:, place * S : (place + 1) * S]
         source = [sb("source%d" % s, [P, S], F32)[:] if s in (0, 1, 5, 6) else None for s in range(SLICES)]
         source[2] = late_room[:, 3 * S : 4 * S]
-        source[3] = late_room[:, 0:S]
+        source[3] = prior_t[4]
         source[4] = source[1]
-        product = {4: late_kept[:, S + S // 2 : 2 * S + S // 2], 5: late_kept[:, 2 * S + S // 2 : 3 * S + S // 2], 6: source[0]}
+        product = {3: late_room[:, 0:S], 4: late_kept[:, S + S // 2 : 2 * S + S // 2], 5: late_kept[:, 2 * S + S // 2 : 3 * S + S // 2], 6: source[0]}
         source[7] = source[0]
         total = [total_banks[s % 2] for s in range(SLICES)]
         total[6] = side_banks[0]
@@ -310,10 +311,14 @@ def tile_list_demand_response_baseline_kernel(
             turn_into(total[s], parts[0], True, False)
             turn_into(total[s], parts[1], False, True)
 
+        def add_one(s):
+            nc.scalar.activation(source[s], product[s], COPY, bias=1.0)
+
         def make_source(s, h):
             if s in ONE_PAGE_SLICES:
                 nc.vector.scalar_tensor_tensor(product[s], h, -1.0, wgs_sb[:], MULT, MULT)
-                nc.gpsimd.tensor_scalar(source[s], product[s], 1.0, 1.0, MULT, ADD)
+                if s > 3:
+                    add_one(s)
             elif s == LAST:
                 nc.scalar.activation(factors[0][:, 0:S], h, COPY, scale=-1.0)
                 nc.gpsimd.tensor_tensor(source[s], factors[0][:, 0:S], wgs_sb[:], MULT)
@@ -331,7 +336,7 @@ def tile_list_demand_response_baseline_kernel(
         def z_on_vector(s, cols):
             nc.vector.scalar_tensor_tensor(late_rows[:, s - PACK, cols], pages[s % 2][:, cols], 1.0, load_sb[s][:, cols], ADD, MULT)
 
-        factors = [wa_raw[0, 0][:, j : j + 2, :].rearrange("p j c -> p (j c)") for j in (2, 2, 2, 2)]
+        factors = [wa_raw[0, 0][:, j : j + 2, :].rearrange("p j c -> p (j c)") for j in (2, 2, 2)]
         factors += [one_pages[s][:] for s in ONE_PAGE_SLICES]
 
         def z_on_gpsimd(s):
@@ -351,7 +356,7 @@ def tile_list_demand_response_baseline_kernel(
                 nc.gpsimd.tensor_tensor(late_rows[:, s - PACK, :], factors[s], load_sb[s], MULT)
 
         chunks = [slice(c0, c1) for c0, c1 in zip(CUTS, CUTS[1:])]
-        early_woven = sb("early_woven", [P, T2, PACK], BF16)
+        early_woven = late_kept.bitcast(BF16).rearrange("p (t i) -> p t i", i=PACK)
         late_woven = [sb("late_woven%d" % q, [P, cols.stop - cols.start, PACK], BF16) for q, cols in enumerate(chunks)]
 
         def weave(copy, woven, rows, i0, i1):
@@ -404,6 +409,7 @@ def tile_list_demand_response_baseline_kernel(
             turned_fit(1, c)
         for s in range(PACK, SLICES):
             make_kept(s)
+        add_one(3)
 
         scatter(2)
         for c in range(PACK):
@@ -418,12 +424,12 @@ def tile_list_demand_response_baseline_kernel(
         scatter(4)
         blend(7)
         z_on_gpsimd(4)
-        weave_early(0)
         weave_early(1)
+        weave_early(2)
         scatter(5)
         z_on_gpsimd(5)
-        weave_early(2)
         weave_early(3)
+        weave_early(0)
         scatter(6)
         z_on_gpsimd(6)
         for q in range(len(chunks)):
@@ -455,8 +461,7 @@ def tile_list_demand_response_baseline_kernel(
                     )
 
         out_view = out.rearrange("(n p) t -> p n t", p=P)
-        staged = [wa_raw[a, b][:].rearrange("p j c -> p (j c)") for a in range(PASSES) for b in range(PASSES)]
-        staged.append(prior_sb[0][:].rearrange("p i j -> p (i j)"))
+        staged = [load_sb[s] for s in range(3)] + [tile[:].rearrange("p i j -> p (i j)") for tile in prior_sb]
 
         def fill(q):
             weave_late(nc.scalar.copy if q in SCALAR_FILLS else nc.vector.tensor_copy, q, 2, PACK)
@@ -482,8 +487,8 @@ def tile_list_demand_response_baseline_kernel(
                 nc.sync.dma_start(out=out_view[:, :, cols], in_=room)
 
         scatter(LAST)
-        early_words = sb("early_words", [P, T2], U32, tag="source0")
-        for q in range(len(chunks)):
+        early_words = sb("early_words", [P, T2], U32, tag="load6")
+        for q in (2, 3, 4, 0, 1):
             finish(0, q)
         last_chunk = len(chunks) - 1
         z_on_vector(LAST, chunks[0])

@@ -27,7 +27,7 @@ PASSES = 2
 SLICES = H // P
 LAST = SLICES - 1
 POOL_SLICES = SLICES - 2
-ONE_PAGE_SLICES = (3, 4, 5, 6)
+ONE_PAGE_SLICES = (0, 3, 4, 5, 6)
 CUTS = [0, 128, 384, 640, 896, 1024]
 WEAVE = 256
 SCALAR_FILLS = (1,)
@@ -65,7 +65,7 @@ def tile_list_demand_response_baseline_kernel(
         wg_w = [sb("wg_w%d" % b, [P, PASSES, 2 * PASS], U8) for b in range(PASSES)]
         tab_w = [sb("tab_w%d" % a, [P, T], I32) for a in range(PASSES)]
         pages = [sb("page%d" % n, [P, T2], F32) for n in range(2)]
-        one_pages = {s: sb("one_page%d" % s, [P, T2], F32) for s in ONE_PAGE_SLICES}
+        one_pages = {s: sb("one_page%d" % s, [P, T2], F32) for s in range(3, LAST)}
         ident = sb("ident", [P, P], F32)
         wa_raw = {}
         for a in range(PASSES):
@@ -91,8 +91,9 @@ def tile_list_demand_response_baseline_kernel(
         make_identity(nc, ident[:])
         for page in pages:
             nc.vector.memset(page[:], 0.0)
-        for s in ONE_PAGE_SLICES:
+        for s in (6, 3, 4, 5):
             nc.gpsimd.memset(one_pages[s][:], 1.0)
+        one_pages[0] = one_pages[6]
         clear(nc.gpsimd, wg_sc[1])
         clear(nc.gpsimd, wo_sc)
 
@@ -130,8 +131,9 @@ def tile_list_demand_response_baseline_kernel(
         fetch_prior(0, 1, PACK)
         fetch_wg(1)
         fetch_wa(1)
+        fetch_load(0)
         fetch_prior(1, 0, PACK)
-        for s in range(SLICES):
+        for s in range(1, SLICES):
             fetch_load(s)
         nc.sync.dma_start(
             out=wo_w[:], in_=wo_words.rearrange("a p c i -> a p (c i)").bitcast(I32).rearrange("a p c -> p a c")
@@ -235,16 +237,17 @@ def tile_list_demand_response_baseline_kernel(
         late_values = late_room[:, 0 : PACK * S].bitcast(BF16)
         late_rounded = late_values.rearrange("p (a i m j) -> p a i m j", a=PASSES, i=PACK, j=PACK)
         taken_t = [sb("taken_t0", [P, PACK, S], F32, tag="tab_w1"), late_room[:, 2 * S + S // 2 :].rearrange("p (c r) -> p c r", c=PACK)]
-        late_prior_t = sb("late_prior_t", [P, PACK, S], F32, tag="tab_w0")
-        prior_t = [(late_prior_t if s // PACK else wa_raw[0, 0])[:, s % PACK, :] for s in range(SLICES)]
+        late_prior_t = sb("late_prior_t", [P, (PACK + 1) * S], F32, tag="tab_w0")
+        prior_t = [wa_raw[0, 0][:, s, :] for s in range(PACK)]
+        prior_t += [late_prior_t[:, place * S : (place + 1) * S] for place in (2, 3, 1, 4)]
         kept_t = [wa_raw[1 - s // PACK, s // PACK][:, s % PACK, :] for s in range(SLICES)]
         for place, s in enumerate((7, 5, 6, 4)):
             kept_t[s] = late_kept[:, place * S : (place + 1) * S]
         source = [sb("source%d" % s, [P, S], F32)[:] if s in (0, 1, 5, 6) else None for s in range(SLICES)]
         source[2] = late_room[:, 3 * S : 4 * S]
-        source[3] = prior_t[4]
+        source[3] = prior_t[7]
         source[4] = source[1]
-        product = {3: late_room[:, 0:S], 4: late_kept[:, S + S // 2 : 2 * S + S // 2], 5: late_kept[:, 2 * S + S // 2 : 3 * S + S // 2], 6: source[0]}
+        product = {0: source[5], 3: late_room[:, 0:S], 4: late_kept[:, S + S // 2 : 2 * S + S // 2], 5: late_kept[:, 2 * S + S // 2 : 3 * S + S // 2], 6: source[0]}
         source[7] = source[0]
         total = [total_banks[s % 2] for s in range(SLICES)]
         total[6] = side_banks[0]
@@ -293,7 +296,7 @@ def tile_list_demand_response_baseline_kernel(
 
         def make_kept(s):
             b, i = divmod(s, PACK)
-            turned = side_banks[s % 2]
+            turned = fit_banks[s - PACK] if s >= PACK else side_banks[s % 2]
             turn_into(turned, quarters(prior_of(s)), True, True)
             nc.scalar.activation(prior_t[s], turned[:], COPY, scale=-1.0)
             nc.gpsimd.tensor_tensor(
@@ -312,16 +315,19 @@ def tile_list_demand_response_baseline_kernel(
             turn_into(total[s], parts[1], False, True)
 
         def add_one(s):
-            nc.scalar.activation(source[s], product[s], COPY, bias=1.0)
+            if s == 0:
+                nc.gpsimd.tensor_scalar(source[s], product[s], 1.0, 1.0, MULT, ADD)
+            else:
+                nc.scalar.activation(source[s], product[s], COPY, bias=1.0)
 
         def make_source(s, h):
             if s in ONE_PAGE_SLICES:
                 nc.vector.scalar_tensor_tensor(product[s], h, -1.0, wgs_sb[:], MULT, MULT)
-                if s > 3:
+                if s != 3:
                     add_one(s)
             elif s == LAST:
-                nc.scalar.activation(factors[0][:, 0:S], h, COPY, scale=-1.0)
-                nc.gpsimd.tensor_tensor(source[s], factors[0][:, 0:S], wgs_sb[:], MULT)
+                nc.scalar.activation(load_sb[3][:, 0:S], h, COPY, scale=-1.0)
+                nc.gpsimd.tensor_tensor(source[s], load_sb[3][:, 0:S], wgs_sb[:], MULT)
             else:
                 nc.vector.scalar_tensor_tensor(source[s], h, -1.0, wgs_sb[:], MULT, MULT)
 
@@ -336,13 +342,13 @@ def tile_list_demand_response_baseline_kernel(
         def z_on_vector(s, cols):
             nc.vector.scalar_tensor_tensor(late_rows[:, s - PACK, cols], pages[s % 2][:, cols], 1.0, load_sb[s][:, cols], ADD, MULT)
 
-        factors = [wa_raw[0, 0][:, j : j + 2, :].rearrange("p j c -> p (j c)") for j in (2, 2, 2)]
-        factors += [one_pages[s][:] for s in ONE_PAGE_SLICES]
+        factor = late_prior_t[:, 0:T2]
+        factors = [page_of[s][:] for s in range(LAST)]
+        factors[1] = factor
+        factors[2] = late_room[:, 0:T2]
 
         def z_on_gpsimd(s):
-            if s == 0:
-                nc.gpsimd.tensor_scalar(factors[s], pages[s % 2][:], 1.0, 1.0, MULT, ADD)
-            elif s not in ONE_PAGE_SLICES:
+            if s not in ONE_PAGE_SLICES:
                 nc.scalar.activation(factors[s], pages[s % 2][:], COPY, bias=1.0)
             if s < PACK:
                 for q in ([slice(0, 2), slice(2, 4)] if s == 0 else [slice(0, 4)]):
@@ -404,11 +410,11 @@ def tile_list_demand_response_baseline_kernel(
         pieces[1] = [(a, slice(0, PASS), late_words[:, a, :], late_sc[:, a, :]) for a in range(PASSES)]
         blend(2)
         blend(3)
+        for s in range(PACK, SLICES):
+            make_kept(s)
         z_on_gpsimd(1)
         for c in range(PACK):
             turned_fit(1, c)
-        for s in range(PACK, SLICES):
-            make_kept(s)
         add_one(3)
 
         scatter(2)

@@ -33,6 +33,7 @@ WEAVE = 256
 SCALAR_FILLS = (1,)
 VECTOR_LEAVES = ((3, 0), (4, 0))
 BY_BANK = (1, 2, 3)
+AHEAD = 2
 N_TILES = N // P
 NEIGHBOURS = 4
 
@@ -326,8 +327,8 @@ def tile_list_demand_response_baseline_kernel(
                 if s != 3:
                     add_one(s)
             elif s == LAST:
-                nc.scalar.activation(load_sb[3][:, 0:S], h, COPY, scale=-1.0)
-                nc.gpsimd.tensor_tensor(source[s], load_sb[3][:, 0:S], wgs_sb[:], MULT)
+                nc.scalar.activation(load_sb[3][:, S:], h, COPY, scale=-1.0)
+                nc.gpsimd.tensor_tensor(source[s], load_sb[3][:, S:], wgs_sb[:], MULT)
             else:
                 nc.vector.scalar_tensor_tensor(source[s], h, -1.0, wgs_sb[:], MULT, MULT)
 
@@ -430,12 +431,12 @@ def tile_list_demand_response_baseline_kernel(
         scatter(4)
         blend(7)
         z_on_gpsimd(4)
+        weave_early(0)
         weave_early(1)
-        weave_early(2)
         scatter(5)
         z_on_gpsimd(5)
+        weave_early(2)
         weave_early(3)
-        weave_early(0)
         scatter(6)
         z_on_gpsimd(6)
         for q in range(len(chunks)):
@@ -494,7 +495,7 @@ def tile_list_demand_response_baseline_kernel(
 
         scatter(LAST)
         early_words = sb("early_words", [P, T2], U32, tag="load6")
-        for q in (2, 3, 4, 0, 1):
+        for q in range(AHEAD):
             finish(0, q)
         last_chunk = len(chunks) - 1
         z_on_vector(LAST, chunks[0])
@@ -503,6 +504,8 @@ def tile_list_demand_response_baseline_kernel(
             fill(q)
             if q + 2 <= last_chunk:
                 z_on_vector(LAST, chunks[q + 2])
+            if AHEAD <= q + 1 <= last_chunk:
+                finish(0, q + 1)
             finish(1, q)
         for q in range(len(chunks)):
             leave(q)

@@ -27,7 +27,7 @@ PASSES = 2
 SLICES = H // P
 LAST = SLICES - 1
 POOL_SLICES = SLICES - 2
-ONE_PAGE_SLICES = (0, 3, 4, 5, 6)
+ONE_PAGE_SLICES = (3, 4, 5, 6)
 CUTS = [0, 128, 384, 640, 896, 1024]
 WEAVE = 256
 SCALAR_FILLS = (1,)
@@ -234,10 +234,12 @@ def tile_list_demand_response_baseline_kernel(
             nc.scalar.activation(gate[:], score[:], SIGMOID)
             return gate
 
-        late_room = sb("late_room", [P, 6 * S + S // 2], F32)[:]
+        late_room = sb("late_room", [P, PACK * S], F32)[:]
         late_values = late_room[:, 0 : PACK * S].bitcast(BF16)
         late_rounded = late_values.rearrange("p (a i m j) -> p a i m j", a=PASSES, i=PACK, j=PACK)
-        taken_t = [sb("taken_t0", [P, PACK, S], F32, tag="tab_w1"), late_room[:, 2 * S + S // 2 :].rearrange("p (c r) -> p c r", c=PACK)]
+        early_room_t = sb("early_taken", [P, 2 * S], F32, tag="tab_w1")
+        early_taken_t = {1: early_room_t[:, 0:S], 2: early_room_t[:, S:], 3: early_room_t[:, 0:S]}
+        taken_t = [None, wa_raw[0, 1]]
         late_prior_t = sb("late_prior_t", [P, (PACK + 1) * S], F32, tag="tab_w0")
         prior_t = [wa_raw[0, 0][:, s, :] for s in range(PACK)]
         prior_t += [late_prior_t[:, place * S : (place + 1) * S] for place in (2, 3, 1, 4)]
@@ -248,7 +250,7 @@ def tile_list_demand_response_baseline_kernel(
         source[2] = late_room[:, 3 * S : 4 * S]
         source[3] = prior_t[7]
         source[4] = source[1]
-        product = {0: source[5], 3: late_room[:, 0:S], 4: late_kept[:, S + S // 2 : 2 * S + S // 2], 5: late_kept[:, 2 * S + S // 2 : 3 * S + S // 2], 6: source[0]}
+        product = {3: late_room[:, 0:S], 4: late_kept[:, S + S // 2 : 2 * S + S // 2], 5: late_kept[:, 2 * S + S // 2 : 3 * S + S // 2], 6: source[0]}
         source[7] = source[0]
         total = [total_banks[s % 2] for s in range(SLICES)]
         total[6] = side_banks[0]
@@ -289,6 +291,32 @@ def tile_list_demand_response_baseline_kernel(
                     stop=(n == len(pieces[b]) - 1),
                 )
 
+        def early_fit(s):
+            for a, rows, codes, scales in pieces[0]:
+                if rows.start <= s * P < rows.stop:
+                    mine = slice(s * P - rows.start, (s + 1) * P - rows.start)
+                    for c in range(S // P):
+                        cols = slice(c * P, (c + 1) * P)
+                        nc.tensor.matmul_mx(
+                            out=fit_banks[s - 1][:, cols],
+                            lhsT=v_w[a][:, cols].bitcast(FP8X4),
+                            lhsT_scale=v_sc[a][:, cols],
+                            rhs=codes[:, mine].bitcast(FP8X4),
+                            rhs_scale=scales[:, mine],
+                            start=(a == 0 and c == 0),
+                            stop=(a == PASSES - 1 and c == S // P - 1),
+                        )
+
+        def early_taken(s):
+            nc.vector.scalar_tensor_tensor(
+                early_taken_t[s].rearrange("e (c m) -> e c m", m=P),
+                gate_t[0][:, :, s * P : (s + 1) * P],
+                1.0,
+                fit_banks[s - 1][:].rearrange("e (c m) -> e c m", m=P),
+                SUB,
+                MULT,
+            )
+
         def make_taken(b, c, first):
             rows = slice(first * P, PASS)
             nc.vector.scalar_tensor_tensor(
@@ -309,17 +337,15 @@ def tile_list_demand_response_baseline_kernel(
 
         def make_total(s):
             b, i = divmod(s, PACK)
-            parts = [quarters(kept_t[s]), [taken_t[b][:, c, i * P : (i + 1) * P] for c in range(S // P)]]
+            taken = quarters(early_taken_t[s]) if b == 0 else [taken_t[b][:, c, i * P : (i + 1) * P] for c in range(S // P)]
+            parts = [quarters(kept_t[s]), taken]
             if s == 6:
                 parts = parts[::-1]
             turn_into(total[s], parts[0], True, False)
             turn_into(total[s], parts[1], False, True)
 
         def add_one(s):
-            if s == 0:
-                nc.gpsimd.tensor_scalar(source[s], product[s], 1.0, 1.0, MULT, ADD)
-            else:
-                nc.scalar.activation(source[s], product[s], COPY, bias=1.0)
+            nc.scalar.activation(source[s], product[s], COPY, bias=1.0)
 
         def make_source(s, h):
             if s in ONE_PAGE_SLICES:
@@ -349,7 +375,7 @@ def tile_list_demand_response_baseline_kernel(
         factors[2] = late_room[:, 0:T2]
 
         def z_on_gpsimd(s):
-            if s not in ONE_PAGE_SLICES:
+            if s in (1, 2):
                 nc.scalar.activation(factors[s], pages[s % 2][:], COPY, bias=1.0)
             if s < PACK:
                 for q in ([slice(0, 2), slice(2, 4)] if s == 0 else [slice(0, 4)]):
@@ -385,10 +411,13 @@ def tile_list_demand_response_baseline_kernel(
         first_half_of_wa(nc.vector.tensor_copy, 1, 2, PACK)
         first = first_h(gate)
 
-        make_source(0, first)
-        for c in range(PACK):
-            turned_fit(0, c)
-            make_taken(0, c, 1)
+        for cols in (slice(0, S // 2), slice(S // 2, S)):
+            nc.vector.scalar_tensor_tensor(source[5][:, cols], first[:, cols], -1.0, wgs_sb[:, cols], MULT, MULT)
+        nc.gpsimd.tensor_scalar(source[0], source[5], 1.0, 1.0, MULT, ADD)
+        for s in range(1, PACK):
+            early_fit(s)
+        early_taken(1)
+        early_taken(2)
         for s in range(1, PACK):
             make_kept(s)
 
@@ -398,6 +427,7 @@ def tile_list_demand_response_baseline_kernel(
 
         scatter(0)
         blend(1)
+        early_taken(3)
         z_on_gpsimd(0)
         for a in range(PASSES):
             for i0 in range(0, PACK, 2):

@@ -26,15 +26,14 @@ PASS = P * PACK
 PASSES = 2
 SLICES = H // P
 LAST = SLICES - 1
-POOL_SLICES = SLICES - 2
+N_TILES = N // P
+CHUNKS = S // P
 ONE_PAGE_SLICES = (3, 4, 5, 6)
 CUTS = [0, 128, 384, 640, 896, 1024]
-WEAVE = 256
+AHEAD = 2
 SCALAR_FILLS = (1,)
 VECTOR_LEAVES = ((3, 0), (4, 0))
-BY_BANK = (1, 2, 3)
-AHEAD = 2
-N_TILES = N // P
+WEAVE = 256
 NEIGHBOURS = 4
 
 
@@ -66,7 +65,7 @@ def tile_list_demand_response_baseline_kernel(
         wg_w = [sb("wg_w%d" % b, [P, PASSES, 2 * PASS], U8) for b in range(PASSES)]
         tab_w = [sb("tab_w%d" % a, [P, T], I32) for a in range(PASSES)]
         pages = [sb("page%d" % n, [P, T2], F32) for n in range(2)]
-        one_pages = {s: sb("one_page%d" % s, [P, T2], F32) for s in range(3, LAST)}
+        one_pages = {s: sb("one_page%d" % s, [P, T2], F32) for s in ONE_PAGE_SLICES}
         ident = sb("ident", [P, P], F32)
         wa_raw = {}
         for a in range(PASSES):
@@ -132,7 +131,8 @@ def tile_list_demand_response_baseline_kernel(
         fetch_prior(0, 1, PACK)
         fetch_wg(1)
         fetch_wa(1)
-        fetch_load(0)
+        for cols in (slice(0, T2 // 2), slice(T2 // 2, T2)):
+            nc.sync.dma_start(out=load_sb[0][:, cols], in_=load_view[0, 0][:, cols])
         fetch_prior(1, 0, PACK)
         for s in range(1, SLICES):
             fetch_load(s)
@@ -158,7 +158,7 @@ def tile_list_demand_response_baseline_kernel(
             out=first_wg_sc[:], in_=wg_sc[0][:].rearrange("p a (m i) -> p a i m", i=PACK)[:, :, 0:1, :]
         )
 
-        pieces = [[], []]
+        early_wa = []
 
         def round_wa(copy, rounded, a, b, i0, i1):
             copy(
@@ -169,19 +169,19 @@ def tile_list_demand_response_baseline_kernel(
         def quantize(words, scales, values):
             nc.vector.quantize_mx(out=words.bitcast(FP8X4), scales=scales, in_=values)
 
-        def first_half_of_wa(copy, a, i0, i1, tag=None):
+        def early_piece(a, i0, i1):
             rounded = sb("wa_rounded%d0%d" % (a, i0), [P, i1 - i0, P, PACK], BF16)[:]
-            round_wa(copy, rounded, a, 0, i0, i1)
-            codes = sb("wa_w%d0%d" % (a, i0), [P, (i1 - i0) * P], U32, tag=tag)[:]
+            round_wa(nc.vector.tensor_copy, rounded, a, 0, i0, i1)
+            codes = sb("wa_w%d0%d" % (a, i0), [P, (i1 - i0) * P], U32)[:]
             scales = sb("wa_sc%d0%d" % (a, i0), [P, (i1 - i0) * P], U8)[:]
             quantize(codes, scales, rounded.rearrange("p i m j -> p (i m j)"))
-            pieces[0].append((a, slice(i0 * P, i1 * P), codes, scales))
+            early_wa.append((a, slice(i0 * P, i1 * P), codes, scales))
 
-        gate_t = {}
+        rest_t = {}
 
-        def turned_gates(b, first, scores):
-            gate_t[b] = wa_raw[1, 1] if b else sb("gate_t0", [P, PACK, S], F32)
-            for c in range(S // P):
+        def turned_rests(b, first, scores):
+            rest_t[b] = wa_raw[1, 1] if b else sb("rest_t0", [P, PACK, S], F32)
+            for c in range(CHUNKS):
                 score = scores[c]
                 cols = slice(c * P, (c + 1) * P)
                 for a in range(PASSES):
@@ -195,7 +195,7 @@ def tile_list_demand_response_baseline_kernel(
                         stop=(a == PASSES - 1),
                     )
                 nc.scalar.activation(
-                    gate_t[b][:, c, first * P :].rearrange("e (i m) -> e i m", m=P),
+                    rest_t[b][:, c, first * P :].rearrange("e (i m) -> e i m", m=P),
                     score[:].rearrange("e (m i) -> e i m", i=PACK)[:, first:PACK, :],
                     SIGMOID,
                     scale=-1.0,
@@ -205,7 +205,7 @@ def tile_list_demand_response_baseline_kernel(
             return prior_sb[s // PACK][:, s % PACK, :]
 
         def quarters(src):
-            return [src[:, c * P : (c + 1) * P] for c in range(S // P)]
+            return [src[:, c * P : (c + 1) * P] for c in range(CHUNKS)]
 
         def turn_into(target, parts, start, stop):
             for c, part in enumerate(parts):
@@ -215,7 +215,7 @@ def tile_list_demand_response_baseline_kernel(
                     ident[:],
                     is_transpose=True,
                     start=(start and c == 0),
-                    stop=(stop and c == S // P - 1),
+                    stop=(stop and c == CHUNKS - 1),
                 )
 
         def first_gate():
@@ -235,30 +235,39 @@ def tile_list_demand_response_baseline_kernel(
             return gate
 
         late_room = sb("late_room", [P, PACK * S], F32)[:]
-        late_values = late_room[:, 0 : PACK * S].bitcast(BF16)
+        late_values = late_room.bitcast(BF16)
         late_rounded = late_values.rearrange("p (a i m j) -> p a i m j", a=PASSES, i=PACK, j=PACK)
-        early_room_t = sb("early_taken", [P, 2 * S], F32, tag="tab_w1")
-        early_taken_t = {1: early_room_t[:, 0:S], 2: early_room_t[:, S:], 3: early_room_t[:, 0:S]}
-        taken_t = [None, wa_raw[0, 1]]
+        early_taken = sb("early_taken", [P, 2 * S], F32, tag="tab_w1")
+        taken_t = {1: early_taken[:, 0:S], 2: early_taken[:, S:], 3: early_taken[:, 0:S]}
+        late_taken_t = wa_raw[0, 1]
         late_prior_t = sb("late_prior_t", [P, (PACK + 1) * S], F32, tag="tab_w0")
         prior_t = [wa_raw[0, 0][:, s, :] for s in range(PACK)]
         prior_t += [late_prior_t[:, place * S : (place + 1) * S] for place in (2, 3, 1, 4)]
-        kept_t = [wa_raw[1 - s // PACK, s // PACK][:, s % PACK, :] for s in range(SLICES)]
-        for place, s in enumerate((7, 5, 6, 4)):
-            kept_t[s] = late_kept[:, place * S : (place + 1) * S]
-        source = [sb("source%d" % s, [P, S], F32)[:] if s in (0, 1, 5, 6) else None for s in range(SLICES)]
+        kept_t = [wa_raw[1, 0][:, s, :] for s in range(PACK)]
+        kept_t += [late_kept[:, place * S : (place + 1) * S] for place in (3, 1, 2, 0)]
+        source = {s: sb("source%d" % s, [P, S], F32)[:] for s in (0, 1, 5, 6)}
         source[2] = late_room[:, 3 * S : 4 * S]
         source[3] = prior_t[7]
         source[4] = source[1]
-        product = {3: late_room[:, 0:S], 4: late_kept[:, S + S // 2 : 2 * S + S // 2], 5: late_kept[:, 2 * S + S // 2 : 3 * S + S // 2], 6: source[0]}
-        source[7] = source[0]
+        product = {
+            0: source[5],
+            3: late_room[:, 0:S],
+            4: late_kept[:, S + S // 2 : 2 * S + S // 2],
+            5: late_kept[:, 2 * S + S // 2 : 3 * S + S // 2],
+            6: source[0],
+        }
+        source[7] = product[6]
         total = [total_banks[s % 2] for s in range(SLICES)]
         total[6] = side_banks[0]
         total[7] = total_banks[0]
+        halves = [slice(0, S // 2), slice(S // 2, S)]
 
-        def first_h(gate):
+        def by_chunk(rows):
+            return rows.rearrange("e (c m) -> e c m", m=P)
+
+        def first_source(gate):
             fit = total_banks[1]
-            for a, unused, codes, scales in pieces[0][0:PASSES]:
+            for a, rows, codes, scales in early_wa[0:PASSES]:
                 nc.tensor.matmul_mx(
                     out=fit[:],
                     lhsT=codes[:, 0:P].bitcast(FP8X4),
@@ -271,31 +280,32 @@ def tile_list_demand_response_baseline_kernel(
             kept = sb("kept", [P, S], F32)
             taken = sb("taken", [P, S], F32)
             nc.vector.scalar_tensor_tensor(kept[:], gate[:], 1.0, prior_of(0), SUB, MULT)
-            halves = [slice(0, S // 2), slice(S // 2, S)]
             for cols in halves:
                 nc.vector.tensor_tensor(taken[:, cols], fit[:, cols], gate[:, cols], MULT)
             for cols in halves:
                 nc.vector.tensor_tensor(taken[:, cols], kept[:, cols], taken[:, cols], SUB)
-            return taken[:]
+            for cols in halves:
+                nc.vector.scalar_tensor_tensor(product[0][:, cols], taken[:, cols], -1.0, wgs_sb[:, cols], MULT, MULT)
+            nc.gpsimd.tensor_scalar(source[0], product[0], 1.0, 1.0, MULT, ADD)
 
-        def turned_fit(b, c):
+        def late_fit(c, words, scales):
             cols = slice(c * P, (c + 1) * P)
-            for n, (a, rows, codes, scales) in enumerate(pieces[b]):
+            for a in range(PASSES):
                 nc.tensor.matmul_mx(
-                    out=fit_banks[c][:, rows],
+                    out=fit_banks[c][:],
                     lhsT=v_w[a][:, cols].bitcast(FP8X4),
                     lhsT_scale=v_sc[a][:, cols],
-                    rhs=codes.bitcast(FP8X4),
-                    rhs_scale=scales,
-                    start=(n == 0),
-                    stop=(n == len(pieces[b]) - 1),
+                    rhs=words[:, a, :].bitcast(FP8X4),
+                    rhs_scale=scales[:, a, :],
+                    start=(a == 0),
+                    stop=(a == PASSES - 1),
                 )
 
         def early_fit(s):
-            for a, rows, codes, scales in pieces[0]:
+            for a, rows, codes, scales in early_wa:
                 if rows.start <= s * P < rows.stop:
                     mine = slice(s * P - rows.start, (s + 1) * P - rows.start)
-                    for c in range(S // P):
+                    for c in range(CHUNKS):
                         cols = slice(c * P, (c + 1) * P)
                         nc.tensor.matmul_mx(
                             out=fit_banks[s - 1][:, cols],
@@ -304,40 +314,26 @@ def tile_list_demand_response_baseline_kernel(
                             rhs=codes[:, mine].bitcast(FP8X4),
                             rhs_scale=scales[:, mine],
                             start=(a == 0 and c == 0),
-                            stop=(a == PASSES - 1 and c == S // P - 1),
+                            stop=(a == PASSES - 1 and c == CHUNKS - 1),
                         )
 
-        def early_taken(s):
-            nc.vector.scalar_tensor_tensor(
-                early_taken_t[s].rearrange("e (c m) -> e c m", m=P),
-                gate_t[0][:, :, s * P : (s + 1) * P],
-                1.0,
-                fit_banks[s - 1][:].rearrange("e (c m) -> e c m", m=P),
-                SUB,
-                MULT,
-            )
+        def make_early_taken(s):
+            rest = rest_t[0][:, :, s * P : (s + 1) * P]
+            nc.vector.scalar_tensor_tensor(by_chunk(taken_t[s]), rest, 1.0, by_chunk(fit_banks[s - 1][:]), SUB, MULT)
 
-        def make_taken(b, c, first):
-            rows = slice(first * P, PASS)
-            nc.vector.scalar_tensor_tensor(
-                taken_t[b][:, c, rows], gate_t[b][:, c, rows], 1.0, fit_banks[c][:, rows], SUB, MULT
-            )
+        def make_late_taken(c):
+            nc.vector.scalar_tensor_tensor(late_taken_t[:, c, :], rest_t[1][:, c, :], 1.0, fit_banks[c][:], SUB, MULT)
 
         def make_kept(s):
             b, i = divmod(s, PACK)
-            turned = fit_banks[s - PACK] if s >= PACK else side_banks[s % 2]
+            turned = fit_banks[i] if b else side_banks[s % 2]
             turn_into(turned, quarters(prior_of(s)), True, True)
             nc.scalar.activation(prior_t[s], turned[:], COPY, scale=-1.0)
-            nc.gpsimd.tensor_tensor(
-                kept_t[s].rearrange("e (c m) -> e c m", m=P),
-                gate_t[b][:, :, i * P : (i + 1) * P],
-                prior_t[s].rearrange("e (c m) -> e c m", m=P),
-                MULT,
-            )
+            nc.gpsimd.tensor_tensor(by_chunk(kept_t[s]), rest_t[b][:, :, i * P : (i + 1) * P], by_chunk(prior_t[s]), MULT)
 
         def make_total(s):
             b, i = divmod(s, PACK)
-            taken = quarters(early_taken_t[s]) if b == 0 else [taken_t[b][:, c, i * P : (i + 1) * P] for c in range(S // P)]
+            taken = [late_taken_t[:, c, i * P : (i + 1) * P] for c in range(CHUNKS)] if b else quarters(taken_t[s])
             parts = [quarters(kept_t[s]), taken]
             if s == 6:
                 parts = parts[::-1]
@@ -347,16 +343,13 @@ def tile_list_demand_response_baseline_kernel(
         def add_one(s):
             nc.scalar.activation(source[s], product[s], COPY, bias=1.0)
 
-        def make_source(s, h):
-            if s in ONE_PAGE_SLICES:
-                nc.vector.scalar_tensor_tensor(product[s], h, -1.0, wgs_sb[:], MULT, MULT)
-                if s != 3:
-                    add_one(s)
-            elif s == LAST:
-                nc.scalar.activation(load_sb[3][:, S:], h, COPY, scale=-1.0)
-                nc.gpsimd.tensor_tensor(source[s], load_sb[3][:, S:], wgs_sb[:], MULT)
+        def make_product(s):
+            if s == LAST:
+                moved = load_sb[3][:, S:]
+                nc.scalar.activation(moved, total[s][:], COPY, scale=-1.0)
+                nc.gpsimd.tensor_tensor(source[s], moved, wgs_sb[:], MULT)
             else:
-                nc.vector.scalar_tensor_tensor(source[s], h, -1.0, wgs_sb[:], MULT, MULT)
+                nc.vector.scalar_tensor_tensor(product.get(s, source[s]), total[s][:], -1.0, wgs_sb[:], MULT, MULT)
 
         page_of = [one_pages.get(s, pages[s % 2]) for s in range(SLICES)]
 
@@ -366,19 +359,20 @@ def tile_list_demand_response_baseline_kernel(
         early_room = sb("early_room", [P, 2 * T2], F32)[:]
         early_rows = early_room.bitcast(BF16).rearrange("p (q i t) -> p q i t", i=PACK, t=WEAVE)
 
-        def z_on_vector(s, cols):
-            nc.vector.scalar_tensor_tensor(late_rows[:, s - PACK, cols], pages[s % 2][:, cols], 1.0, load_sb[s][:, cols], ADD, MULT)
+        def last_z(cols):
+            nc.vector.scalar_tensor_tensor(
+                late_rows[:, LAST - PACK, cols], page_of[LAST][:, cols], 1.0, load_sb[LAST][:, cols], ADD, MULT
+            )
 
-        factor = late_prior_t[:, 0:T2]
         factors = [page_of[s][:] for s in range(LAST)]
-        factors[1] = factor
+        factors[1] = late_prior_t[:, 0:T2]
         factors[2] = late_room[:, 0:T2]
 
         def z_on_gpsimd(s):
             if s in (1, 2):
-                nc.scalar.activation(factors[s], pages[s % 2][:], COPY, bias=1.0)
+                nc.scalar.activation(factors[s], page_of[s][:], COPY, bias=1.0)
             if s < PACK:
-                for q in ([slice(0, 2), slice(2, 4)] if s == 0 else [slice(0, 4)]):
+                for q in [slice(0, 2), slice(2, 4)] if s == 0 else [slice(0, 4)]:
                     nc.gpsimd.tensor_tensor(
                         early_rows[:, q, s, :],
                         factors[s].rearrange("p (q t) -> p q t", t=WEAVE)[:, q, :],
@@ -405,58 +399,54 @@ def tile_list_demand_response_baseline_kernel(
             weave(copy, late_woven[q][:], late_rows[:, :, chunks[q]], i0, i1)
 
         gate = first_gate()
-        turned_gates(0, 1, [banks[1], banks[2], banks[3], banks[4]])
-        first_half_of_wa(nc.vector.tensor_copy, 0, 0, PACK)
-        first_half_of_wa(nc.vector.tensor_copy, 1, 0, 2)
-        first_half_of_wa(nc.vector.tensor_copy, 1, 2, PACK)
-        first = first_h(gate)
-
-        for cols in (slice(0, S // 2), slice(S // 2, S)):
-            nc.vector.scalar_tensor_tensor(source[5][:, cols], first[:, cols], -1.0, wgs_sb[:, cols], MULT, MULT)
-        nc.gpsimd.tensor_scalar(source[0], source[5], 1.0, 1.0, MULT, ADD)
+        turned_rests(0, 1, [banks[1], banks[2], banks[3], banks[4]])
+        early_piece(0, 0, PACK)
+        early_piece(1, 0, 2)
+        early_piece(1, 2, PACK)
+        first_source(gate)
         for s in range(1, PACK):
             early_fit(s)
-        early_taken(1)
-        early_taken(2)
+        make_early_taken(1)
+        make_early_taken(2)
         for s in range(1, PACK):
             make_kept(s)
 
         def blend(s):
             make_total(s)
-            make_source(s, total[s][:])
+            make_product(s)
 
         scatter(0)
         blend(1)
-        early_taken(3)
+        make_early_taken(3)
         z_on_gpsimd(0)
         for a in range(PASSES):
             for i0 in range(0, PACK, 2):
                 round_wa(nc.scalar.copy, late_rounded[:, a, i0 : i0 + 2, :, :], a, 1, i0, i0 + 2)
 
-        turned_gates(1, 0, fit_banks)
+        turned_rests(1, 0, fit_banks)
         scatter(1)
         late_words = sb("late_words", [P, PASSES, PASS], U32)
         late_sc = sb("late_sc", [P, PASSES, PASS], U8)
         quantize(late_words[:].rearrange("p a c -> p (a c)"), late_sc[:].rearrange("p a c -> p (a c)"), late_values)
-        pieces[1] = [(a, slice(0, PASS), late_words[:, a, :], late_sc[:, a, :]) for a in range(PASSES)]
         blend(2)
         blend(3)
         for s in range(PACK, SLICES):
             make_kept(s)
         z_on_gpsimd(1)
-        for c in range(PACK):
-            turned_fit(1, c)
+        for c in range(CHUNKS):
+            late_fit(c, late_words, late_sc)
         add_one(3)
 
         scatter(2)
-        for c in range(PACK):
-            make_taken(1, c, 0)
+        for c in range(CHUNKS):
+            make_late_taken(c)
         z_on_gpsimd(2)
         scatter(3)
         for s in (4, 5, 6):
             make_total(s)
         for s in (4, 5, 6):
-            make_source(s, total[s][:])
+            make_product(s)
+            add_one(s)
         z_on_gpsimd(3)
         scatter(4)
         blend(7)
@@ -518,22 +508,19 @@ def tile_list_demand_response_baseline_kernel(
             for k, (tile, n0, count) in enumerate(held[q]):
                 copy = nc.vector.tensor_copy if (q, k) in VECTOR_LEAVES else nc.scalar.copy
                 copy(room[:, n0 : n0 + count, :], tile)
-                if q in BY_BANK:
-                    nc.sync.dma_start(out=out_view[:, n0 : n0 + count, cols], in_=room[:, n0 : n0 + count, :])
-            if q not in BY_BANK:
-                nc.sync.dma_start(out=out_view[:, :, cols], in_=room)
+                nc.sync.dma_start(out=out_view[:, n0 : n0 + count, cols], in_=room[:, n0 : n0 + count, :])
 
         scatter(LAST)
         early_words = sb("early_words", [P, T2], U32, tag="load6")
         for q in range(AHEAD):
             finish(0, q)
         last_chunk = len(chunks) - 1
-        z_on_vector(LAST, chunks[0])
-        z_on_vector(LAST, chunks[1])
+        last_z(chunks[0])
+        last_z(chunks[1])
         for q in range(len(chunks)):
             fill(q)
             if q + 2 <= last_chunk:
-                z_on_vector(LAST, chunks[q + 2])
+                last_z(chunks[q + 2])
             if AHEAD <= q + 1 <= last_chunk:
                 finish(0, q + 1)
             finish(1, q)

@@ -78,7 +78,7 @@ def tile_list_demand_response_baseline_kernel(
         late_rows = late_loads.bitcast(BF16)[:, :, 0:T2]
         late_kept = late_tile[:, (PACK - 1) * T2 :]
         load_sb = [
-            late_loads[:, s - PACK + 1, :] if PACK - 1 <= s < LAST - 1 else sb("load%d" % s, [P, T2], F32)[:]
+            late_loads[:, s - PACK + 1, :] if s in (3, 5) else sb("load%d" % s, [P, T2], F32)[:]
             for s in range(SLICES)
         ]
         wo_w = sb("wo_w", [P, PASSES, N], I32)
@@ -94,6 +94,7 @@ def tile_list_demand_response_baseline_kernel(
         for s in (6, 3, 4, 5):
             nc.gpsimd.memset(one_pages[s][:], 1.0)
         one_pages[0] = one_pages[6]
+        one_pages[7] = one_pages[3]
         clear(nc.gpsimd, wg_sc[1])
         clear(nc.gpsimd, wo_sc)
 
@@ -231,8 +232,10 @@ def tile_list_demand_response_baseline_kernel(
                     stop=(a == PASSES - 1),
                 )
             gate = sb("first_gate", [P, S], F32)
+            rest = sb("first_rest", [P, S], F32)
             nc.scalar.activation(gate[:], score[:], SIGMOID)
-            return gate
+            nc.scalar.activation(rest[:], score[:], SIGMOID, scale=-1.0)
+            return gate, rest
 
         late_room = sb("late_room", [P, PACK * S], F32)[:]
         late_values = late_room.bitcast(BF16)
@@ -256,7 +259,8 @@ def tile_list_demand_response_baseline_kernel(
             5: late_kept[:, 2 * S + S // 2 : 3 * S + S // 2],
             6: source[0],
         }
-        source[7] = product[6]
+        product[7] = load_sb[4][:, 0:S]
+        source[7] = source[4]
         total = [total_banks[s % 2] for s in range(SLICES)]
         total[6] = side_banks[0]
         total[7] = total_banks[0]
@@ -265,7 +269,7 @@ def tile_list_demand_response_baseline_kernel(
         def by_chunk(rows):
             return rows.rearrange("e (c m) -> e c m", m=P)
 
-        def first_source(gate):
+        def first_source(gate, rest):
             fit = total_banks[1]
             for a, rows, codes, scales in early_wa[0:PASSES]:
                 nc.tensor.matmul_mx(
@@ -279,13 +283,13 @@ def tile_list_demand_response_baseline_kernel(
                 )
             kept = sb("kept", [P, S], F32)
             taken = sb("taken", [P, S], F32)
-            nc.vector.scalar_tensor_tensor(kept[:], gate[:], 1.0, prior_of(0), SUB, MULT)
+            nc.vector.tensor_tensor(kept[:], rest[:], prior_of(0), MULT)
             for cols in halves:
                 nc.vector.tensor_tensor(taken[:, cols], fit[:, cols], gate[:, cols], MULT)
             for cols in halves:
-                nc.vector.tensor_tensor(taken[:, cols], kept[:, cols], taken[:, cols], SUB)
+                nc.vector.tensor_tensor(taken[:, cols], kept[:, cols], taken[:, cols], ADD)
             for cols in halves:
-                nc.vector.scalar_tensor_tensor(product[0][:, cols], taken[:, cols], -1.0, wgs_sb[:, cols], MULT, MULT)
+                nc.vector.tensor_tensor(product[0][:, cols], taken[:, cols], wgs_sb[:, cols], MULT)
             nc.gpsimd.tensor_scalar(source[0], product[0], 1.0, 1.0, MULT, ADD)
 
         def late_fit(c, words, scales):
@@ -345,9 +349,10 @@ def tile_list_demand_response_baseline_kernel(
 
         def make_product(s):
             if s == LAST:
-                moved = load_sb[3][:, S:]
+                moved = late_loads[:, 1, 0:S]
                 nc.scalar.activation(moved, total[s][:], COPY, scale=-1.0)
-                nc.gpsimd.tensor_tensor(source[s], moved, wgs_sb[:], MULT)
+                nc.gpsimd.tensor_tensor(product[s], moved, wgs_sb[:], MULT)
+                add_one(s)
             else:
                 nc.vector.scalar_tensor_tensor(product.get(s, source[s]), total[s][:], -1.0, wgs_sb[:], MULT, MULT)
 
@@ -360,9 +365,7 @@ def tile_list_demand_response_baseline_kernel(
         early_rows = early_room.bitcast(BF16).rearrange("p (q i t) -> p q i t", i=PACK, t=WEAVE)
 
         def last_z(cols):
-            nc.vector.scalar_tensor_tensor(
-                late_rows[:, LAST - PACK, cols], page_of[LAST][:, cols], 1.0, load_sb[LAST][:, cols], ADD, MULT
-            )
+            nc.vector.tensor_tensor(late_rows[:, LAST - PACK, cols], page_of[LAST][:, cols], load_sb[LAST][:, cols], MULT)
 
         factors = [page_of[s][:] for s in range(LAST)]
         factors[1] = late_prior_t[:, 0:T2]
@@ -398,12 +401,12 @@ def tile_list_demand_response_baseline_kernel(
         def weave_late(copy, q, i0, i1):
             weave(copy, late_woven[q][:], late_rows[:, :, chunks[q]], i0, i1)
 
-        gate = first_gate()
+        gate, rest = first_gate()
         turned_rests(0, 1, [banks[1], banks[2], banks[3], banks[4]])
         early_piece(0, 0, PACK)
         early_piece(1, 0, 2)
         early_piece(1, 2, PACK)
-        first_source(gate)
+        first_source(gate, rest)
         for s in range(1, PACK):
             early_fit(s)
         make_early_taken(1)
@@ -449,8 +452,8 @@ def tile_list_demand_response_baseline_kernel(
             add_one(s)
         z_on_gpsimd(3)
         scatter(4)
-        blend(7)
         z_on_gpsimd(4)
+        blend(7)
         weave_early(0)
         weave_early(1)
         scatter(5)

@@ -28,11 +28,11 @@ SLICES = H // P
 LAST = SLICES - 1
 N_TILES = N // P
 CHUNKS = S // P
-ONE_PAGE_SLICES = (3, 4, 5, 6)
+ONE_PAGE_SLICES = (3, 5, 6)
 CUTS = [0, 128, 384, 640, 896, 1024]
 AHEAD = 2
-SCALAR_FILLS = (1,)
-VECTOR_LEAVES = ((3, 0), (4, 0))
+SCALAR_FILLS = (3,)
+VECTOR_LEAVES = ((3, 1),)
 WEAVE = 256
 NEIGHBOURS = 4
 
@@ -70,17 +70,17 @@ def tile_list_demand_response_baseline_kernel(
         wa_raw = {}
         for a in range(PASSES):
             for b in range(PASSES):
-                wa_raw[a, b] = sb("wa_raw%d%d" % (a, b), [P, PACK, PASS], F32)
+                if (a, b) != (1, 1):
+                    wa_raw[a, b] = sb("wa_raw%d%d" % (a, b), [P, PACK, PASS], F32)[:]
+        last_room = sb("last_room", [P, (PACK + 1) * S], F32)[:]
+        wa_raw[1, 1] = last_room[:, S // 2 : S // 2 + PACK * S].rearrange("p (j c) -> p j c", j=PACK)
         prior_sb = [sb("prior%d" % b, [P, PACK, S], F32) for b in range(PASSES)]
-        wgs_sb = sb("wgs_sb", [P, S], F32)
-        late_tile = sb("late_tile", [P, (PACK + 1) * T2], F32)[:]
-        late_loads = late_tile[:, 0 : PACK * T2].rearrange("p (r t) -> p r t", r=PACK)
-        late_rows = late_loads.bitcast(BF16)[:, :, 0:T2]
-        late_kept = late_tile[:, (PACK - 1) * T2 :]
-        load_sb = [
-            late_loads[:, s - PACK + 1, :] if s in (3, 5) else sb("load%d" % s, [P, T2], F32)[:]
-            for s in range(SLICES)
-        ]
+        early_room = sb("early_room", [P, 2 * PACK * S], F32)[:]
+        wgs_sb = early_room[:, (PACK - 1) * S : PACK * S]
+        late_tile = sb("late_tile", [P, (2 * PACK - 1) * S], F32)[:]
+        late_rows = late_tile[:, 0 : PACK * S].bitcast(BF16).rearrange("p (r t) -> p r t", r=PACK)
+        late_kept = late_tile[:, (PACK - 1) * S :]
+        load_sb = [sb("load%d" % s, [P, T2], F32)[:] for s in range(SLICES)]
         wo_w = sb("wo_w", [P, PASSES, N], I32)
 
         def clear(engine, plane):
@@ -91,7 +91,7 @@ def tile_list_demand_response_baseline_kernel(
         make_identity(nc, ident[:])
         for page in pages:
             nc.vector.memset(page[:], 0.0)
-        for s in (6, 3, 4, 5):
+        for s in (6, 3, 5):
             nc.gpsimd.memset(one_pages[s][:], 1.0)
         one_pages[0] = one_pages[6]
         one_pages[7] = one_pages[3]
@@ -112,7 +112,7 @@ def tile_list_demand_response_baseline_kernel(
 
         def fetch_wa(b):
             for a in range(PASSES):
-                nc.sync.dma_start(out=wa_raw[a, b][:], in_=wa_view[a, b])
+                nc.sync.dma_start(out=wa_raw[a, b], in_=wa_view[a, b])
 
         def fetch_prior(b, i0, i1):
             nc.sync.dma_start(out=prior_sb[b][:, i0:i1, :], in_=prior_view[b, :, i0:i1, :])
@@ -126,7 +126,7 @@ def tile_list_demand_response_baseline_kernel(
         fetch_tab(1)
         fetch_wg(0)
         fetch_wa(0)
-        nc.sync.dma_start(out=wgs_sb[:], in_=wgs)
+        nc.sync.dma_start(out=wgs_sb, in_=wgs)
         fetch_prior(0, 0, 1)
         nc.sync.dma_start(idx2[:], offs2)
         fetch_prior(0, 1, PACK)
@@ -164,7 +164,7 @@ def tile_list_demand_response_baseline_kernel(
         def round_wa(copy, rounded, a, b, i0, i1):
             copy(
                 out=rounded.rearrange("p i m j -> p m j i"),
-                in_=wa_raw[a, b][:].rearrange("p j (m i) -> p m j i", i=PACK)[:, :, :, i0:i1],
+                in_=wa_raw[a, b].rearrange("p j (m i) -> p m j i", i=PACK)[:, :, :, i0:i1],
             )
 
         def quantize(words, scales, values):
@@ -181,7 +181,7 @@ def tile_list_demand_response_baseline_kernel(
         rest_t = {}
 
         def turned_rests(b, first, scores):
-            rest_t[b] = wa_raw[1, 1] if b else sb("rest_t0", [P, PACK, S], F32)
+            rest_t[b] = last_room[:, 0 : PACK * S].rearrange("p (c m) -> p c m", c=CHUNKS) if b else sb("rest_t0", [P, PACK, S], F32)
             for c in range(CHUNKS):
                 score = scores[c]
                 cols = slice(c * P, (c + 1) * P)
@@ -237,33 +237,33 @@ def tile_list_demand_response_baseline_kernel(
             nc.scalar.activation(rest[:], score[:], SIGMOID, scale=-1.0)
             return gate, rest
 
-        late_room = sb("late_room", [P, PACK * S], F32)[:]
+        late_room = early_room[:, PACK * S :]
         late_values = late_room.bitcast(BF16)
         late_rounded = late_values.rearrange("p (a i m j) -> p a i m j", a=PASSES, i=PACK, j=PACK)
-        early_taken = sb("early_taken", [P, 2 * S], F32, tag="tab_w1")
-        taken_t = {1: early_taken[:, 0:S], 2: early_taken[:, S:], 3: early_taken[:, 0:S]}
-        late_taken_t = wa_raw[0, 1]
-        late_prior_t = sb("late_prior_t", [P, (PACK + 1) * S], F32, tag="tab_w0")
+        early_taken = sb("early_taken", [P, 5 * S // 2], F32, tag="tab_w1")
+        taken_t = {1: early_taken[:, 0:S], 2: early_taken[:, S : 2 * S], 3: early_taken[:, 0:S]}
+        third_taken = [early_taken[:, 2 * S :], early_taken[:, S // 2 : S]]
+        late_prior_t = sb("late_prior_t", [P, PACK * S], F32, tag="tab_w0")
         prior_t = [wa_raw[0, 0][:, s, :] for s in range(PACK)]
-        prior_t += [late_prior_t[:, place * S : (place + 1) * S] for place in (2, 3, 1, 4)]
+        prior_t += [late_prior_t[:, place * S : (place + 1) * S] for place in range(PACK)]
         kept_t = [wa_raw[1, 0][:, s, :] for s in range(PACK)]
-        kept_t += [late_kept[:, place * S : (place + 1) * S] for place in (3, 1, 2, 0)]
+        kept_room = prior_sb[0][:].rearrange("p i j -> p (i j)")
+        kept_t += [kept_room[:, place * S : (place + 1) * S] for place in (3, 0, 1, 2)]
         source = {s: sb("source%d" % s, [P, S], F32)[:] for s in (0, 1, 5, 6)}
-        source[2] = late_room[:, 3 * S : 4 * S]
-        source[3] = prior_t[7]
-        source[4] = source[1]
+        source[2] = last_room[:, PACK * S :]
+        source[4] = kept_room[:, S // 2 : S + S // 2]
         product = {
             0: source[5],
             3: late_room[:, 0:S],
-            4: late_kept[:, S + S // 2 : 2 * S + S // 2],
-            5: late_kept[:, 2 * S + S // 2 : 3 * S + S // 2],
-            6: source[0],
+            5: kept_room[:, S + S // 2 : 2 * S + S // 2],
+            6: prior_t[0],
+            7: prior_t[1],
         }
-        product[7] = load_sb[4][:, 0:S]
-        source[7] = source[4]
+        last_moved = late_tile[:, S // 2 : 5 * S // 2]
+        source[7] = source[1]
         total = [total_banks[s % 2] for s in range(SLICES)]
         total[6] = side_banks[0]
-        total[7] = total_banks[0]
+        total[7] = side_banks[1]
         halves = [slice(0, S // 2), slice(S // 2, S)]
 
         def by_chunk(rows):
@@ -325,6 +325,17 @@ def tile_list_demand_response_baseline_kernel(
             rest = rest_t[0][:, :, s * P : (s + 1) * P]
             nc.vector.scalar_tensor_tensor(by_chunk(taken_t[s]), rest, 1.0, by_chunk(fit_banks[s - 1][:]), SUB, MULT)
 
+        def make_third_taken(half):
+            chunk_pair = slice(2 * half, 2 * half + 2)
+            nc.vector.scalar_tensor_tensor(
+                by_chunk(third_taken[half]),
+                rest_t[0][:, chunk_pair, 3 * P :],
+                1.0,
+                by_chunk(fit_banks[2][:])[:, chunk_pair, :],
+                SUB,
+                MULT,
+            )
+
         def make_late_taken(c):
             nc.vector.scalar_tensor_tensor(late_taken_t[:, c, :], rest_t[1][:, c, :], 1.0, fit_banks[c][:], SUB, MULT)
 
@@ -333,13 +344,23 @@ def tile_list_demand_response_baseline_kernel(
             turned = fit_banks[i] if b else side_banks[s % 2]
             turn_into(turned, quarters(prior_of(s)), True, True)
             nc.scalar.activation(prior_t[s], turned[:], COPY, scale=-1.0)
-            nc.gpsimd.tensor_tensor(by_chunk(kept_t[s]), rest_t[b][:, :, i * P : (i + 1) * P], by_chunk(prior_t[s]), MULT)
+            if s < 6:
+                nc.gpsimd.tensor_tensor(by_chunk(kept_t[s]), rest_t[b][:, :, i * P : (i + 1) * P], by_chunk(prior_t[s]), MULT)
+            if s == LAST:
+                nc.gpsimd.tensor_tensor(
+                    kept_room[:, S : 3 * S].rearrange("e (i c m) -> e i c m", i=2, m=P),
+                    rest_t[1][:, :, 2 * P :].rearrange("e c (i m) -> e i c m", i=2),
+                    late_prior_t[:, 2 * S :].rearrange("e (i c m) -> e i c m", i=2, m=P),
+                    MULT,
+                )
 
         def make_total(s):
             b, i = divmod(s, PACK)
             taken = [late_taken_t[:, c, i * P : (i + 1) * P] for c in range(CHUNKS)] if b else quarters(taken_t[s])
+            if s == 3:
+                taken = [half[:, c * P : (c + 1) * P] for half in third_taken for c in range(2)]
             parts = [quarters(kept_t[s]), taken]
-            if s == 6:
+            if s == LAST:
                 parts = parts[::-1]
             turn_into(total[s], parts[0], True, False)
             turn_into(total[s], parts[1], False, True)
@@ -348,42 +369,39 @@ def tile_list_demand_response_baseline_kernel(
             nc.scalar.activation(source[s], product[s], COPY, bias=1.0)
 
         def make_product(s):
-            if s == LAST:
-                moved = late_loads[:, 1, 0:S]
-                nc.scalar.activation(moved, total[s][:], COPY, scale=-1.0)
-                nc.gpsimd.tensor_tensor(product[s], moved, wgs_sb[:], MULT)
-                add_one(s)
-            else:
-                nc.vector.scalar_tensor_tensor(product.get(s, source[s]), total[s][:], -1.0, wgs_sb[:], MULT, MULT)
+            nc.vector.scalar_tensor_tensor(product[s] if s in product else source[s], total[s][:], -1.0, wgs_sb, MULT, MULT)
 
-        page_of = [one_pages.get(s, pages[s % 2]) for s in range(SLICES)]
+        def last_products():
+            for s in (6, 7):
+                nc.scalar.activation(last_moved[:, (s - 6) * S : (s - 5) * S], total[s][:], COPY, scale=-1.0)
+            nc.gpsimd.tensor_tensor(
+                wa_raw[0, 0][:, 0:2, :],
+                last_moved.rearrange("p (i j) -> p i j", i=2),
+                wgs_sb.unsqueeze(1).to_broadcast([P, 2, S]),
+                MULT,
+            )
+
+        page_of = [one_pages.get(s, pages[s % 2 if s < PACK else 1]) for s in range(SLICES)]
 
         def scatter(s):
             nc.vector.tensor_copy(page_of[s][:].indirect(idx2[:]), source[s])
 
-        early_room = sb("early_room", [P, 2 * T2], F32)[:]
-        early_rows = early_room.bitcast(BF16).rearrange("p (q i t) -> p q i t", i=PACK, t=WEAVE)
+        early_rows = early_room[:, 0 : PACK * S].bitcast(BF16).rearrange("p (i t) -> p i t", i=PACK)
 
         def last_z(cols):
             nc.vector.tensor_tensor(late_rows[:, LAST - PACK, cols], page_of[LAST][:, cols], load_sb[LAST][:, cols], MULT)
 
         factors = [page_of[s][:] for s in range(LAST)]
-        factors[1] = late_prior_t[:, 0:T2]
+        factors[1] = prior_sb[1][:].rearrange("p i j -> p (i j)")[:, T2:]
         factors[2] = late_room[:, 0:T2]
+        factors[4] = kept_room[:, T2:]
 
         def z_on_gpsimd(s):
-            if s in (1, 2):
+            if s in (1, 2, 4):
                 nc.scalar.activation(factors[s], page_of[s][:], COPY, bias=1.0)
-            if s < PACK:
-                for q in [slice(0, 2), slice(2, 4)] if s == 0 else [slice(0, 4)]:
-                    nc.gpsimd.tensor_tensor(
-                        early_rows[:, q, s, :],
-                        factors[s].rearrange("p (q t) -> p q t", t=WEAVE)[:, q, :],
-                        load_sb[s].rearrange("p (q t) -> p q t", t=WEAVE)[:, q, :],
-                        MULT,
-                    )
-            else:
-                nc.gpsimd.tensor_tensor(late_rows[:, s - PACK, :], factors[s], load_sb[s], MULT)
+            rows = early_rows if s < PACK else late_rows
+            for cols in [slice(0, S), slice(S, T2)] if s == 0 else [slice(0, T2)]:
+                nc.gpsimd.tensor_tensor(rows[:, s % PACK, cols], factors[s][:, cols], load_sb[s][:, cols], MULT)
 
         chunks = [slice(c0, c1) for c0, c1 in zip(CUTS, CUTS[1:])]
         early_woven = late_kept.bitcast(BF16).rearrange("p (t i) -> p t i", i=PACK)
@@ -396,7 +414,7 @@ def tile_list_demand_response_baseline_kernel(
             )
 
         def weave_early(piece):
-            weave(nc.scalar.copy, early_woven[:, piece * WEAVE : (piece + 1) * WEAVE, :], early_rows[:, piece, :, :], 0, PACK)
+            weave(nc.scalar.copy, early_woven[:, piece * WEAVE : (piece + 1) * WEAVE, :], early_rows[:, :, piece * WEAVE : (piece + 1) * WEAVE], 0, PACK)
 
         def weave_late(copy, q, i0, i1):
             weave(copy, late_woven[q][:], late_rows[:, :, chunks[q]], i0, i1)
@@ -411,6 +429,7 @@ def tile_list_demand_response_baseline_kernel(
             early_fit(s)
         make_early_taken(1)
         make_early_taken(2)
+        make_third_taken(0)
         for s in range(1, PACK):
             make_kept(s)
 
@@ -420,7 +439,7 @@ def tile_list_demand_response_baseline_kernel(
 
         scatter(0)
         blend(1)
-        make_early_taken(3)
+        make_third_taken(1)
         z_on_gpsimd(0)
         for a in range(PASSES):
             for i0 in range(0, PACK, 2):
@@ -438,22 +457,33 @@ def tile_list_demand_response_baseline_kernel(
         z_on_gpsimd(1)
         for c in range(CHUNKS):
             late_fit(c, late_words, late_sc)
-        add_one(3)
+        taken_room = sb("taken_room", [P, (PACK + 1) * S], F32, tag="late_words")[:]
+        late_taken_t = taken_room[:, S:].rearrange("p (c m) -> p c m", c=CHUNKS)
+        source[3] = taken_room[:, P // 2 : P // 2 + S]
 
         scatter(2)
         for c in range(CHUNKS):
             make_late_taken(c)
+            for s in range(PACK, SLICES):
+                cols = slice((s - PACK) * P, (s - PACK + 1) * P)
+                nc.tensor.matmul(
+                    total[s][:, c * P : (c + 1) * P], late_taken_t[:, c, cols], ident[:], is_transpose=True, start=(c == 0), stop=False
+                )
+            if c == 0:
+                add_one(3)
         z_on_gpsimd(2)
         scatter(3)
-        for s in (4, 5, 6):
-            make_total(s)
-        for s in (4, 5, 6):
-            make_product(s)
-            add_one(s)
+        for s in range(PACK, SLICES):
+            turn_into(total[s], quarters(kept_t[s]), False, True)
+        last_products()
+        make_product(4)
+        make_product(5)
+        add_one(5)
         z_on_gpsimd(3)
+        add_one(6)
+        add_one(7)
         scatter(4)
         z_on_gpsimd(4)
-        blend(7)
         weave_early(0)
         weave_early(1)
         scatter(5)
@@ -471,8 +501,8 @@ def tile_list_demand_response_baseline_kernel(
             width = cols.stop - cols.start
             per_bank = min(N_TILES, S // width)
             held[q] = []
-            for n0 in range(0, N_TILES, per_bank):
-                count = min(per_bank, N_TILES - n0)
+            first = N_TILES % per_bank or per_bank
+            for n0, count in [(0, first)] + [(n0, per_bank) for n0 in range(first, N_TILES, per_bank)]:
                 tile = free_banks.pop(0)[:, 0 : count * width].rearrange("p (n t) -> p n t", n=count)
                 held[q].append((tile, n0, count))
 
@@ -498,7 +528,8 @@ def tile_list_demand_response_baseline_kernel(
 
         def finish(b, q):
             width = chunks[q].stop - chunks[q].start
-            words = sb("late_z_words%d" % q, [P, width], U32)[:] if b else early_words[:, chunks[q]]
+            tag = "late_woven%d" % (q - 1) if q == len(chunks) - 1 else None
+            words = sb("late_z_words%d" % q, [P, width], U32, tag=tag)[:] if b else early_words[:, chunks[q]]
             scales = sb("z_sc%d%d" % (b, q), [P, width], U8)
             woven = late_woven[q][:] if b else early_woven[:, chunks[q], :]
             quantize(words, scales[:], woven.rearrange("p t i -> p (t i)"))
@@ -517,15 +548,23 @@ def tile_list_demand_response_baseline_kernel(
         early_words = sb("early_words", [P, T2], U32, tag="load6")
         for q in range(AHEAD):
             finish(0, q)
-        last_chunk = len(chunks) - 1
         last_z(chunks[0])
         last_z(chunks[1])
-        for q in range(len(chunks)):
-            fill(q)
-            if q + 2 <= last_chunk:
-                last_z(chunks[q + 2])
-            if AHEAD <= q + 1 <= last_chunk:
-                finish(0, q + 1)
-            finish(1, q)
+        fill(0)
+        last_z(chunks[3])
+        fill(3)
+        finish(1, 0)
+        fill(1)
+        last_z(chunks[2])
+        finish(1, 1)
+        finish(0, 2)
+        fill(2)
+        last_z(chunks[4])
+        finish(1, 2)
+        finish(0, 3)
+        fill(4)
+        finish(1, 3)
+        finish(0, 4)
+        finish(1, 4)
         for q in range(len(chunks)):
             leave(q)

@@ -120,8 +120,8 @@ def tile_list_demand_response_baseline_kernel(
         def fetch_load(s):
             nc.sync.dma_start(out=load_sb[s], in_=load_view[s // PACK, s % PACK])
 
-        nc.sync.dma_start(idx[:], offs)
         fetch_tab(0)
+        nc.sync.dma_start(idx[:], offs)
         load_scale_rows(nc, tab_sc, tab_scales, 0, T)
         fetch_tab(1)
         fetch_wg(0)
@@ -365,8 +365,8 @@ def tile_list_demand_response_baseline_kernel(
             turn_into(total[s], parts[0], True, False)
             turn_into(total[s], parts[1], False, True)
 
-        def add_one(s):
-            nc.scalar.activation(source[s], product[s], COPY, bias=1.0)
+        def add_one(s, cols=slice(0, S)):
+            nc.scalar.activation(source[s][:, cols], product[s][:, cols], COPY, bias=1.0)
 
         def make_product(s):
             nc.vector.scalar_tensor_tensor(product[s] if s in product else source[s], total[s][:], -1.0, wgs_sb, MULT, MULT)
@@ -460,6 +460,7 @@ def tile_list_demand_response_baseline_kernel(
         taken_room = sb("taken_room", [P, (PACK + 1) * S], F32, tag="late_words")[:]
         late_taken_t = taken_room[:, S:].rearrange("p (c m) -> p c m", c=CHUNKS)
         source[3] = taken_room[:, P // 2 : P // 2 + S]
+        add_one(3, slice(0, S - P // 2))
 
         scatter(2)
         for c in range(CHUNKS):
@@ -470,7 +471,7 @@ def tile_list_demand_response_baseline_kernel(
                     total[s][:, c * P : (c + 1) * P], late_taken_t[:, c, cols], ident[:], is_transpose=True, start=(c == 0), stop=False
                 )
             if c == 0:
-                add_one(3)
+                add_one(3, slice(S - P // 2, S))
         z_on_gpsimd(2)
         scatter(3)
         for s in range(PACK, SLICES):

@@ -457,7 +457,7 @@ def tile_list_demand_response_baseline_kernel(
         z_on_gpsimd(1)
         for c in range(CHUNKS):
             late_fit(c, late_words, late_sc)
-        taken_room = sb("taken_room", [P, (PACK + 1) * S], F32, tag="late_words")[:]
+        taken_room = sb("taken_room", [P, (PACK + 1) * S], F32, tag="wa_raw01")[:]
         late_taken_t = taken_room[:, S:].rearrange("p (c m) -> p c m", c=CHUNKS)
         source[3] = taken_room[:, P // 2 : P // 2 + S]
         add_one(3, slice(0, S - P // 2))

from contextlib import ExitStack

import concourse.mybir as mybir
from concourse.masks import make_identity

K, T, S, H, T2, N = 1024, 2048, 512, 1024, 1024, 384
FLOPS = 2 * (2 * K * H * S + H * N * T2)

F32 = mybir.dt.float32
BF16 = mybir.dt.bfloat16
I32 = mybir.dt.int32
U32 = mybir.dt.uint32
U16 = mybir.dt.uint16
U8 = mybir.dt.uint8
FP8X4 = mybir.dt.float8_e4m3fn_x4
FP4X4 = mybir.dt.float4_e2m1fn_x4
ADD = mybir.AluOpType.add
SUB = mybir.AluOpType.subtract
MULT = mybir.AluOpType.mult
SIGMOID = mybir.ActivationFunctionType.Sigmoid
COPY = mybir.ActivationFunctionType.Copy

P = 128
PACK = 4
PASS = P * PACK
PASSES = 2
SLICES = H // P
LAST = SLICES - 1
N_TILES = N // P
CHUNKS = S // P
ONE_PAGE_SLICES = (3, 5, 6)
CUTS = [0, 128, 384, 640, 896, 1024]
AHEAD = 2
SCALAR_FILLS = (3,)
VECTOR_LEAVES = ((3, 1),)
WEAVE = 256
NEIGHBOURS = 4


def load_scale_rows(nc, plane, scales, c0, c1):
    rows = scales.bitcast(I32).rearrange("a (q r) c -> r q a c", r=4)
    for r in range(4):
        nc.sync.dma_start(out=plane[r:P:32, :, :].bitcast(I32), in_=rows[r, :, :, c0 // 4 : c1 // 4])


def tile_list_demand_response_baseline_kernel(
    tc, tab_words, tab_scales, offs, wa, wg_words, wg_scales, prior, wgs, offs2, load, wo_words, wo_scales, out
):
    nc = tc.nc
    with ExitStack() as ctx:
        keep = ctx.enter_context(tc.tile_pool(name="keep", bufs=1))
        psum = ctx.enter_context(tc.psum_pool(name="psum", bufs=1))

        def sb(name, shape, dtype, tag=None):
            return keep.tile(shape, dtype, name=name, tag=tag or name, align_bytes=64)

        banks = [psum.tile([P, S], F32, name="bank%d" % n) for n in range(8)]
        fit_banks, total_banks, side_banks = banks[0:4], banks[4:6], banks[6:8]

        idx = keep.tile([P, S // 16], U16, name="idx")
        idx2 = keep.tile([P, S // 16], U16, name="idx2")
        tab_sc = sb("tab_sc", [P, PASSES, T], U8)
        wg_sc = [sb("wg_sc%d" % b, [P, PASSES, PASS], U8) for b in range(PASSES)]
        wo_sc = sb("wo_sc", [P, PASSES, N], U8)
        wg_w = [sb("wg_w%d" % b, [P, PASSES, 2 * PASS], U8) for b in range(PASSES)]
        tab_w = [sb("tab_w%d" % a, [P, T], I32) for a in range(PASSES)]
        pages = [sb("page%d" % n, [P, T2], F32) for n in range(2)]
        one_pages = {s: sb("one_page%d" % s, [P, T2], F32) for s in ONE_PAGE_SLICES}
        ident = sb("ident", [P, P], F32)
        wa_raw = {}
        for a in range(PASSES):
            for b in range(PASSES):
                if (a, b) != (1, 1):
                    wa_raw[a, b] = sb("wa_raw%d%d" % (a, b), [P, PACK, PASS], F32)[:]
        last_room = sb("last_room", [P, (PACK + 1) * S], F32)[:]
        wa_raw[1, 1] = last_room[:, S // 2 : S // 2 + PACK * S].rearrange("p (j c) -> p j c", j=PACK)
        prior_sb = [sb("prior%d" % b, [P, PACK, S], F32) for b in range(PASSES)]
        early_room = sb("early_room", [P, 2 * PACK * S], F32)[:]
        wgs_sb = early_room[:, (PACK - 1) * S : PACK * S]
        late_tile = sb("late_tile", [P, (2 * PACK - 1) * S], F32)[:]
        late_rows = late_tile[:, 0 : PACK * S].bitcast(BF16).rearrange("p (r t) -> p r t", r=PACK)
        late_kept = late_tile[:, (PACK - 1) * S :]
        load_sb = [sb("load%d" % s, [P, T2], F32)[:] for s in range(SLICES)]
        wo_w = sb("wo_w", [P, PASSES, N], I32)

        def clear(engine, plane):
            engine.memset(plane[:].rearrange("p a c -> p (a c)").bitcast(I32), 0)

        clear(nc.vector, tab_sc)
        clear(nc.vector, wg_sc[0])
        make_identity(nc, ident[:])
        for page in pages:
            nc.vector.memset(page[:], 0.0)
        for s in (6, 3, 5):
            nc.gpsimd.memset(one_pages[s][:], 1.0)
        one_pages[0] = one_pages[6]
        one_pages[7] = one_pages[3]
        clear(nc.gpsimd, wg_sc[1])
        clear(nc.gpsimd, wo_sc)

        wa_view = wa.rearrange("(a p j) (b c) -> a b p j c", a=PASSES, j=PACK, b=PASSES)
        prior_view = prior.rearrange("(b p i) j -> b p i j", b=PASSES, i=PACK)
        load_view = load.rearrange("(b p i) t -> b i p t", b=PASSES, i=PACK)

        def fetch_tab(a):
            nc.sync.dma_start(out=tab_w[a][:], in_=tab_words[a].rearrange("p t i -> p (t i)").bitcast(I32))

        def fetch_wg(b):
            words = wg_words.bitcast(I32).rearrange("a p (b c) -> b p a c", b=PASSES)
            nc.sync.dma_start(out=wg_w[b][:].bitcast(I32), in_=words[b])
            load_scale_rows(nc, wg_sc[b], wg_scales, b * PASS, (b + 1) * PASS)

        def fetch_wa(b):
            for a in range(PASSES):
                nc.sync.dma_start(out=wa_raw[a, b], in_=wa_view[a, b])

        def fetch_prior(b, i0, i1):
            nc.sync.dma_start(out=prior_sb[b][:, i0:i1, :], in_=prior_view[b, :, i0:i1, :])

        def fetch_load(s):
            nc.sync.dma_start(out=load_sb[s], in_=load_view[s // PACK, s % PACK])

        fetch_tab(0)
        nc.sync.dma_start(idx[:], offs)
        load_scale_rows(nc, tab_sc, tab_scales, 0, T)
        fetch_tab(1)
        fetch_wg(0)
        fetch_wa(0)
        nc.sync.dma_start(out=wgs_sb, in_=wgs)
        fetch_prior(0, 0, 1)
        nc.sync.dma_start(idx2[:], offs2)
        fetch_prior(0, 1, PACK)
        fetch_wg(1)
        fetch_wa(1)
        for cols in (slice(0, T2 // 2), slice(T2 // 2, T2)):
            nc.sync.dma_start(out=load_sb[0][:, cols], in_=load_view[0, 0][:, cols])
        fetch_prior(1, 0, PACK)
        for s in range(1, SLICES):
            fetch_load(s)
        nc.sync.dma_start(
            out=wo_w[:], in_=wo_words.rearrange("a p c i -> a p (c i)").bitcast(I32).rearrange("a p c -> p a c")
        )
        load_scale_rows(nc, wo_sc, wo_scales, 0, N)

        v_w = [sb("v_w%d" % a, [P, S], U32) for a in range(PASSES)]
        v_sc = [sb("v_sc%d" % a, [P, S], U8) for a in range(PASSES)]
        nc.vector.tensor_copy(v_w[0][:], tab_w[0][:].bitcast(U32).indirect(idx[:]))
        for a in range(PASSES):
            nc.vector.tensor_copy(v_sc[a][:], tab_sc[:, a, :].indirect(idx[:]))
        nc.vector.tensor_copy(v_w[1][:], tab_w[1][:].bitcast(U32).indirect(idx[:]))

        first_wg_w = sb("first_wg_w", [P, PASSES, 1, 2 * P], U8)
        first_wg_sc = sb("first_wg_sc", [P, PASSES, 1, P], U8)
        nc.vector.tensor_copy(
            out=first_wg_w[:].bitcast(U16),
            in_=wg_w[0][:].bitcast(U16).rearrange("p a (m i) -> p a i m", i=PACK)[:, :, 0:1, :],
        )
        nc.vector.tensor_copy(
            out=first_wg_sc[:], in_=wg_sc[0][:].rearrange("p a (m i) -> p a i m", i=PACK)[:, :, 0:1, :]
        )

        early_wa = []

        def round_wa(copy, rounded, a, b, i0, i1):
            copy(
                out=rounded.rearrange("p i m j -> p m j i"),
                in_=wa_raw[a, b].rearrange("p j (m i) -> p m j i", i=PACK)[:, :, :, i0:i1],
            )

        def quantize(words, scales, values):
            nc.vector.quantize_mx(out=words.bitcast(FP8X4), scales=scales, in_=values)

        def early_piece(a, i0, i1):
            rounded = sb("wa_rounded%d0%d" % (a, i0), [P, i1 - i0, P, PACK], BF16)[:]
            round_wa(nc.vector.tensor_copy, rounded, a, 0, i0, i1)
            codes = sb("wa_w%d0%d" % (a, i0), [P, (i1 - i0) * P], U32)[:]
            scales = sb("wa_sc%d0%d" % (a, i0), [P, (i1 - i0) * P], U8)[:]
            quantize(codes, scales, rounded.rearrange("p i m j -> p (i m j)"))
            early_wa.append((a, slice(i0 * P, i1 * P), codes, scales))

        rest_t = {}

        def turned_rests(b, first, scores):
            rest_t[b] = last_room[:, 0 : PACK * S].rearrange("p (c m) -> p c m", c=CHUNKS) if b else sb("rest_t0", [P, PACK, S], F32)
            for c in range(CHUNKS):
                score = scores[c]
                cols = slice(c * P, (c + 1) * P)
                for a in range(PASSES):
                    nc.tensor.matmul_mx(
                        out=score[:],
                        lhsT=v_w[a][:, cols].bitcast(FP8X4),
                        lhsT_scale=v_sc[a][:, cols],
                        rhs=wg_w[b][:, a, :].bitcast(FP4X4),
                        rhs_scale=wg_sc[b][:, a, :],
                        start=(a == 0),
                        stop=(a == PASSES - 1),
                    )
                nc.scalar.activation(
                    rest_t[b][:, c, first * P :].rearrange("e (i m) -> e i m", m=P),
                    score[:].rearrange("e (m i) -> e i m", i=PACK)[:, first:PACK, :],
                    SIGMOID,
                    scale=-1.0,
                )

        def prior_of(s):
            return prior_sb[s // PACK][:, s % PACK, :]

        def quarters(src):
            return [src[:, c * P : (c + 1) * P] for c in range(CHUNKS)]

        def turn_into(target, parts, start, stop):
            for c, part in enumerate(parts):
                nc.tensor.matmul(
                    target[:, c * P : (c + 1) * P],
                    part,
                    ident[:],
                    is_transpose=True,
                    start=(start and c == 0),
                    stop=(stop and c == CHUNKS - 1),
                )

        def first_gate():
            score = banks[0]
            for a in range(PASSES):
                nc.tensor.matmul_mx(
                    out=score[:],
                    lhsT=first_wg_w[:, a, 0, :].bitcast(FP4X4),
                    lhsT_scale=first_wg_sc[:, a, 0, :],
                    rhs=v_w[a][:].bitcast(FP8X4),
                    rhs_scale=v_sc[a][:],
                    start=(a == 0),
                    stop=(a == PASSES - 1),
                )
            gate = sb("first_gate", [P, S], F32)
            rest = sb("first_rest", [P, S], F32)
            nc.scalar.activation(gate[:], score[:], SIGMOID)
            nc.scalar.activation(rest[:], score[:], SIGMOID, scale=-1.0)
            return gate, rest

        late_room = early_room[:, PACK * S :]
        late_values = late_room.bitcast(BF16)
        late_rounded = late_values.rearrange("p (a i m j) -> p a i m j", a=PASSES, i=PACK, j=PACK)
        early_taken = sb("early_taken", [P, 5 * S // 2], F32, tag="tab_w1")
        taken_t = {1: early_taken[:, 0:S], 2: early_taken[:, S : 2 * S], 3: early_taken[:, 0:S]}
        third_taken = [early_taken[:, 2 * S :], early_taken[:, S // 2 : S]]
        late_prior_t = sb("late_prior_t", [P, PACK * S], F32, tag="tab_w0")
        prior_t = [wa_raw[0, 0][:, s, :] for s in range(PACK)]
        prior_t += [late_prior_t[:, place * S : (place + 1) * S] for place in range(PACK)]
        kept_t = [wa_raw[1, 0][:, s, :] for s in range(PACK)]
        kept_room = prior_sb[0][:].rearrange("p i j -> p (i j)")
        kept_t += [kept_room[:, place * S : (place + 1) * S] for place in (3, 0, 1, 2)]
        source = {s: sb("source%d" % s, [P, S], F32)[:] for s in (0, 1, 5, 6)}
        source[2] = last_room[:, PACK * S :]
        source[4] = kept_room[:, S // 2 : S + S // 2]
        product = {
            0: source[5],
            3: late_room[:, 0:S],
            5: kept_room[:, S + S // 2 : 2 * S + S // 2],
            6: prior_t[0],
            7: prior_t[1],
        }
        last_moved = late_tile[:, S // 2 : 5 * S // 2]
        source[7] = source[1]
        total = [total_banks[s % 2] for s in range(SLICES)]
        total[6] = side_banks[0]
        total[7] = side_banks[1]
        halves = [slice(0, S // 2), slice(S // 2, S)]

        def by_chunk(rows):
            return rows.rearrange("e (c m) -> e c m", m=P)

        def first_source(gate, rest):
            fit = total_banks[1]
            for a, rows, codes, scales in early_wa[0:PASSES]:
                nc.tensor.matmul_mx(
                    out=fit[:],
                    lhsT=codes[:, 0:P].bitcast(FP8X4),
                    lhsT_scale=scales[:, 0:P],
                    rhs=v_w[a][:].bitcast(FP8X4),
                    rhs_scale=v_sc[a][:],
                    start=(a == 0),
                    stop=(a == PASSES - 1),
                )
            kept = sb("kept", [P, S], F32)
            taken = sb("taken", [P, S], F32)
            nc.vector.tensor_tensor(kept[:], rest[:], prior_of(0), MULT)
            for cols in halves:
                nc.vector.tensor_tensor(taken[:, cols], fit[:, cols], gate[:, cols], MULT)
            for cols in halves:
                nc.vector.tensor_tensor(taken[:, cols], kept[:, cols], taken[:, cols], ADD)
            for cols in halves:
                nc.vector.tensor_tensor(product[0][:, cols], taken[:, cols], wgs_sb[:, cols], MULT)
            nc.gpsimd.tensor_scalar(source[0], product[0], 1.0, 1.0, MULT, ADD)

        def late_fit(c, words, scales):
            cols = slice(c * P, (c + 1) * P)
            for a in range(PASSES):
                nc.tensor.matmul_mx(
                    out=fit_banks[c][:],
                    lhsT=v_w[a][:, cols].bitcast(FP8X4),
                    lhsT_scale=v_sc[a][:, cols],
                    rhs=words[:, a, :].bitcast(FP8X4),
                    rhs_scale=scales[:, a, :],
                    start=(a == 0),
                    stop=(a == PASSES - 1),
                )

        def early_fit(s):
            for a, rows, codes, scales in early_wa:
                if rows.start <= s * P < rows.stop:
                    mine = slice(s * P - rows.start, (s + 1) * P - rows.start)
                    for c in range(CHUNKS):
                        cols = slice(c * P, (c + 1) * P)
                        nc.tensor.matmul_mx(
                            out=fit_banks[s - 1][:, cols],
                            lhsT=v_w[a][:, cols].bitcast(FP8X4),
                            lhsT_scale=v_sc[a][:, cols],
                            rhs=codes[:, mine].bitcast(FP8X4),
                            rhs_scale=scales[:, mine],
                            start=(a == 0 and c == 0),
                            stop=(a == PASSES - 1 and c == CHUNKS - 1),
                        )

        def make_early_taken(s):
            rest = rest_t[0][:, :, s * P : (s + 1) * P]
            nc.vector.scalar_tensor_tensor(by_chunk(taken_t[s]), rest, 1.0, by_chunk(fit_banks[s - 1][:]), SUB, MULT)

        def make_third_taken(half):
            chunk_pair = slice(2 * half, 2 * half + 2)
            nc.vector.scalar_tensor_tensor(
                by_chunk(third_taken[half]),
                rest_t[0][:, chunk_pair, 3 * P :],
                1.0,
                by_chunk(fit_banks[2][:])[:, chunk_pair, :],
                SUB,
                MULT,
            )

        def make_late_taken(c):
            nc.vector.scalar_tensor_tensor(late_taken_t[:, c, :], rest_t[1][:, c, :], 1.0, fit_banks[c][:], SUB, MULT)

        def make_kept(s):
            b, i = divmod(s, PACK)
            turned = fit_banks[i] if b else side_banks[s % 2]
            turn_into(turned, quarters(prior_of(s)), True, True)
            nc.scalar.activation(prior_t[s], turned[:], COPY, scale=-1.0)
            if s < 6:
                nc.gpsimd.tensor_tensor(by_chunk(kept_t[s]), rest_t[b][:, :, i * P : (i + 1) * P], by_chunk(prior_t[s]), MULT)
            if s == LAST:
                nc.gpsimd.tensor_tensor(
                    kept_room[:, S : 3 * S].rearrange("e (i c m) -> e i c m", i=2, m=P),
                    rest_t[1][:, :, 2 * P :].rearrange("e c (i m) -> e i c m", i=2),
                    late_prior_t[:, 2 * S :].rearrange("e (i c m) -> e i c m", i=2, m=P),
                    MULT,
                )

        def make_total(s):
            b, i = divmod(s, PACK)
            taken = [late_taken_t[:, c, i * P : (i + 1) * P] for c in range(CHUNKS)] if b else quarters(taken_t[s])
            if s == 3:
                taken = [half[:, c * P : (c + 1) * P] for half in third_taken for c in range(2)]
            parts = [quarters(kept_t[s]), taken]
            if s == LAST:
                parts = parts[::-1]
            turn_into(total[s], parts[0], True, False)
            turn_into(total[s], parts[1], False, True)

        def add_one(s, cols=slice(0, S)):
            nc.scalar.activation(source[s][:, cols], product[s][:, cols], COPY, bias=1.0)

        def make_product(s):
            nc.vector.scalar_tensor_tensor(product[s] if s in product else source[s], total[s][:], -1.0, wgs_sb, MULT, MULT)

        def last_products():
            for s in (6, 7):
                nc.scalar.activation(last_moved[:, (s - 6) * S : (s - 5) * S], total[s][:], COPY, scale=-1.0)
            nc.gpsimd.tensor_tensor(
                wa_raw[0, 0][:, 0:2, :],
                last_moved.rearrange("p (i j) -> p i j", i=2),
                wgs_sb.unsqueeze(1).to_broadcast([P, 2, S]),
                MULT,
            )

        page_of = [one_pages.get(s, pages[s % 2 if s < PACK else 1]) for s in range(SLICES)]

        def scatter(s):
            nc.vector.tensor_copy(page_of[s][:].indirect(idx2[:]), source[s])

        early_rows = early_room[:, 0 : PACK * S].bitcast(BF16).rearrange("p (i t) -> p i t", i=PACK)

        def last_z(cols):
            nc.vector.tensor_tensor(late_rows[:, LAST - PACK, cols], page_of[LAST][:, cols], load_sb[LAST][:, cols], MULT)

        factors = [page_of[s][:] for s in range(LAST)]
        factors[1] = prior_sb[1][:].rearrange("p i j -> p (i j)")[:, T2:]
        factors[2] = late_room[:, 0:T2]
        factors[4] = kept_room[:, T2:]

        def z_on_gpsimd(s):
            if s in (1, 2, 4):
                nc.scalar.activation(factors[s], page_of[s][:], COPY, bias=1.0)
            rows = early_rows if s < PACK else late_rows
            for cols in [slice(0, S), slice(S, T2)] if s == 0 else [slice(0, T2)]:
                nc.gpsimd.tensor_tensor(rows[:, s % PACK, cols], factors[s][:, cols], load_sb[s][:, cols], MULT)

        chunks = [slice(c0, c1) for c0, c1 in zip(CUTS, CUTS[1:])]
        early_woven = late_kept.bitcast(BF16).rearrange("p (t i) -> p t i", i=PACK)
        late_woven = [sb("late_woven%d" % q, [P, cols.stop - cols.start, PACK], BF16) for q, cols in enumerate(chunks)]

        def weave(copy, woven, rows, i0, i1):
            copy(
                out=woven.rearrange("p (c n) i -> p c i n", n=NEIGHBOURS)[:, :, i0:i1, :],
                in_=rows[:, i0:i1, :].rearrange("p i (c n) -> p c i n", n=NEIGHBOURS),
            )

        def weave_early(piece):
            weave(nc.scalar.copy, early_woven[:, piece * WEAVE : (piece + 1) * WEAVE, :], early_rows[:, :, piece * WEAVE : (piece + 1) * WEAVE], 0, PACK)

        def weave_late(copy, q, i0, i1):
            weave(copy, late_woven[q][:], late_rows[:, :, chunks[q]], i0, i1)

        gate, rest = first_gate()
        turned_rests(0, 1, [banks[1], banks[2], banks[3], banks[4]])
        early_piece(0, 0, PACK)
        early_piece(1, 0, 2)
        early_piece(1, 2, PACK)
        first_source(gate, rest)
        for s in range(1, PACK):
            early_fit(s)
        make_early_taken(1)
        make_early_taken(2)
        make_third_taken(0)
        for s in range(1, PACK):
            make_kept(s)

        def blend(s):
            make_total(s)
            make_product(s)

        scatter(0)
        blend(1)
        make_third_taken(1)
        z_on_gpsimd(0)
        for a in range(PASSES):
            for i0 in range(0, PACK, 2):
                round_wa(nc.scalar.copy, late_rounded[:, a, i0 : i0 + 2, :, :], a, 1, i0, i0 + 2)

        turned_rests(1, 0, fit_banks)
        scatter(1)
        late_words = sb("late_words", [P, PASSES, PASS], U32)
        late_sc = sb("late_sc", [P, PASSES, PASS], U8)
        quantize(late_words[:].rearrange("p a c -> p (a c)"), late_sc[:].rearrange("p a c -> p (a c)"), late_values)
        blend(2)
        blend(3)
        for s in range(PACK, SLICES):
            make_kept(s)
        z_on_gpsimd(1)
        for c in range(CHUNKS):
            late_fit(c, late_words, late_sc)
        taken_room = sb("taken_room", [P, (PACK + 1) * S], F32, tag="wa_raw01")[:]
        late_taken_t = taken_room[:, S:].rearrange("p (c m) -> p c m", c=CHUNKS)
        source[3] = taken_room[:, P // 2 : P // 2 + S]
        add_one(3, slice(0, S - P // 2))

        scatter(2)
        for c in range(CHUNKS):
            make_late_taken(c)
            for s in range(PACK, SLICES):
                cols = slice((s - PACK) * P, (s - PACK + 1) * P)
                nc.tensor.matmul(
                    total[s][:, c * P : (c + 1) * P], late_taken_t[:, c, cols], ident[:], is_transpose=True, start=(c == 0), stop=False
                )
            if c == 0:
                add_one(3, slice(S - P // 2, S))
        z_on_gpsimd(2)
        scatter(3)
        for s in range(PACK, SLICES):
            turn_into(total[s], quarters(kept_t[s]), False, True)
        last_products()
        make_product(4)
        make_product(5)
        add_one(5)
        z_on_gpsimd(3)
        add_one(6)
        add_one(7)
        scatter(4)
        z_on_gpsimd(4)
        weave_early(0)
        weave_early(1)
        scatter(5)
        z_on_gpsimd(5)
        weave_early(2)
        weave_early(3)
        scatter(6)
        z_on_gpsimd(6)
        for q in range(len(chunks)):
            weave_late(nc.scalar.copy, q, 0, 2)

        free_banks = list(banks)
        held = {}
        for q, cols in enumerate(chunks):
            width = cols.stop - cols.start
            per_bank = min(N_TILES, S // width)
            held[q] = []
            first = N_TILES % per_bank or per_bank
            for n0, count in [(0, first)] + [(n0, per_bank) for n0 in range(first, N_TILES, per_bank)]:
                tile = free_banks.pop(0)[:, 0 : count * width].rearrange("p (n t) -> p n t", n=count)
                held[q].append((tile, n0, count))

        def out_pass(b, q, words, scales):
            for tile, n0, count in held[q]:
                for k in range(count):
                    rows = slice((n0 + k) * P, (n0 + k + 1) * P)
                    nc.tensor.matmul_mx(
                        out=tile[:, k, :],
                        lhsT=wo_w[:, b, rows].bitcast(FP8X4),
                        lhsT_scale=wo_sc[:, b, rows],
                        rhs=words.bitcast(FP8X4),
                        rhs_scale=scales,
                        start=(b == 0 and k == 0),
                        stop=(b == PASSES - 1 and k == count - 1),
                    )

        out_view = out.rearrange("(n p) t -> p n t", p=P)
        staged = [load_sb[s] for s in range(3)] + [tile[:].rearrange("p i j -> p (i j)") for tile in prior_sb]

        def fill(q):
            weave_late(nc.scalar.copy if q in SCALAR_FILLS else nc.vector.tensor_copy, q, 2, PACK)

        def finish(b, q):
            width = chunks[q].stop - chunks[q].start
            tag = "late_woven%d" % (q - 1) if q == len(chunks) - 1 else None
            words = sb("late_z_words%d" % q, [P, width], U32, tag=tag)[:] if b else early_words[:, chunks[q]]
            scales = sb("z_sc%d%d" % (b, q), [P, width], U8)
            woven = late_woven[q][:] if b else early_woven[:, chunks[q], :]
            quantize(words, scales[:], woven.rearrange("p t i -> p (t i)"))
            out_pass(b, q, words, scales[:])

        def leave(q):
            cols = chunks[q]
            width = cols.stop - cols.start
            room = staged[q][:, 0 : N_TILES * width].rearrange("p (n t) -> p n t", n=N_TILES)
            for k, (tile, n0, count) in enumerate(held[q]):
                copy = nc.vector.tensor_copy if (q, k) in VECTOR_LEAVES else nc.scalar.copy
                copy(room[:, n0 : n0 + count, :], tile)
                nc.sync.dma_start(out=out_view[:, n0 : n0 + count, cols], in_=room[:, n0 : n0 + count, :])

        scatter(LAST)
        early_words = sb("early_words", [P, T2], U32, tag="load6")
        for q in range(AHEAD):
            finish(0, q)
        last_z(chunks[0])
        last_z(chunks[1])
        fill(0)
        last_z(chunks[3])
        fill(3)
        finish(1, 0)
        fill(1)
        last_z(chunks[2])
        finish(1, 1)
        finish(0, 2)
        fill(2)
        last_z(chunks[4])
        finish(1, 2)
        finish(0, 3)
        fill(4)
        finish(1, 3)
        finish(0, 4)
        finish(1, 4)
        for q in range(len(chunks)):
            leave(q)
